import numpy as np, ml_dtypes
CORES = [40,64,80,88,96,104,120,144]
N = 8
BF = ml_dtypes.bfloat16
def gentries(a):
    return np.ascontiguousarray(a.reshape(8, 16, -1).transpose(0, 2, 1)).reshape(8, -1)
def gtable(e):
    e = np.asarray(e); return np.ascontiguousarray(e.reshape(8, -1, 16).transpose(0, 2, 1)).reshape(128, -1).astype(np.int32)
TP, C, W, S, Q, P, B = 16, 64, 4096, 6, 3, 2, 1024
CB = C // P
def sign(rng, *shape):
    return 1.0 - 2.0 * rng.integers(0, 2, shape)
def draw_lists(rng):
    nt = np.ascontiguousarray(np.argsort(rng.random((N, 8, S, W)), axis=-1)[..., :C])
    return rng.integers(0, W, (N, 8, TP, C)), rng.integers(0, W, (N, 8, Q, C)), nt
def draw_floats(rng):
    w = rng.standard_normal((N, 8, 16, TP, C), dtype=np.float32) * 0.25 * np.exp2(rng.integers(-1, 2, (N, 8, 1, TP, C)).astype(np.float32))
    r = rng.standard_normal((N, 8, 16, W), dtype=np.float32) * np.exp2(rng.integers(-1, 2, (N, 8, 16, 1)).astype(np.float32))
    d = rng.standard_normal((N, 8, 16, S, C), dtype=np.float32) * np.exp2(rng.integers(-1, 2, (N, 8, 16, 1, 1)).astype(np.float32))
    return w, r, d
def wide(rng, v, lo, hi):
    k = v.shape[:2] + (1,) + v.shape[3:]
    return v * np.exp2(rng.integers(lo, hi + 1, k).astype(np.float32)) * (rng.random(k) > 0.0625)
def pack(w, r, d, dl, qu, nt):
    b = lambda v: np.ascontiguousarray(np.clip(np.where(np.abs(v) < 2.0 ** -20, 0, v), -8, 8).reshape(N, 128, -1)).astype(np.float32).astype(BF)
    i = lambda v: np.stack([gtable(a.reshape(8, -1)) for a in v])
    return {"w0": b(w), "r0": b(r), "d0": b(d), "dl": i(dl), "qu": i(qu), "nt": i(nt)}
def kinds(rng):
    return ((np.arange(8) + np.arange(N)[:, None] + rng.integers(0, 4)) & 3).reshape(N, 8, 1, 1)
def plant(v, c, wt, x, des, tap, off):
    w, r, d, dl, qu, nt = v; col = W // 2 + TP * c + np.arange(TP)
    dl[:, :, :, c] = (nt[:, :, 0, c][:, :, None] - col) & (W - 1)
    qu[:, :, 0, c] = (dl[:, :, tap, c] + off) & (W - 1)
    w[..., c] = wt; r[..., col] = x; d[:, :, :, 0, c] = des
def setup_inputs(rng):
    w, r, d = draw_floats(rng); dl, qu, nt = draw_lists(rng)
    return pack(w, r, d, dl, qu, nt)
def setup_inputs_spread(rng):
    w, r, d = draw_floats(rng); dl, qu, nt = draw_lists(rng)
    return pack(wide(rng, w, -2, 2), wide(rng, r, -2, 2), wide(rng, d, -2, 2), dl, qu, nt)
def setup_inputs_ends(rng):
    w, r, d = draw_floats(rng); dr, qr, nt = draw_lists(rng)
    free = rng.random((N, 8, 1, C)) < 0.25; free[..., 0] = False; free[..., C - 1] = False
    dl = np.where(free, dr, rng.integers(0, 2, (N, 8, TP, C)) * (W - 1)); qu = np.where(free, qr, rng.integers(0, 2, (N, 8, Q, C)) * (W - 1))
    pool = np.concatenate([np.arange(C // 2), W - C // 2 + np.arange(C // 2)]); rest = pool[(pool != 1) & (pool != W - 1)]
    nt = pool[np.argsort(rng.random((N, 8, S, C)), axis=-1)]
    nt[:, :, 0, 1:C - 1] = rest[np.argsort(rng.random((N, 8, C - 2)), axis=-1)]; nt[:, :, 0, 0] = 1; nt[:, :, 0, C - 1] = W - 1
    w = np.where(rng.random((N, 8, 1, 1, C)) < 0.3, 8.0 * sign(rng, N, 8, 16, TP, C), w); w[..., C - 1] = 8.0; w[..., 0] = -8.0
    r = np.where(rng.random((N, 8, 1, W)) < 0.3, 8.0 * sign(rng, N, 8, 16, W), r)
    for j in (0, 1, 2, W - 1): r[..., j] = 8.0
    d = np.where(rng.random((N, 8, 1, S, C)) < 0.4, 8.0 * sign(rng, N, 8, 16, S, C), d); d[:, :, :, 0, C - 1] = -8.0; d[:, :, :, 0, 0] = 8.0
    v = (w, r, d, dl, qu, nt)
    u = 7.0 + rng.random((N, 8, 16, TP // 2))
    plant(v, 1, np.concatenate([u, -u], axis=3), 8.0, np.where(rng.random((N, 8, 16)) < 0.25, 0.0, 2.0 * rng.random((N, 8, 16)) - 1.0), 0, 0)
    x = 2.0 ** -6 + 2.0 ** -7 * rng.random((N, 8, 16, TP)); x[..., 4] = 2.0 ** -7; x[..., 2] = 2.0 ** -5; u = sign(rng, N, 8, 16, TP)
    plant(v, 2, 8.0 * u, x * u, 8.0, 2, 0)
    return pack(*v)
def setup_inputs_crowd(rng):
    w, r, d = draw_floats(rng); dl, qu, nt = draw_lists(rng); r = np.clip(r, -2, 2); kind = kinds(rng)
    row = np.arange(16).reshape(1, 1, 16, 1); tap = np.arange(TP).reshape(TP, 1)
    four = np.argsort(rng.random((N, 8, TP, C)), axis=2)[:, :, :4, None]
    turn = (row + rng.integers(0, 16, (N, 8, 1, C))) & 15
    other = np.where(kind == 1, turn == 0, (kind == 2) & (turn < 8))
    lo = np.where(other, four[:, :, 1], four[:, :, 0]); hi = np.where(other, four[:, :, 3], four[:, :, 2])
    w = sign(rng, N, 8, 16, TP, C) * (0.5 + 0.5 * rng.random((N, 8, 16, TP, C)))
    w = np.where(tap == lo[:, :, :, None], 0.0, w); w = np.where(tap == hi[:, :, :, None], 2.0 * sign(rng, N, 8, 16, TP, C), w)
    w = np.where(kind[..., None] == 3, sign(rng, N, 8, 16, 1, C) * (0.5 + 0.5 * rng.random((N, 8, 16, 1, C))), w)
    dl = np.where(kind == 3, dl[:, :, :1], dl)
    v = (w, r, d, dl, qu, nt)
    odd = np.arange(16) == rng.integers(0, 16, (N, 8, 1))
    u = sign(rng, N, 8, 16, TP) * (0.5 + 0.5 * rng.random((N, 8, 16, TP)))
    u[..., 1] = np.where(odd, 0.5, 0.125); u[..., 4] = 0.125; u[..., 2] = np.where(odd, 1.0, 2.0); u[..., 6] = 2.0
    plant(v, 0, u, 0.5 + rng.random((N, 8, 16, 1)), 2.0 * rng.random((N, 8, 16)) - 1.0, 6, -B)
    u = sign(rng, N, 8, 16, TP) * (1.5 + 0.5 * rng.random((N, 8, 16, TP))); x = 2.0 ** -4 * sign(rng, N, 8, 16, TP)
    u[..., 1] = 1.0; u[..., 4] = 1.0; u[..., 2] = 3.0; u[..., 6] = 3.0
    x[..., 1] = 1.5 * 2.0 ** -20; x[..., 4] = 2.0 ** -20; x[..., 2] = 2.0 ** -20; x[..., 6] = 1.5 * 2.0 ** -20
    plant(v, 1, u, x, 8.0, 2, B)
    return pack(*v)
def setup_inputs_corners(rng):
    w, r, d = draw_floats(rng); dl, qu, nt = draw_lists(rng); kind = kinds(rng); half = rng.random((N, 8, 1, C)) < 0.5
    w = np.where(kind[..., None] == 0, 0.0, w); dl = np.where((kind == 0) & half, dl[:, :, :1], dl)
    one = rng.integers(0, W, (N, 8, 1, C)); far = np.where(half, one, (one + W // 2) & (W - 1))
    dl = np.where(kind == 1, one, dl); qu = np.where(kind == 1, far, qu)
    few = rng.choice(np.array([0, 1, W // 2, W - 1]), (N, 8, Q, C)); qu = np.where(kind >= 2, few, qu)
    first = nt[:, :, :1]; nt = np.where(kind == 2, (first + np.arange(S)[:, None]) & (W - 1), np.where(kind == 3, first, nt))
    near = 1 + rng.integers(0, S, (N, 8, TP, C)); own = np.where(rng.random((N, 8, TP, C)) < 0.5, 0, rng.choice(np.array([0, 1, W // 2, W - 1]), (N, 8, TP, C)))
    dl = np.where(kind == 2, near, np.where(kind == 3, own, dl))
    v = (w, r, d, dl, qu, nt)
    u = np.zeros((N, 8, 16, TP)); u[..., 0] = 2.0 ** -16; x = 2.0 + 6.0 * rng.random((N, 8, 16, TP)); x[..., 0] = 2.0 ** -17; x[..., 4] = 1.0
    plant(v, 0, u, x, 0.0, 0, 0)
    u = sign(rng, N, 8, 16, TP) * (3.0 + rng.random((N, 8, 16, TP))); x = 2.0 ** -5 * sign(rng, N, 8, 16, TP)
    u[..., 1] = 1.9921875; u[..., 4] = 1.9921875; u[..., 2] = 6.0; x[..., 1] = 3.0 * 2.0 ** -18; x[..., 4] = 2.0 ** -17
    plant(v, 1, u, x, 8.0, 2, 0)
    return pack(*v)
def setup_inputs_edge(rng):
    w, r, d = draw_floats(rng); dl, qu, nt = draw_lists(rng); r = np.clip(r, -2, 2); w = np.clip(w, -0.5, 0.5)
    tap = np.arange(TP).reshape(TP, 1); k = rng.integers(0, TP, (N, 8, 1, C)); base = rng.integers(0, W, (N, 8, 1, C))
    w = np.where(tap == k[:, :, None], 1.5 * sign(rng, N, 8, 16, 1, C), w)
    away = np.array([B - 1, B, B + 1, 1 - B, -B, -B - 1, 0, W // 2])
    dl = np.where(tap == k, base, (base + rng.choice(away, (N, 8, TP, C))) & (W - 1)); qu = (base + rng.choice(away, (N, 8, Q, C))) & (W - 1)
    v = (w, r, d, dl, qu, nt)
    side = sign(rng, N, 8, 16); way = side * sign(rng, N, 8, 16)
    u = np.zeros((N, 8, 16, TP)); x = 1.0 + rng.random((N, 8, 16, TP))
    u[..., 0] = 7.5 * side; u[..., 1] = 1.5 * 2.0 ** -10 * way; u[..., 2] = -7.5 * side; u[..., 3] = -(2.0 ** -10) * way
    x[..., 0] = 8.0; x[..., 1] = 2.0 ** -10; x[..., 2] = 8.0; x[..., 3] = 2.0 ** -10
    plant(v, 0, u, x, 2.0 * side, 0, 0)
    return pack(*v)
def check_inputs(d):
    bad = []
    for k in ("dl", "qu", "nt"):
        if np.min(d[k]) < 0 or np.max(d[k]) > W - 1: bad.append("range of " + k)
    for k in ("w0", "r0", "d0"):
        m = np.abs(np.asarray(d[k]).astype(np.float32))
        if not np.all((m <= 8) & ((m == 0) | (m >= 2.0 ** -20))): bad.append("size of " + k)
    n = np.sort(np.stack([gentries(a) for a in d["nt"]]).reshape(N, 8, S, C), axis=-1)
    if np.any(n[..., 1:] == n[..., :-1]): bad.append("times of a step differ")
    return bad
def reference(w0, r0, d0, dl, qu, nt):
    w = w0.astype(np.float32).reshape(N, 8, 16, TP, C); r = r0.astype(np.float32).reshape(N, 8, 16, W); d = d0.astype(np.float32).reshape(N, 8, 16, S, C)
    a = np.stack([gentries(v) for v in dl]).astype(np.int64).reshape(N, 8, TP, C)
    q = np.stack([gentries(v) for v in qu]).astype(np.int64).reshape(N, 8, Q, C)
    n = np.stack([gentries(v) for v in nt]).astype(np.int64).reshape(N, 8, S, C)
    tap = np.arange(TP).reshape(TP, 1)
    for s in range(S):
        t = n[:, :, s]
        ix = (t[:, :, None] - a) & (W - 1)
        x = np.take_along_axis(r, ix.reshape(N, 8, 1, TP * C), 3).reshape(N, 8, 16, TP, C)
        p = w * x; y = p[:, :, :, 0]
        for k in range(1, TP): y = y + p[:, :, :, k]
        e = np.minimum(np.maximum(d[:, :, :, s] - y, np.float32(-2)), np.float32(2))
        w = w + np.float32(0.015625) * (e[:, :, :, None] * x)
        m = np.abs(w)
        least = np.add.reduce((m == np.min(m, axis=3, keepdims=True)).astype(np.int64), axis=2)
        most = np.add.reduce((m == np.max(m, axis=3, keepdims=True)).astype(np.int64), axis=2)
        weak = np.argmax(least, axis=2)[:, :, None]; strong = np.argmax(most, axis=2)[:, :, None]
        head = q[:, :, s % Q][:, :, None].copy()
        gap = (head - np.take_along_axis(a, strong, 2)) & (W - 1)
        ok = np.minimum(gap, W - gap) <= B
        q[:, :, s % Q] = np.where(ok, np.take_along_axis(a, weak, 2), head)[:, :, 0]
        hit = ok & (tap == weak)
        a = np.where(hit, head, a); w = np.where(hit[:, :, None], np.float32(0.25), w)
        come = np.concatenate([np.roll(np.roll(e[..., b * CB:(b + 1) * CB], 1 + b, axis=0), 1 + s, axis=1) for b in range(P)], axis=3)
        np.put_along_axis(r, t[:, :, None], come, 3)
    q = np.roll(q, -(S % Q), axis=2)
    return {"yw": np.ascontiguousarray(w.reshape(N, 128, TP * C)), "yr": np.ascontiguousarray(come.reshape(N, 128, C)),
            "yd": np.stack([gtable(v.reshape(8, -1)) for v in a]).astype(np.float32), "yq": np.stack([gtable(v.reshape(8, -1)) for v in q]).astype(np.float32)}

@@ -1,0 +1,533 @@
+from concourse.bass import DstId, RemoteDMATransfer
+from concourse.mybir import AluOpType, ActivationFunctionType
+
+TP, C, W, S, Q = 16, 64, 4096, 6, 3
+NW = TP * C
+H = NW // 2
+ENG = 8
+RCH = 2
+KW, KS = H - C, H
+PMODE = 1
+RPOS = 3
+LATE = 1
+
+F, B, I, U = "float32", "bfloat16", "int32", "uint16"
+SCRATCH = {
+    "r0b": ("sbuf", [128, W], B), "R": ("sbuf", [128, W], F),
+    "w0b": ("sbuf", [128, NW], B), "d0b": ("sbuf", [128, S * C], B),
+    "dli": ("sbuf", [128, C], I), "qui": ("sbuf", [128, 12], I), "nti": ("sbuf", [128, 24], I),
+    "w": ("sbuf", [128, 2 * NW], F), "p": ("sbuf", [128, 2 * NW], F), "x": ("sbuf", [128, 2 * NW], F),
+    "xq": ("sbuf", [128, C], F), "quart": ("sbuf", [128, C], F),
+    "Y": ("sbuf", [128, NW], F), "df": ("sbuf", [128, C], F), "e": ("sbuf", [128, C], F),
+    "t": ("sbuf", [128, NW], F),
+    "smin": ("sbuf", [128, NW], F), "smax": ("sbuf", [128, NW], F),
+    "rmin": ("sbuf", [128, NW], F), "rmax": ("sbuf", [128, NW], F),
+    "kmin": ("sbuf", [128, NW], B), "kmax": ("sbuf", [128, NW], B),
+    "mmul": ("sbuf", [128, NW], B), "madd": ("sbuf", [128, H], B),
+    "M": ("sbuf", [128, 2 * C], F), "D": ("sbuf", [128, 4], I), "Z": ("sbuf", [128, 4], I), "idx": ("sbuf", [128, 4], U),
+    "aL": ("sbuf", [128, C], F), "qL": ("sbuf", [128, 12], F), "nL": ("sbuf", [128, 24], F), "ntu": ("sbuf", [128, 24], U),
+    "g1": ("sbuf", [128, C], F), "g2": ("sbuf", [128, C], F), "sgn": ("sbuf", [128, C], B),
+    "hit": ("sbuf", [128, C], F), "q16": ("sbuf", [128, 4], F), "junk": ("sbuf", [128, C], F),
+    "a2": ("sbuf", [128, 256], F), "neg": ("sbuf", [128, 256], B), "tr": ("sbuf", [128, 256], F),
+    "ix": ("sbuf", [128, S * C], U), "hd": ("sbuf", [128, 24], I), "ha": ("sbuf", [128, 24], I), "hx": ("sbuf", [128, 24], U),
+    "pI": ("sbuf", [128, 1], I), "pb": ("sbuf", [128, 8], I), "pf": ("sbuf", [128, 8], F), "pg": ("sbuf", [128, 8], F),
+    "iX": ("sbuf", [128, 144], F), "i1": ("sbuf", [128, C], F), "iC": ("sbuf", [128, C], F),
+    "lu": ("sbuf", [128, 176], U),
+    "colL": ("sbuf", [128, C], F), "colN": ("sbuf", [128, C], F),
+    "cWL": ("sbuf", [128, C], F), "cWN": ("sbuf", [128, C], F), "cS": ("sbuf", [128, C], F),
+    "rot": ("sbuf", [128, 256], F), "i512": ("sbuf", [128, 128], B), "i2k": ("sbuf", [128, 128], B), "vot": ("sbuf", [128, 144], B),
+    "ydb": ("sbuf", [128, C], F),
+    "send": ("sbuf", [128, S * C], F), "land": ("sbuf", [128, S * C], F),
+    "ptp": ("psum", [128, NW], F), "pm": ("psum", [128, NW], F), "pK": ("psum", [128, NW], F),
+    "pE": ("psum", [128, H], F), "pN": ("psum", [128, H], F),
+}
+SEMAPHORES = (["eV", "eS", "eT", "eG", "ld_s", "ld_w", "ld_d", "ld_q", "sent", "st_a", "st_b"]
+              + ["ld_r%d" % k for k in range(RCH)] + ["arr%d" % s for s in range(S)])
+PSUM = ("ptp", "pm", "pK", "pE", "pN")
+L_E, L_W, L_R, L_C, L_A, L_T = 0, 64, 128, 160, 164, 168
+DQ, UU = 0, C
+
+
+def routes(T, topo):
+    out = []
+    n = len(T.cores)
+    for r, src in enumerate(T.cores):
+        used = []
+        for b in range(2):
+            dst = T.cores[(r + 1 + b) % n]
+            via = None
+            if not topo.may_write(src, dst):
+                cand = [c for c in topo.cores_of(src) if T.rank_of(c) is None and c not in used and topo.may_write(c, dst)]
+                cand.sort(key=lambda c: (topo.die(c) != topo.die(src), c))
+                via = cand[0]
+                used.append(via)
+            out.append((src, dst, via, b))
+    return out
+
+
+def pick(topo, src, dst, taken):
+    eng = [e for e in topo.engines(src, dst) if e not in taken][:ENG]
+    taken.extend(eng)
+    m = 0
+    for e in eng:
+        m |= 1 << e
+    return m
+
+
+def helper_program(g, core, T, topo, job):
+    src, dst, via, b = job
+    rid, pid = topo.addr(dst, core)
+    m = pick(topo, core, dst, [])
+    for s in range(S):
+        piece = T.land[:, s * C + b * 32:s * C + b * 32 + 32]
+        g.wait_ge(T.sem["arr%d" % s], ENG)
+        g.remote_dma(piece, piece, T.sem["arr%d" % s], T.sem.sent, pid, rid, m)
+    g.wait_ge(T.sem.sent, S * ENG)
+
+
+def emit(g, T, ops):
+    qs = {"V": g.vector, "S": g.scalar, "T": g.tensor, "G": g, "Y": g.sync}
+    known = {q: {} for q in qs}
+    seq = {q: 0 for q in qs}
+    acc = {}
+    for op in ops:
+        q = op["q"]
+        if op["tok"] is None:
+            seq[q] += 1
+            op["key"], op["val"] = q, seq[q]
+        else:
+            op["key"], op["val"] = op["tok"]
+        deps = []
+        for mode, regs in (("r", op["r"]), ("w", op["w"])):
+            for (buf, lo, hi) in regs:
+                ps = buf in PSUM
+                for (o2, m2, l2, h2) in acc.get(buf, []):
+                    same = o2["q"] == q and o2["tok"] is None
+                    if ps and not same:
+                        if l2 // H > (hi - 1) // H or (h2 - 1) // H < lo // H:
+                            continue
+                    elif l2 >= hi or h2 <= lo:
+                        continue
+                    if m2 == "r" and mode == "r" and (same or not ps):
+                        continue
+                    if same and q == "T":
+                        continue
+                    deps.append(o2)
+        op["waits"] = []
+        if q is not None:
+            kn = known[q]
+            best = {}
+            for o2 in deps:
+                if o2["key"] not in best or best[o2["key"]]["val"] < o2["val"]:
+                    best[o2["key"]] = o2
+            for o2 in sorted(best.values(), key=lambda o: -o["n"]):
+                if kn.get(o2["key"], 0) >= o2["val"]:
+                    continue
+                op["waits"].append(o2)
+                o2["flag"] = True
+                kn[o2["key"]] = o2["val"]
+                for k, v in o2["clock"].items():
+                    if kn.get(k, 0) < v:
+                        kn[k] = v
+            op["clock"] = dict(kn)
+        else:
+            op["clock"] = {}
+        for mode, regs in (("r", op["r"]), ("w", op["w"])):
+            for (buf, lo, hi) in regs:
+                lst = acc.setdefault(buf, [])
+                if mode == "w" and buf not in PSUM:
+                    lst[:] = [a for a in lst if not (a[2] >= lo and a[3] <= hi)]
+                lst.append((op, mode, lo, hi))
+    cnt = {q: 0 for q in qs}
+    for op in ops:
+        if op["tok"] is None and op["flag"]:
+            cnt[op["q"]] += 1
+            op["cnt"] = cnt[op["q"]]
+    for op in ops:
+        if op["q"] is None:
+            continue
+        eng = qs[op["q"]]
+        for o2 in op["waits"]:
+            if o2["tok"] is None:
+                eng.wait_ge(T.sem["e" + o2["q"]], o2["cnt"])
+            else:
+                eng.wait_ge(T.sem[o2["key"]], o2["val"])
+        ins = op["fn"](eng)
+        if op["tok"] is None and op["flag"]:
+            ins.then_inc(T.sem["e" + op["q"]], 1)
+
+
+def rank_program(g, core, T, topo):
+    jobs = routes(T, topo)
+    if T.rank_of(core) is None:
+        for job in jobs:
+            if job[2] == core:
+                helper_program(g, core, T, topo, job)
+        return
+    A, AF = AluOpType, ActivationFunctionType
+    ops = []
+
+    def add(q, fn, r, w, tok=None):
+        ops.append({"q": q, "fn": fn, "r": r, "w": w, "tok": tok, "flag": False, "n": len(ops)})
+
+    def ap(a):
+        if len(a) == 3:
+            return T[a[0]][:, a[1]:a[2]]
+        if isinstance(a[3], int):
+            return T[a[0]][:, a[1]:a[2]:a[3]]
+        return T[a[0]][:, a[1]:a[2]].indirect(ap(a[3]))
+
+    def regs(*aps):
+        return [a[:3] for a in aps if isinstance(a, tuple)]
+
+    def lists(*aps):
+        return [a[3] for a in aps if isinstance(a, tuple) and len(a) == 4 and isinstance(a[3], tuple)]
+
+    def val(a):
+        return ap(a) if isinstance(a, tuple) else a
+
+    def tt(out, a, b, op):
+        add("V", lambda e: e.tensor_tensor(ap(out), ap(a), ap(b), op), regs(a, b) + lists(out, a), regs(out))
+
+    def ts(out, a, s1, op0, s2=None, op1=None):
+        if op1 is None:
+            fn = lambda e: e.tensor_scalar(ap(out), ap(a), val(s1), None, op0)
+        else:
+            fn = lambda e: e.tensor_scalar(ap(out), ap(a), val(s1), val(s2), op0, op1)
+        add("V", fn, regs(a, s1, s2) + lists(out, a), regs(out))
+
+    def cp(out, a):
+        add("V", lambda e: e.tensor_copy(ap(out), ap(a)), regs(a) + lists(out, a), regs(out))
+
+    def scan(out, d0, d1, op0, op1):
+        add("V", lambda e: e.tensor_tensor_scan(ap(out), ap(d0), ap(d1), 0.0, op0, op1), regs(d0, d1), regs(out))
+
+    def fill(out, c):
+        add("V", lambda e: e.memset(ap(out), c), [], regs(out))
+
+    def act(out, a, func, bias=None, scale=None, acc=None):
+        kw = {}
+        if bias is not None:
+            kw["bias"] = val(bias)
+        if scale is not None:
+            kw["scale"] = scale
+        if acc is not None:
+            kw["accum_out"] = ap(acc)
+        add("S", lambda e: e.activation(ap(out), ap(a), func, **kw), regs(a, bias) + lists(a), regs(out, acc))
+
+    def mm(out, l, r, start, stop):
+        add("T", lambda e: e.matmul(ap(out), ap(l), ap(r), start, stop), regs(l, r), regs(out))
+
+    def iota(out, pat, base, cm=0, integer=False):
+        if integer:
+            add("G", lambda e: e.iota(ap(out), pat, base, cm), [], regs(out))
+        else:
+            add("G", lambda e: e.iota(ap(out), pat, base, cm, allow_small_or_imprecise_dtypes=True), [], regs(out))
+
+    def load(q, out, src, sem, total=16):
+        add(q, lambda e: e.dma_start(ap(out), src).then_inc(T.sem[sem], 16), [], regs(out), (sem, total))
+
+    def store(q, dst, a, sem, total):
+        add(q, lambda e: e.dma_start(dst, ap(a)).then_inc(T.sem[sem], 16), regs(a), [], (sem, total))
+
+    def half(buf, h):
+        return (buf, h * H, (h + 1) * H)
+
+    load("S", ("dli", 0, C), T.dl[:], "ld_s", 32)
+    load("S", ("nti", 0, 24), T.nt[:], "ld_s", 32)
+    load("Y", ("w0b", 0, NW), T.w0[:], "ld_w")
+    for k in range(RCH):
+        lo, hi = k * W // RCH, (k + 1) * W // RCH
+        load("Y", ("r0b", lo, hi), T.r0[:, lo:hi], "ld_r%d" % k)
+    load("Y", ("d0b", 0, S * C), T.d0[:], "ld_d")
+    load("Y", ("qui", 0, 12), T.qu[:], "ld_q")
+
+    iota(("pI", 0, 1), [[0, 1]], 0, 1, True)
+    iota(("iX", 0, 144), [[1, 144]], 0)
+    iota(("i1", 0, C), [[1, 16], [16, 4]], 0)
+    iota(("cS", 0, C), [[0, 4], [-W, 16]], 15 * W + 1535)
+    iota(("iC", 0, C), [[16, 4], [C, 16]], 0)
+    fill(("mmul", 0, NW), 1.0)
+    P = ("pI", 0, 1)
+    ts(("pb", 0, 1), P, 15, A.bitwise_and)
+    ts(("pb", 1, 2), P, 3, A.bitwise_and)
+    ts(("pb", 2, 3), P, 16, A.bitwise_and)
+    ts(("pb", 3, 4), P, 2, A.logical_shift_right, 3, A.bitwise_and)
+    ts(("pb", 4, 5), P, 112, A.bitwise_and)
+    ts(("pb", 5, 6), P, 127, A.bitwise_and)
+    fill(("madd", 0, H), 0.0)
+    cp(("pf", 0, 6), ("pb", 0, 6))
+    fill(("mmul", 0, NW, TP), 0.0)
+    ROW, LOW, ODD, MID, GRP, PAR = [("pf", k, k + 1) for k in range(6)]
+    ts(("pg", 0, 1), ROW, 64.0, A.mult)
+    ts(("pg", 1, 2), LOW, 32.0, A.mult, ODD, A.add)
+    ts(("pg", 2, 3), GRP, 15.0, A.add)
+    ts(("lu", L_A, L_A + 2), ("iX", 0, 2), 0.0, A.mult, ROW, A.add)
+    ts(("pg", 3, 4), ("pg", 1, 2), MID, A.add)
+    ts(("lu", L_W, L_W + C), ("i1", 0, C), ("pg", 0, 1), A.add)
+    ts(("rot", 0, 128), ("iX", 0, 128), PAR, A.is_equal)
+    ts(("i2k", 0, 128), ("iX", 0, 128), PAR, A.is_equal, -2048.0, A.mult)
+    ts(("lu", L_T, L_T + 4), ("iX", 0, 4), 4.0, A.mult, ("pg", 3, 4), A.add)
+    fill(("madd", 0, H, TP), 1e20)
+    fill(("quart", 0, C), 0.25)
+    ts(("nL", 0, 24), ("nti", 0, 24), 2048.0, A.add)
+    for c in range(4):
+        cp(("aL", c * 16, c * 16 + 16), ("dli", c, C, 4))
+
+    def far(part):
+        if part == 0:
+            act(("g1", 0, C), ("pN", DQ, DQ + C), AF.Abs)
+        elif part == 1:
+            act(("g2", 0, C), ("g1", 0, C), AF.Abs, bias=-2048.0)
+        else:
+            act(("sgn", 0, C), ("g2", 0, C), AF.Sign, bias=1023.5, scale=-1.0)
+
+    def off_a(s, cs):
+        o = (s % 2) * 128
+        for c in cs:
+            act(("a2", o + c * 32, o + c * 32 + 32), ("aL", c * 16, c * 16 + 16, ("lu", L_A, L_A + 2)), AF.Identity,
+                bias=("nL", s * 4 + c, s * 4 + c + 1), scale=-1.0)
+
+    def off_b(s):
+        o = (s % 2) * 128
+        act(("neg", o, o + 128), ("a2", o, o + 128), AF.Sign, bias=-2047.5)
+        mm(("pE", C + o, C + o + 128), ("rot", 0, 128), ("a2", o, o + 128), True, False)
+        mm(("pE", C + o, C + o + 128), ("i2k", 0, 128), ("neg", o, o + 128), False, True)
+
+    def off_c(s):
+        o = (s % 2) * 128
+        add("V", lambda e: e.transpose(T.tr[:, o:o + 128], T.pE[:, C + o:C + o + 128]), [("pE", C + o, C + o + 128)], [("tr", o, o + 128)])
+
+    def off_d(s):
+        o = (s % 2) * 128
+        cp(("ix", s * C, (s + 1) * C), ("tr", o, o + 128, ("lu", L_T, L_T + 4)))
+
+    def heads(s0, s1, part):
+        k = (s0 - 1) % Q
+        if part == 0:
+            tt(("hd", s0 * 4, s1 * 4), ("nti", s0 * 4, s1 * 4), ("qL", k * 4, k * 4 + (s1 - s0) * 4), A.subtract)
+        elif part == 1:
+            ts(("ha", s0 * 4, s1 * 4), ("hd", s0 * 4, s1 * 4), W - 1, A.bitwise_and)
+        else:
+            cp(("hx", s0 * 4, s1 * 4), ("ha", s0 * 4, s1 * 4))
+
+    def gaps(s):
+        k = s % Q
+        for c in range(4):
+            act(("pN", DQ + c * 16, DQ + c * 16 + 16), ("aL", c * 16, c * 16 + 16), AF.Identity,
+                bias=("qL", k * 4 + c, k * 4 + c + 1), scale=-1.0)
+
+    def tails(s):
+        k = s % Q
+        act(("q16", 0, 4), ("qL", k * 4, k * 4 + 4), AF.Copy, scale=0.0625)
+        for c in range(4):
+            act(("junk", c * 16, c * 16 + 16), ("pN", UU + c * 16, UU + c * 16 + 16), AF.Identity, bias=("q16", c, c + 1), scale=-1.0,
+                acc=("qL", k * 4 + c, k * 4 + c + 1))
+
+    def convert(k):
+        act(("R", k * NW, (k + 1) * NW), ("r0b", k * NW, (k + 1) * NW), AF.Copy)
+
+    def prod(s, lo, hi):
+        tt(("p", lo, hi), ("R" if s else "r0b", 0, W, ("ix", s * C + lo // 16, s * C + hi // 16)), ("w", lo, hi), A.mult)
+
+    def prod2(lo, hi):
+        tt(("p", lo, hi), ("ptp", lo, hi), ("x", lo, hi), A.mult)
+
+    def taps(s, lo, hi):
+        act(("x", lo, hi), ("R" if s else "r0b", 0, W, ("ix", s * C + lo // 16, s * C + hi // 16)), AF.Copy)
+
+    mine = [j for j in jobs if j[0] == core]
+    taken, masks = [], {}
+    for j in sorted(mine, key=lambda j: j[2] is not None):
+        masks[j[3]] = pick(topo, core, j[1] if j[2] is None else j[2], taken)
+
+    def pass_on(s):
+        def fn(e):
+            trs = []
+            for (src, dst, via, b) in mine:
+                rid, pid = topo.addr(dst if via is None else via, core)
+                lo = s * C + b * 32
+                trs.append(RemoteDMATransfer(dst_ids=[DstId(rid=rid, pnc=pid)], dma_engine_mask=masks[b],
+                                             remote_sem=T.sem["arr%d" % s], src=T.send[:, lo:lo + 32], dst=T.land[:, lo:lo + 32]))
+            return e.remote_dma_fused(trs, local_sem=T.sem.sent)
+        add("G", fn, [("send", s * C, (s + 1) * C)], [], ("sent", 2 * ENG * S))
+        add(None, None, [], [("land", s * C, (s + 1) * C)], ("arr%d" % s, 2 * ENG))
+
+    def take_in(s):
+        cp(("R", 0, W, ("ntu", s * 4, s * 4 + 4)), ("land", s * C, (s + 1) * C))
+        for part in ((2, 0, 1), (1, 2, 0), (0, 1, 2))[PMODE]:
+            if part == 2:
+                act(("xq", 0, C), ("R", 0, W, ("hx", (s + 1) * 4, (s + 1) * 4 + 4)), AF.Copy)
+            else:
+                taps(s + 1, part * H, (part + 1) * H)
+
+    IDX = ("idx", 0, 4)
+
+    def new_weight():
+        cp(("w", 0, 2 * NW, IDX), ("quart", 0, C))
+
+    def new_delay(s):
+        tt(("aL", 0, C), ("pN", UU, UU + C), ("aL", 0, C), A.add)
+
+    def small_a(s):
+        gaps(s)
+        if s < S - 1:
+            off_a(s + 1, [0])
+        far(0)
+        if s < S - 1:
+            off_a(s + 1, [1, 2])
+
+    def small_b(s):
+        far(1)
+        if s < S - 1:
+            off_a(s + 1, [3])
+        far(2)
+        if s < S - 1:
+            off_b(s + 1)
+
+    off_a(0, range(4))
+    off_b(0)
+    act(("w", 0, NW), ("w0b", 0, NW, ("lu", L_W, L_W + C)), AF.Copy)
+    ts(("rot", 128, 256), ("iX", 0, 128), PAR, A.is_equal)
+    ts(("i512", 0, 128), ("iX", 0, 128), PAR, A.is_equal, 512.0, A.mult)
+    ts(("vot", 0, 144), ("iX", 0, 144), ("pg", 2, 3), A.is_equal, 65536.0, A.mult)
+    cp(("lu", L_E, L_E + C), ("i1", 0, C))
+    off_c(0)
+    ts(("lu", L_R, L_R + 32), ("iX", 0, 32), 16.0, A.mult, 15.0, A.add)
+    cp(("lu", L_C, L_C + 4), ("iX", 0, 4))
+    off_d(0)
+    cp(("ntu", 0, 24), ("nti", 0, 24))
+    ts(("colL", 0, C), ("iX", 0, C), ("pg", 0, 1), A.add)
+    ts(("colN", 0, C), ("iC", 0, C), ROW, A.add)
+    ts(("cWL", 0, C), ("colL", 0, C), -1.0, A.mult, NW - 1.0, A.add)
+    ts(("cWN", 0, C), ("colN", 0, C), -1.0, A.mult, NW - 1.0, A.add)
+    off_a(1, range(4))
+    off_b(1)
+    convert(0)
+    taps(0, 0, NW)
+    prod(0, 0, NW)
+    cp(("qL", 0, 12), ("qui", 0, 12))
+    gaps(0)
+    for s in range(S):
+        last = s == S - 1
+        late = s < LATE
+        early = 0 < s <= LATE
+        scan(("Y", 0, NW), ("mmul", 0, NW), ("p", 0, NW), A.mult, A.subtract)
+        if s and not early:
+            new_delay(s)
+        if s:
+            small_a(s)
+        else:
+            off_c(1)
+        tt(("df", 0, C), ("Y", 0, NW, ("lu", L_W + 60, L_W + C)), ("d0b", s * C, (s + 1) * C), A.add)
+        if s:
+            cp(("x", 0, 2 * NW, IDX), ("xq", 0, C))
+        else:
+            off_d(1)
+        ts(("e", 0, C), ("df", 0, C), -2.0, A.max, 2.0, A.min)
+        off = 128 - 16 * (1 + s)
+        mm(("pE", 0, C), ("rot", off, off + 128), ("e", 0, C), True, True)
+        act(("send", s * C, (s + 1) * C), ("pE", 0, C), AF.Copy)
+        pass_on(s)
+        if s and not early:
+            new_weight()
+        if s:
+            small_b(s)
+        else:
+            heads(1, Q + 1, 0)
+            for k in range(3):
+                far(k)
+        for h in range(2):
+            tt(half("t", h), ("e", 0, C, ("lu", L_E + h * 32, L_E + h * 32 + 32)), half("x", h), A.mult)
+            act(half("ptp", h), half("t", h), AF.Copy, scale=0.015625)
+        tt(half("w", 0), half("ptp", 0), half("w", 0), A.add)
+        act(half("pm", 0), half("w", 0), AF.Abs)
+        if s == 0:
+            heads(1, Q + 1, 1)
+        elif not last:
+            off_c(s + 1)
+        tt(half("w", 1), half("ptp", 1), half("w", 1), A.add)
+        act(half("pm", 1), half("w", 1), AF.Abs)
+        if s == 0:
+            heads(1, Q + 1, 2)
+        elif not last:
+            off_d(s + 1)
+        if not last:
+            for h in range(2 - PMODE, 2):
+                mm(half("ptp", h), ("rot", 0, 128), half("w", h), True, True)
+        mm(("pK", KW, KW + C), ("rot", 0, 128), ("cWN" if last else "cWL", 0, C), True, False)
+        mm(("pK", KS, KS + C), ("rot", 0, 128), ("cS", 0, C), True, False)
+        mm(("pK", KS, KS + C), ("i512", 0, 128), ("sgn", 0, C), False, False)
+        for h in range(2):
+            scan(half("smin", h), ("madd", 0, H), half("pm", h), A.add, A.min)
+            act(half("rmin", h), half("smin", h) + (("lu", L_R, L_R + 32),), AF.Copy)
+            if s == 2:
+                heads(Q + 1, S, h)
+            scan(half("smax", h), ("mmul", 0, H), half("pm", h), A.mult, A.max)
+            act(half("rmax", h), half("smax", h) + (("lu", L_R, L_R + 32),), AF.Copy)
+        if s == 2:
+            heads(Q + 1, S, 2)
+        if s == 0:
+            for k in range(1, 4):
+                convert(k)
+        n = 0
+        for h in range(2):
+            for (kb, rb, col) in (("kmin", "rmin", KW), ("kmax", "rmax", KS)):
+                if n == RPOS and not last and not late:
+                    take_in(s)
+                n += 1
+                tt(half(kb, h), half("pm", h), half(rb, h), A.is_equal)
+                for j in range(8 * h, 8 * h + 8):
+                    mm(("pK", col, col + C), ("vot", 15 - j, 143 - j), (kb, j * C, (j + 1) * C), False, j == 15)
+
+        def big(k, now=False):
+            lo, hi = k * 256, k * 256 + 256
+            if last:
+                if k == 0:
+                    cp(("p", lo, hi), ("w", 0, NW, ("lu", L_W, L_W + 16)))
+            elif late and not now:
+                pass
+            elif k < 4 - 2 * PMODE:
+                prod(s + 1, lo, hi)
+            else:
+                prod2(lo, hi)
+        if last:
+            store("Y", T.yr[:], ("land", s * C, (s + 1) * C), "st_a", 32)
+            act(("p", 256, NW), ("w", 0, NW, ("lu", L_W + 16, L_W + C)), AF.Copy)
+        big(0)
+        scan(("M", 0, 2 * C), ("mmul", 0, 2 * C), ("pK", KW, KW + 2 * C), A.mult, A.max)
+        big(1)
+        tt(("D", 0, 4), ("M", C + 15, 2 * C, 16), ("M", 15, C, 16), A.subtract)
+        big(2)
+        ts(("Z", 0, 4), ("D", 0, 4), W - 1, A.bitwise_and)
+        big(3)
+        cp(IDX, ("Z", 0, 4))
+        tt(("hit", 0, C), ("Z", 0, 4, ("lu", L_C, L_C + 4)), ("colN" if last else "colL", 0, C), A.is_equal)
+        if last:
+            cp(("p", 0, 2 * NW, IDX), ("quart", 0, C))
+            store("Y", T.yw[:], ("p", 0, NW), "st_a", 32)
+        elif late:
+            new_weight()
+        else:
+            ts(("p", 0, 2 * NW, IDX), ("xq", 0, C), 0.25, A.mult, 0.0, A.add)
+        tt(("pN", UU, UU + C), ("pN", DQ, DQ + C), ("hit", 0, C), A.mult)
+        if last:
+            for c in range(4):
+                tt(("ydb", c, C, 4), ("pN", UU + c * 16, UU + c * 16 + 16), ("aL", c * 16, c * 16 + 16), A.add)
+        if late and not last:
+            new_delay(s + 1)
+        tails(s)
+        if late and not last:
+            take_in(s)
+            prod(s + 1, 0, H)
+            if PMODE:
+                prod2(H, NW)
+            else:
+                prod(s + 1, H, NW)
+            ts(("p", 0, 2 * NW, IDX), ("xq", 0, C), 0.25, A.mult, 0.0, A.add)
+    store("S", T.yd[:], ("ydb", 0, C), "st_b", 32)
+    store("S", T.yq[:], ("qL", 0, 12), "st_b", 32)
+    emit(g, T, ops)
+    g.sync.wait_ge(T.sem.st_a, 32)
+    g.scalar.wait_ge(T.sem.st_b, 32)
+    g.wait_ge(T.sem.sent, 2 * ENG * S)

@@ -3,49 +3,62 @@ from concourse.mybir import AluOpType, ActivationFunctionType
 
 TP, C, W, S, Q = 16, 64, 4096, 6, 3
 NW = TP * C
-H = NW // 2
+QW = NW // 4
+SL = TP + 1
+NP = SL * C
+FAR = 2048
+AQ = C + 4 * Q
+BANK = 512
 ENG = 8
-RCH = 2
-KW, KS = H - C, H
-PMODE = 1
-RPOS = 3
+RCUT = 2560
+OFF = 2
+RPOS = 8
+PA = 7
 LATE = 1
+VG = 5
+VS = 2
+WIDE = 1
+CUT = 0
+LOOSE = 0
+SG = 0
+P1, P2, P3 = 10, 13, 16
+XFIRST = 1
+SPLIT = 0
 
 F, B, I, U = "float32", "bfloat16", "int32", "uint16"
 SCRATCH = {
     "r0b": ("sbuf", [128, W], B), "R": ("sbuf", [128, W], F),
     "w0b": ("sbuf", [128, NW], B), "d0b": ("sbuf", [128, S * C], B),
     "dli": ("sbuf", [128, C], I), "qui": ("sbuf", [128, 12], I), "nti": ("sbuf", [128, 24], I),
-    "w": ("sbuf", [128, 2 * NW], F), "p": ("sbuf", [128, 2 * NW], F), "x": ("sbuf", [128, 2 * NW], F),
+    "w": ("sbuf", [128, FAR + NW], F), "x": ("sbuf", [128, FAR + NW], F), "p": ("sbuf", [128, FAR + NP], F),
     "xq": ("sbuf", [128, C], F), "quart": ("sbuf", [128, C], F),
-    "Y": ("sbuf", [128, NW], F), "df": ("sbuf", [128, C], F), "e": ("sbuf", [128, C], F),
-    "t": ("sbuf", [128, NW], F),
-    "smin": ("sbuf", [128, NW], F), "smax": ("sbuf", [128, NW], F),
-    "rmin": ("sbuf", [128, NW], F), "rmax": ("sbuf", [128, NW], F),
+    "Y": ("sbuf", [128, NP], F), "t": ("sbuf", [128, NW], F), "ms": ("sbuf", [128, 2 * QW], F),
+    "l1": ("sbuf", [128, 2 * QW], F), "l2": ("sbuf", [128, QW], F), "l3": ("sbuf", [128, 2 * C], F), "l4": ("sbuf", [128, 4 * C], F),
     "kmin": ("sbuf", [128, NW], B), "kmax": ("sbuf", [128, NW], B),
-    "mmul": ("sbuf", [128, NW], B), "madd": ("sbuf", [128, H], B),
-    "M": ("sbuf", [128, 2 * C], F), "D": ("sbuf", [128, 4], I), "Z": ("sbuf", [128, 4], I), "idx": ("sbuf", [128, 4], U),
-    "aL": ("sbuf", [128, C], F), "qL": ("sbuf", [128, 12], F), "nL": ("sbuf", [128, 24], F), "ntu": ("sbuf", [128, 24], U),
+    "msum": ("sbuf", [128, NP], B), "mkey": ("sbuf", [128, 48], B),
+    "M": ("sbuf", [128, 3 * C], F), "D": ("sbuf", [128, 8], I), "Z": ("sbuf", [128, 8], I), "idx": ("sbuf", [128, 8], U),
+    "aq": ("sbuf", [128, AQ], F), "nL": ("sbuf", [128, 24], F), "ntu": ("sbuf", [128, 24], U),
     "g1": ("sbuf", [128, C], F), "g2": ("sbuf", [128, C], F), "sgn": ("sbuf", [128, C], B),
     "hit": ("sbuf", [128, C], F), "q16": ("sbuf", [128, 4], F), "junk": ("sbuf", [128, C], F),
-    "a2": ("sbuf", [128, 256], F), "neg": ("sbuf", [128, 256], B), "tr": ("sbuf", [128, 256], F),
-    "ix": ("sbuf", [128, S * C], U), "hd": ("sbuf", [128, 24], I), "ha": ("sbuf", [128, 24], I), "hx": ("sbuf", [128, 24], U),
+    "a2": ("sbuf", [128, AQ], F), "neg": ("sbuf", [128, AQ], B), "ix": ("sbuf", [128, S * AQ], U),
     "pI": ("sbuf", [128, 1], I), "pb": ("sbuf", [128, 8], I), "pf": ("sbuf", [128, 8], F), "pg": ("sbuf", [128, 8], F),
-    "iX": ("sbuf", [128, 144], F), "i1": ("sbuf", [128, C], F), "iC": ("sbuf", [128, C], F),
-    "lu": ("sbuf", [128, 176], U),
-    "colL": ("sbuf", [128, C], F), "colN": ("sbuf", [128, C], F),
-    "cWL": ("sbuf", [128, C], F), "cWN": ("sbuf", [128, C], F), "cS": ("sbuf", [128, C], F),
-    "rot": ("sbuf", [128, 256], F), "i512": ("sbuf", [128, 128], B), "i2k": ("sbuf", [128, 128], B), "vot": ("sbuf", [128, 144], B),
-    "ydb": ("sbuf", [128, C], F),
+    "iX": ("sbuf", [128, 144], F), "iP": ("sbuf", [128, C], F), "lh": ("sbuf", [128, 4], U),
+    "ky": ("sbuf", [128, 12], F), "cu": ("sbuf", [128, 8], F), "k16": ("sbuf", [128, TP], F),
+    "col": ("sbuf", [128, C], F), "cK": ("sbuf", [128, 3 * C], F),
+    "rot": ("sbuf", [128, 256], F), "nid": ("sbuf", [128, 128], F),
+    "i1k": ("sbuf", [128, 128], B), "i2k": ("sbuf", [128, 128], B), "vot": ("sbuf", [128, 144], B),
     "send": ("sbuf", [128, S * C], F), "land": ("sbuf", [128, S * C], F),
-    "ptp": ("psum", [128, NW], F), "pm": ("psum", [128, NW], F), "pK": ("psum", [128, NW], F),
-    "pE": ("psum", [128, H], F), "pN": ("psum", [128, H], F),
+    "ps": ("psum", [128, 8 * BANK], F),
 }
-SEMAPHORES = (["eV", "eS", "eT", "eG", "ld_s", "ld_w", "ld_d", "ld_q", "sent", "st_a", "st_b"]
-              + ["ld_r%d" % k for k in range(RCH)] + ["arr%d" % s for s in range(S)])
-PSUM = ("ptp", "pm", "pK", "pE", "pN")
-L_E, L_W, L_R, L_C, L_A, L_T = 0, 64, 128, 160, 164, 168
-DQ, UU = 0, C
+SEMAPHORES = (["eV", "eS", "eT", "eG", "ld_s", "ld_w", "ld_d", "ld_q", "ld_r0", "ld_r1", "sent", "st_a", "st_b"]
+              + ["arr%d" % s for s in range(S)])
+PW = [q * BANK for q in range(4)]
+PM = [q * BANK + QW for q in range(4)]
+PT, PE = 4 * BANK, 4 * BANK
+DQ, UU = 5 * BANK, 5 * BANK + C
+PR, PO, PK = 6 * BANK, 6 * BANK + C, 6 * BANK + 4 * C
+PD = 7 * BANK
+KP, KS, KW = 0, C, 2 * C
 
 
 def routes(T, topo):
@@ -80,16 +93,27 @@ def helper_program(g, core, T, topo, job):
     m = pick(topo, core, dst, [])
     for s in range(S):
         piece = T.land[:, s * C + b * 32:s * C + b * 32 + 32]
-        g.wait_ge(T.sem["arr%d" % s], ENG)
+        g.wait_ge(T.sem["arr%d" % s], len(topo.engines(src, core)) if WIDE else ENG)
         g.remote_dma(piece, piece, T.sem["arr%d" % s], T.sem.sent, pid, rid, m)
     g.wait_ge(T.sem.sent, S * ENG)
+
+
+def columns(a):
+    step = a[3] if len(a) == 4 and isinstance(a[3], int) else 1
+    if step == 1:
+        m = ((1 << (a[2] - a[1])) - 1) << a[1]
+    else:
+        m = 0
+        for c in range(a[1], a[2], step):
+            m |= 1 << c
+    return a[0], m, range(a[1] // BANK, (a[2] - 1) // BANK + 1) if a[0] == "ps" else []
 
 
 def emit(g, T, ops):
     qs = {"V": g.vector, "S": g.scalar, "T": g.tensor, "G": g, "Y": g.sync}
     known = {q: {} for q in qs}
     seq = {q: 0 for q in qs}
-    acc = {}
+    acc, held = {}, {}
     for op in ops:
         q = op["q"]
         if op["tok"] is None:
@@ -98,21 +122,18 @@ def emit(g, T, ops):
         else:
             op["key"], op["val"] = op["tok"]
         deps = []
-        for mode, regs in (("r", op["r"]), ("w", op["w"])):
-            for (buf, lo, hi) in regs:
-                ps = buf in PSUM
-                for (o2, m2, l2, h2) in acc.get(buf, []):
-                    same = o2["q"] == q and o2["tok"] is None
-                    if ps and not same:
-                        if l2 // H > (hi - 1) // H or (h2 - 1) // H < lo // H:
-                            continue
-                    elif l2 >= hi or h2 <= lo:
-                        continue
-                    if m2 == "r" and mode == "r" and (same or not ps):
-                        continue
-                    if same and q == "T":
-                        continue
-                    deps.append(o2)
+        touch = [("r", columns(a)) for a in op["r"]] + [("w", columns(a)) for a in op["w"]]
+        for mode, (buf, m, banks) in touch:
+            for k in banks:
+                deps.extend(o2 for q2, o2 in held.get(k, {}).items() if q2 != q)
+            for (o2, mode2, m2) in acc.get((buf, q) if banks else buf, []):
+                if not m & m2 or (mode2 == "r" and mode == "r"):
+                    continue
+                if banks and q == "T" and m == m2 and op["more"]:
+                    continue
+                if LOOSE and mode == "w" and q in "VS" and o2["key"] == q:
+                    continue
+                deps.append(o2)
         op["waits"] = []
         if q is not None:
             kn = known[q]
@@ -132,12 +153,15 @@ def emit(g, T, ops):
             op["clock"] = dict(kn)
         else:
             op["clock"] = {}
-        for mode, regs in (("r", op["r"]), ("w", op["w"])):
-            for (buf, lo, hi) in regs:
-                lst = acc.setdefault(buf, [])
-                if mode == "w" and buf not in PSUM:
-                    lst[:] = [a for a in lst if not (a[2] >= lo and a[3] <= hi)]
-                lst.append((op, mode, lo, hi))
+        for mode, (buf, m, banks) in touch:
+            for k in banks:
+                held.setdefault(k, {})[q] = op
+            lst = acc.setdefault((buf, q) if banks else buf, [])
+            if mode == "w":
+                lst[:] = [a for a in lst if a[2] & ~m or (a[0] is op and a[1] == "r")]
+            else:
+                lst[:] = [a for a in lst if a[1] == "w" or a[2] & ~m or a[0]["key"] != op["key"]]
+            lst.append((op, mode, m))
     cnt = {q: 0 for q in qs}
     for op in ops:
         if op["tok"] is None and op["flag"]:
@@ -167,8 +191,8 @@ def rank_program(g, core, T, topo):
     A, AF = AluOpType, ActivationFunctionType
     ops = []
 
-    def add(q, fn, r, w, tok=None):
-        ops.append({"q": q, "fn": fn, "r": r, "w": w, "tok": tok, "flag": False, "n": len(ops)})
+    def add(q, fn, r, w, tok=None, more=False):
+        ops.append({"q": q, "fn": fn, "r": r, "w": w, "tok": tok, "flag": False, "n": len(ops), "more": more})
 
     def ap(a):
         if len(a) == 3:
@@ -178,7 +202,7 @@ def rank_program(g, core, T, topo):
         return T[a[0]][:, a[1]:a[2]].indirect(ap(a[3]))
 
     def regs(*aps):
-        return [a[:3] for a in aps if isinstance(a, tuple)]
+        return [a for a in aps if isinstance(a, tuple)]
 
     def lists(*aps):
         return [a[3] for a in aps if isinstance(a, tuple) and len(a) == 4 and isinstance(a[3], tuple)]
@@ -187,6 +211,10 @@ def rank_program(g, core, T, topo):
         return ap(a) if isinstance(a, tuple) else a
 
     def tt(out, a, b, op):
+        if CUT and len(out) == len(a) == len(b) == 3 and out[2] - out[1] > C:
+            for o in range(0, out[2] - out[1], C):
+                tt(at(out[0], out[1] + o, C), at(a[0], a[1] + o, C), at(b[0], b[1] + o, C), op)
+            return
         add("V", lambda e: e.tensor_tensor(ap(out), ap(a), ap(b), op), regs(a, b) + lists(out, a), regs(out))
 
     def ts(out, a, s1, op0, s2=None, op1=None):
@@ -216,7 +244,7 @@ def rank_program(g, core, T, topo):
         add("S", lambda e: e.activation(ap(out), ap(a), func, **kw), regs(a, bias) + lists(a), regs(out, acc))
 
     def mm(out, l, r, start, stop):
-        add("T", lambda e: e.matmul(ap(out), ap(l), ap(r), start, stop), regs(l, r), regs(out))
+        add("T", lambda e: e.matmul(ap(out), ap(l), ap(r), start, stop), regs(l, r), regs(out), None, not start)
 
     def iota(out, pat, base, cm=0, integer=False):
         if integer:
@@ -230,304 +258,365 @@ def rank_program(g, core, T, topo):
     def store(q, dst, a, sem, total):
         add(q, lambda e: e.dma_start(dst, ap(a)).then_inc(T.sem[sem], 16), regs(a), [], (sem, total))
 
-    def half(buf, h):
-        return (buf, h * H, (h + 1) * H)
+    def at(buf, lo, n):
+        return (buf, lo, lo + n)
 
-    load("S", ("dli", 0, C), T.dl[:], "ld_s", 32)
-    load("S", ("nti", 0, 24), T.nt[:], "ld_s", 32)
-    load("Y", ("w0b", 0, NW), T.w0[:], "ld_w")
-    for k in range(RCH):
-        lo, hi = k * W // RCH, (k + 1) * W // RCH
-        load("Y", ("r0b", lo, hi), T.r0[:, lo:hi], "ld_r%d" % k)
-    load("Y", ("d0b", 0, S * C), T.d0[:], "ld_d")
-    load("Y", ("qui", 0, 12), T.qu[:], "ld_q")
+    def ps(lo, n):
+        return ("ps", lo, lo + n)
 
-    iota(("pI", 0, 1), [[0, 1]], 0, 1, True)
-    iota(("iX", 0, 144), [[1, 144]], 0)
-    iota(("i1", 0, C), [[1, 16], [16, 4]], 0)
-    iota(("cS", 0, C), [[0, 4], [-W, 16]], 15 * W + 1535)
-    iota(("iC", 0, C), [[16, 4], [C, 16]], 0)
-    fill(("mmul", 0, NW), 1.0)
-    P = ("pI", 0, 1)
-    ts(("pb", 0, 1), P, 15, A.bitwise_and)
-    ts(("pb", 1, 2), P, 3, A.bitwise_and)
-    ts(("pb", 2, 3), P, 16, A.bitwise_and)
-    ts(("pb", 3, 4), P, 2, A.logical_shift_right, 3, A.bitwise_and)
-    ts(("pb", 4, 5), P, 112, A.bitwise_and)
-    ts(("pb", 5, 6), P, 127, A.bitwise_and)
-    fill(("madd", 0, H), 0.0)
-    cp(("pf", 0, 6), ("pb", 0, 6))
-    fill(("mmul", 0, NW, TP), 0.0)
-    ROW, LOW, ODD, MID, GRP, PAR = [("pf", k, k + 1) for k in range(6)]
-    ts(("pg", 0, 1), ROW, 64.0, A.mult)
-    ts(("pg", 1, 2), LOW, 32.0, A.mult, ODD, A.add)
-    ts(("pg", 2, 3), GRP, 15.0, A.add)
-    ts(("lu", L_A, L_A + 2), ("iX", 0, 2), 0.0, A.mult, ROW, A.add)
-    ts(("pg", 3, 4), ("pg", 1, 2), MID, A.add)
-    ts(("lu", L_W, L_W + C), ("i1", 0, C), ("pg", 0, 1), A.add)
-    ts(("rot", 0, 128), ("iX", 0, 128), PAR, A.is_equal)
-    ts(("i2k", 0, 128), ("iX", 0, 128), PAR, A.is_equal, -2048.0, A.mult)
-    ts(("lu", L_T, L_T + 4), ("iX", 0, 4), 4.0, A.mult, ("pg", 3, 4), A.add)
-    fill(("madd", 0, H, TP), 1e20)
-    fill(("quart", 0, C), 0.25)
-    ts(("nL", 0, 24), ("nti", 0, 24), 2048.0, A.add)
-    for c in range(4):
-        cp(("aL", c * 16, c * 16 + 16), ("dli", c, C, 4))
+    def tap(buf, k):
+        return at(buf, k * C, C)
 
-    def far(part):
+    def quarter(buf, q):
+        return at(buf, q * QW, QW)
+
+    def size(k):
+        q, o = k // 4, (k % 4) * C
+        return at("ms", (q // 2) * QW + o, C) if q % 2 else ps(PM[q] + o, C)
+
+    load("S", at("dli", 0, C), T.dl[:], "ld_s", 32)
+    load("S", at("nti", 0, 24), T.nt[:], "ld_s", 32)
+    load("Y", at("w0b", 0, NW), T.w0[:], "ld_w")
+    load("Y", ("r0b", 0, RCUT), T.r0[:, 0:RCUT], "ld_r0")
+    load("Y", ("r0b", RCUT, W), T.r0[:, RCUT:W], "ld_r1")
+    load("Y", at("d0b", 0, S * C), T.d0[:], "ld_d")
+    load("Y", at("qui", 0, 12), T.qu[:], "ld_q")
+
+    helped = range(4, 4 + OFF)
+    iota(at("pI", 0, 1), [[0, 1]], 0, 1, True)
+    iota(at("iX", 0, 144), [[1, 144]], 0)
+    iota(at("iP", 0, C), [[1, 16], [16 * SL, 4]], 0)
+    iota(at("cK", KS, C), [[-W, 16], [0, 4]], 15 * W + FAR - 1 + FAR // 2)
+    fill(at("msum", 0, NP), 1.0)
+    fill(at("mkey", 0, 48), 1.0)
+    P = at("pI", 0, 1)
+    ts(at("pb", 0, 1), P, 15, A.bitwise_and)
+    ts(at("pb", 1, 1), P, 3, A.bitwise_and)
+    ts(at("pb", 2, 1), P, 112, A.bitwise_and)
+    ts(at("pb", 3, 1), P, 127, A.bitwise_and)
+    fill(("msum", 0, NP, SL), 0.0)
+    fill(("msum", TP, NP, SL), -1.0)
+    cp(at("pf", 0, 4), at("pb", 0, 4))
+    fill(("mkey", 0, 48, TP), 0.0)
+    fill(at("quart", 0, C), 0.25)
+    ROW, LOW, GRP, PAR = [at("pf", k, 1) for k in range(4)]
+    ts(at("rot", 0, 128), at("iX", 0, 128), PAR, A.is_equal)
+    ts(at("i2k", 0, 128), at("iX", 0, 128), PAR, A.is_equal, -2048.0, A.mult)
+    ts(at("pg", 0, 1), ROW, -float(SL), A.mult, FAR - 1.0, A.add)
+    ts(at("pg", 1, 1), GRP, 15.0, A.add)
+    ts(at("k16", 0, TP), at("iX", 0, TP), -float(TP), A.add)
+    ts(at("col", 0, C), at("iX", 0, C), 16.0, A.mult, ROW, A.add)
+    ts(at("rot", 128, 128), at("iX", 0, 128), PAR, A.is_equal)
+    ts(at("cK", KP, C), at("iP", 0, C), -1.0, A.mult, at("pg", 0, 1), A.add)
+    ts(at("cK", KW, C), at("col", 0, C), -1.0, A.mult, FAR - 1.0, A.add)
+    ts(at("lh", 0, 4), at("iX", 0, 4), 0.0, A.mult, LOW, A.add)
+    ts(at("cu", 0, 4), at("col", 0, 4), float(SL), A.mult, float(TP), A.add)
+    ts(at("cu", 4, 4), at("col", 0, 4), float(NW), A.add)
+    fill(at("Z", 4, 4), 0)
+    ts(at("i1k", 0, 128), at("iX", 0, 128), PAR, A.is_equal, FAR / 2.0, A.mult)
+    ts(at("vot", 0, 144), at("iX", 0, 144), at("pg", 1, 1), A.is_equal, 65536.0, A.mult)
+    ts(at("nid", 0, 128), at("iX", 0, 128), PAR, A.is_equal, -1.0, A.mult)
+    if OFF:
+        ts(at("cK", KS + 16, 4 * OFF), at("cK", KS + 16, 4 * OFF), 16 * 65536.0, A.add)
+
+    def offsets(s, part, n=AQ):
         if part == 0:
-            act(("g1", 0, C), ("pN", DQ, DQ + C), AF.Abs)
+            for c in range(4):
+                act(("a2", c, n, 4), ("aq", c, n, 4), AF.Identity, bias=at("nL", s * 4 + c, 1), scale=-1.0)
+            act(at("neg", 0, n), at("a2", 0, n), AF.Sign, bias=-2047.5)
         elif part == 1:
-            act(("g2", 0, C), ("g1", 0, C), AF.Abs, bias=-2048.0)
+            mm(ps(PO, n), at("rot", 0, 128), at("a2", 0, n), True, False)
+            mm(ps(PO, n), at("i2k", 0, 128), at("neg", 0, n), False, True)
         else:
-            act(("sgn", 0, C), ("g2", 0, C), AF.Sign, bias=1023.5, scale=-1.0)
+            cp(at("ix", s * AQ, n), ps(PO, n))
 
-    def off_a(s, cs):
-        o = (s % 2) * 128
-        for c in cs:
-            act(("a2", o + c * 32, o + c * 32 + 32), ("aL", c * 16, c * 16 + 16, ("lu", L_A, L_A + 2)), AF.Identity,
-                bias=("nL", s * 4 + c, s * 4 + c + 1), scale=-1.0)
-
-    def off_b(s):
-        o = (s % 2) * 128
-        act(("neg", o, o + 128), ("a2", o, o + 128), AF.Sign, bias=-2047.5)
-        mm(("pE", C + o, C + o + 128), ("rot", 0, 128), ("a2", o, o + 128), True, False)
-        mm(("pE", C + o, C + o + 128), ("i2k", 0, 128), ("neg", o, o + 128), False, True)
-
-    def off_c(s):
-        o = (s % 2) * 128
-        add("V", lambda e: e.transpose(T.tr[:, o:o + 128], T.pE[:, C + o:C + o + 128]), [("pE", C + o, C + o + 128)], [("tr", o, o + 128)])
-
-    def off_d(s):
-        o = (s % 2) * 128
-        cp(("ix", s * C, (s + 1) * C), ("tr", o, o + 128, ("lu", L_T, L_T + 4)))
-
-    def heads(s0, s1, part):
-        k = (s0 - 1) % Q
+    def gaps(s, part):
         if part == 0:
-            tt(("hd", s0 * 4, s1 * 4), ("nti", s0 * 4, s1 * 4), ("qL", k * 4, k * 4 + (s1 - s0) * 4), A.subtract)
+            for c in range(4):
+                act(("ps", DQ + c, DQ + C, 4), ("aq", c, C, 4), AF.Identity, bias=at("aq", C + (s % Q) * 4 + c, 1), scale=-1.0)
         elif part == 1:
-            ts(("ha", s0 * 4, s1 * 4), ("hd", s0 * 4, s1 * 4), W - 1, A.bitwise_and)
+            act(at("g1", 0, C), ps(DQ, C), AF.Abs)
+        elif part == 2:
+            act(at("g2", 0, C), at("g1", 0, C), AF.Abs, bias=-2048.0)
         else:
-            cp(("hx", s0 * 4, s1 * 4), ("ha", s0 * 4, s1 * 4))
+            act(at("sgn", 0, C), at("g2", 0, C), AF.Sign, bias=1023.5, scale=-1.0)
 
-    def gaps(s):
-        k = s % Q
+    def tails(s, part):
+        o = C + (s % Q) * 4
+        if part == 0:
+            act(at("q16", 0, 4), at("aq", o, 4), AF.Copy, scale=0.0625)
+            return
         for c in range(4):
-            act(("pN", DQ + c * 16, DQ + c * 16 + 16), ("aL", c * 16, c * 16 + 16), AF.Identity,
-                bias=("qL", k * 4 + c, k * 4 + c + 1), scale=-1.0)
+            act(("junk", c, C, 4), ("ps", UU + c, UU + C, 4), AF.Identity, bias=at("q16", c, 1), scale=-1.0, acc=at("aq", o + c, 1))
 
-    def tails(s):
-        k = s % Q
-        act(("q16", 0, 4), ("qL", k * 4, k * 4 + 4), AF.Copy, scale=0.0625)
-        for c in range(4):
-            act(("junk", c * 16, c * 16 + 16), ("pN", UU + c * 16, UU + c * 16 + 16), AF.Identity, bias=("q16", c, c + 1), scale=-1.0,
-                acc=("qL", k * 4 + c, k * 4 + c + 1))
+    def keep(quarters):
+        for q in quarters:
+            act(quarter("w", q), ps(PW[q], QW), AF.Copy)
 
-    def convert(k):
-        act(("R", k * NW, (k + 1) * NW), ("r0b", k * NW, (k + 1) * NW), AF.Copy)
+    def desired(s):
+        act(("p", TP, NP, SL), at("d0b", s * C, C), AF.Copy)
 
-    def prod(s, lo, hi):
-        tt(("p", lo, hi), ("R" if s else "r0b", 0, W, ("ix", s * C + lo // 16, s * C + hi // 16)), ("w", lo, hi), A.mult)
+    def early(s):
+        if s < S - 1:
+            offsets(s + 1, 0)
+            offsets(s + 1, 1)
 
-    def prod2(lo, hi):
-        tt(("p", lo, hi), ("ptp", lo, hi), ("x", lo, hi), A.mult)
+    def small(s):
+        if s:
+            gaps(s, 0)
+            tails(s - 1, 0)
+        gaps(s, 1)
+        if s < S - 1:
+            desired(s + 1)
+        gaps(s, 2)
+        if s:
+            tails(s - 1, 1)
+        gaps(s, 3)
 
-    def taps(s, lo, hi):
-        act(("x", lo, hi), ("R" if s else "r0b", 0, W, ("ix", s * C + lo // 16, s * C + hi // 16)), AF.Copy)
+    def window(s, k0, k1):
+        return ("R" if s else "r0b", 0, W, ("ix", s * AQ + 4 * k0, s * AQ + 4 * k1))
+
+    def gather(s, vg=0, between=None):
+        n = 4 if vg < 4 else 3
+        cuts = [vg + (TP - vg) * i // n for i in range(n + 1)]
+        for i in range(n):
+            if between and i == SG:
+                between()
+            act(("x", cuts[i] * C, cuts[i + 1] * C), window(s, cuts[i], cuts[i + 1]), AF.Copy)
+            if s and i == n - 1:
+                o = s * AQ + C + ((s - 1) % Q) * 4
+                act(at("xq", 0, C), ("R", 0, W, at("ix", o, 4)), AF.Copy)
+
+    def own(s, vg):
+        if vg:
+            cp(("x", 0, vg * C), window(s, 0, vg))
+
+    def prod(k0, k1, vg=VS):
+        first = vg + (TP - vg) // (4 if vg < 4 else 3)
+        for k in (list(range(vg, first)) + list(range(vg)) + list(range(first, TP)))[k0:k1]:
+            tt(("p", k, NP, SL), ps(PW[k // 4] + (k % 4) * C, C), tap("x", k), A.mult)
 
     mine = [j for j in jobs if j[0] == core]
     taken, masks = [], {}
     for j in sorted(mine, key=lambda j: j[2] is not None):
-        masks[j[3]] = pick(topo, core, j[1] if j[2] is None else j[2], taken)
+        to = j[1] if j[2] is None else j[2]
+        masks[j[3]] = topo.mask(core, to) if WIDE else pick(topo, core, to, taken)
+    order = [j[3] for j in sorted(mine, key=lambda j: j[2] is None)]
+    sent = S * sum(bin(m).count("1") for m in masks.values())
 
-    def pass_on(s):
+    def pass_on(s, blocks):
         def fn(e):
             trs = []
-            for (src, dst, via, b) in mine:
+            for (src, dst, via, b) in [mine[b] for b in blocks]:
                 rid, pid = topo.addr(dst if via is None else via, core)
                 lo = s * C + b * 32
                 trs.append(RemoteDMATransfer(dst_ids=[DstId(rid=rid, pnc=pid)], dma_engine_mask=masks[b],
                                              remote_sem=T.sem["arr%d" % s], src=T.send[:, lo:lo + 32], dst=T.land[:, lo:lo + 32]))
             return e.remote_dma_fused(trs, local_sem=T.sem.sent)
-        add("G", fn, [("send", s * C, (s + 1) * C)], [], ("sent", 2 * ENG * S))
-        add(None, None, [], [("land", s * C, (s + 1) * C)], ("arr%d" % s, 2 * ENG))
+        add("G", fn, [at("send", s * C + b * 32, 32) for b in blocks], [], ("sent", sent))
 
-    def take_in(s):
-        cp(("R", 0, W, ("ntu", s * 4, s * 4 + 4)), ("land", s * C, (s + 1) * C))
-        for part in ((2, 0, 1), (1, 2, 0), (0, 1, 2))[PMODE]:
-            if part == 2:
-                act(("xq", 0, C), ("R", 0, W, ("hx", (s + 1) * 4, (s + 1) * 4 + 4)), AF.Copy)
-            else:
-                taps(s + 1, part * H, (part + 1) * H)
+    def take_in(s, vg=0, between=None):
+        cp(("R", 0, W, at("ntu", s * 4, 4)), at("land", s * C, C))
+        gather(s + 1, vg, between)
 
-    IDX = ("idx", 0, 4)
+    IP, IW = at("idx", 0, 4), at("idx", 4, 4)
 
-    def new_weight():
-        cp(("w", 0, 2 * NW, IDX), ("quart", 0, C))
+    def fix_p():
+        ts(("p", 0, FAR + NP, IP), at("xq", 0, C), 0.25, A.mult, 0.0, A.add)
 
-    def new_delay(s):
-        tt(("aL", 0, C), ("pN", UU, UU + C), ("aL", 0, C), A.add)
+    def fix_w():
+        cp(("w", 0, FAR + NW, IW), at("quart", 0, C))
 
-    def small_a(s):
-        gaps(s)
-        if s < S - 1:
-            off_a(s + 1, [0])
-        far(0)
-        if s < S - 1:
-            off_a(s + 1, [1, 2])
+    def fix_x():
+        cp(("x", 0, FAR + NW, IW), at("xq", 0, C))
 
-    def small_b(s):
-        far(1)
-        if s < S - 1:
-            off_a(s + 1, [3])
-        far(2)
-        if s < S - 1:
-            off_b(s + 1)
+    def delays(part):
+        if part == 0:
+            act(at("ky", 4, 4), at("ky", 0, 4), AF.Relu)
+            for c in range(4):
+                act(("junk", c, C, 4), at("k16", 0, TP), AF.Abs, bias=at("ky", c, 1))
+            for c in range(4):
+                act(at("ky", 8 + c, 1), at("ky", 4 + c, 1), AF.Identity, bias=at("cu", 4 + c, 1), scale=-float(C))
+            act(at("hit", 0, C), at("junk", 0, C), AF.Relu, bias=1.0, scale=-1.0)
+        elif part == 1:
+            tt(ps(UU, C), ps(DQ, C), at("hit", 0, C), A.mult)
+        else:
+            tt(at("aq", 0, C), ps(UU, C), at("aq", 0, C), A.add)
 
-    off_a(0, range(4))
-    off_b(0)
-    act(("w", 0, NW), ("w0b", 0, NW, ("lu", L_W, L_W + C)), AF.Copy)
-    ts(("rot", 128, 256), ("iX", 0, 128), PAR, A.is_equal)
-    ts(("i512", 0, 128), ("iX", 0, 128), PAR, A.is_equal, 512.0, A.mult)
-    ts(("vot", 0, 144), ("iX", 0, 144), ("pg", 2, 3), A.is_equal, 65536.0, A.mult)
-    cp(("lu", L_E, L_E + C), ("i1", 0, C))
-    off_c(0)
-    ts(("lu", L_R, L_R + 32), ("iX", 0, 32), 16.0, A.mult, 15.0, A.add)
-    cp(("lu", L_C, L_C + 4), ("iX", 0, 4))
-    off_d(0)
-    cp(("ntu", 0, 24), ("nti", 0, 24))
-    ts(("colL", 0, C), ("iX", 0, C), ("pg", 0, 1), A.add)
-    ts(("colN", 0, C), ("iC", 0, C), ROW, A.add)
-    ts(("cWL", 0, C), ("colL", 0, C), -1.0, A.mult, NW - 1.0, A.add)
-    ts(("cWN", 0, C), ("colN", 0, C), -1.0, A.mult, NW - 1.0, A.add)
-    off_a(1, range(4))
-    off_b(1)
-    convert(0)
-    taps(0, 0, NW)
-    prod(0, 0, NW)
-    cp(("qL", 0, 12), ("qui", 0, 12))
-    gaps(0)
+    def votes(key, buf, r, stop):
+        for j in range(r, 16, 2):
+            mm(ps(PK + key, C), at("vot", 15 - j, 128), (buf, j, NW, 16), False, stop and j == 15)
+
+    def convert(lo, hi):
+        act(("R", lo, hi), ("r0b", lo, hi), AF.Copy)
+
+    ts(at("nL", 0, 24), at("nti", 0, 24), 2048.0, A.add)
+    cp(at("aq", 0, C), at("dli", 0, C))
+    offsets(0, 0, C)
+    offsets(0, 1, C)
+    cp(at("ntu", 0, 24), at("nti", 0, 24))
+    cp(at("w", 0, NW), at("w0b", 0, NW))
+    for q in range(4):
+        act(ps(PW[q], QW), quarter("w0b", q), AF.Copy)
+    offsets(0, 2, C)
+    cp(("R", 0, RCUT // 2), ("r0b", 0, RCUT // 2))
+    convert(RCUT // 2, RCUT)
+    gather(0, VG)
+    own(0, VG)
+    desired(0)
+    prod(0, TP, VG)
+    cp(at("aq", C, 12), at("qui", 0, 12))
+    offsets(1, 0)
+    offsets(1, 1)
+    gaps(0, 0)
     for s in range(S):
         last = s == S - 1
         late = s < LATE
-        early = 0 < s <= LATE
-        scan(("Y", 0, NW), ("mmul", 0, NW), ("p", 0, NW), A.mult, A.subtract)
-        if s and not early:
-            new_delay(s)
-        if s:
-            small_a(s)
+        DF = ("Y", TP, NP, SL)
+        turn = at("rot", 128 - 16 * (1 + s), 128)
+        if SPLIT:
+            for n, b in enumerate(order):
+                lo, hi = b * NP // 2, (b + 1) * NP // 2
+                scan(("Y", lo, hi), ("msum", lo, hi), ("p", lo, hi), A.mult, A.add)
+                mm(ps(PR + b * 32, 32), turn, ("Y", lo + TP, hi, SL), True, True)
+                if n == 0:
+                    if s:
+                        cp(IW, at("ky", 8, 4))
+                        delays(1)
+                        fix_x()
+                else:
+                    if s:
+                        fix_w()
+                    ts(ps(PE, C), DF, -2.0, A.max, 2.0, A.min)
+                ts(at("send", s * C + b * 32, 32), ps(PR + b * 32, 32), -2.0, A.max, 2.0, A.min)
+                pass_on(s, [b])
+            if s:
+                delays(2)
         else:
-            off_c(1)
-        tt(("df", 0, C), ("Y", 0, NW, ("lu", L_W + 60, L_W + C)), ("d0b", s * C, (s + 1) * C), A.add)
-        if s:
-            cp(("x", 0, 2 * NW, IDX), ("xq", 0, C))
-        else:
-            off_d(1)
-        ts(("e", 0, C), ("df", 0, C), -2.0, A.max, 2.0, A.min)
-        off = 128 - 16 * (1 + s)
-        mm(("pE", 0, C), ("rot", off, off + 128), ("e", 0, C), True, True)
-        act(("send", s * C, (s + 1) * C), ("pE", 0, C), AF.Copy)
-        pass_on(s)
-        if s and not early:
-            new_weight()
-        if s:
-            small_b(s)
-        else:
-            heads(1, Q + 1, 0)
-            for k in range(3):
-                far(k)
-        for h in range(2):
-            tt(half("t", h), ("e", 0, C, ("lu", L_E + h * 32, L_E + h * 32 + 32)), half("x", h), A.mult)
-            act(half("ptp", h), half("t", h), AF.Copy, scale=0.015625)
-        tt(half("w", 0), half("ptp", 0), half("w", 0), A.add)
-        act(half("pm", 0), half("w", 0), AF.Abs)
-        if s == 0:
-            heads(1, Q + 1, 1)
-        elif not last:
-            off_c(s + 1)
-        tt(half("w", 1), half("ptp", 1), half("w", 1), A.add)
-        act(half("pm", 1), half("w", 1), AF.Abs)
-        if s == 0:
-            heads(1, Q + 1, 2)
-        elif not last:
-            off_d(s + 1)
-        if not last:
-            for h in range(2 - PMODE, 2):
-                mm(half("ptp", h), ("rot", 0, 128), half("w", h), True, True)
-        mm(("pK", KW, KW + C), ("rot", 0, 128), ("cWN" if last else "cWL", 0, C), True, False)
-        mm(("pK", KS, KS + C), ("rot", 0, 128), ("cS", 0, C), True, False)
-        mm(("pK", KS, KS + C), ("i512", 0, 128), ("sgn", 0, C), False, False)
-        for h in range(2):
-            scan(half("smin", h), ("madd", 0, H), half("pm", h), A.add, A.min)
-            act(half("rmin", h), half("smin", h) + (("lu", L_R, L_R + 32),), AF.Copy)
-            if s == 2:
-                heads(Q + 1, S, h)
-            scan(half("smax", h), ("mmul", 0, H), half("pm", h), A.mult, A.max)
-            act(half("rmax", h), half("smax", h) + (("lu", L_R, L_R + 32),), AF.Copy)
-        if s == 2:
-            heads(Q + 1, S, 2)
-        if s == 0:
-            for k in range(1, 4):
-                convert(k)
-        n = 0
-        for h in range(2):
-            for (kb, rb, col) in (("kmin", "rmin", KW), ("kmax", "rmax", KS)):
-                if n == RPOS and not last and not late:
-                    take_in(s)
-                n += 1
-                tt(half(kb, h), half("pm", h), half(rb, h), A.is_equal)
-                for j in range(8 * h, 8 * h + 8):
-                    mm(("pK", col, col + C), ("vot", 15 - j, 143 - j), (kb, j * C, (j + 1) * C), False, j == 15)
+            scan(at("Y", 0, NP), at("msum", 0, NP), at("p", 0, NP), A.mult, A.add)
+            mm(ps(PR, C), turn, DF, True, True)
+            if s:
+                cp(IW, at("ky", 8, 4))
+                delays(1)
+            ts(ps(PE, C), DF, -2.0, A.max, 2.0, A.min)
+            if s:
+                fix_x()
+                delays(2)
+            ts(at("send", s * C, C), ps(PR, C), -2.0, A.max, 2.0, A.min)
+            for bs in ([[b] for b in order] if WIDE else [order]):
+                pass_on(s, bs)
+            if s:
+                early(s)
+            if s and XFIRST:
+                fix_w()
+        add(None, None, [], [at("land", s * C, C)], ("arr%d" % s, 2 * ENG))
+        for q in range(4):
+            for k in range(4 * q, 4 * q + 4):
+                tt(tap("t", k), ps(PE, C), tap("x", k), A.mult)
+            act(ps(PW[q], QW), quarter("t", q), AF.Copy, scale=0.015625)
+            if s and q == 2 and not SPLIT and not XFIRST:
+                fix_w()
+        for q in range(4):
+            tt(ps(PW[q], QW), ps(PW[q], QW), quarter("w", q), A.add)
+            act(at("ms", (q // 2) * QW, QW) if q % 2 else ps(PM[q], QW), ps(PW[q], QW), AF.Abs)
 
-        def big(k, now=False):
-            lo, hi = k * 256, k * 256 + 256
-            if last:
-                if k == 0:
-                    cp(("p", lo, hi), ("w", 0, NW, ("lu", L_W, L_W + 16)))
-            elif late and not now:
-                pass
-            elif k < 4 - 2 * PMODE:
-                prod(s + 1, lo, hi)
-            else:
-                prod2(lo, hi)
+        if OFF:
+            mm(ps(PD, OFF * C), at("rot", 0, 128), at("ms", 0, OFF * C), True, False)
+        both = ((0, A.min), (1, A.max))
+        spec = not last and not late
+        for (h, op) in both:
+            tt(ps(PT + h * QW, QW), ps(PM[0], QW), at("ms", 0, QW), op)
+        for q in (1, 3):
+            act(ps(PM[q], QW), ps(PW[q], QW), AF.Abs)
+        small(s)
         if last:
-            store("Y", T.yr[:], ("land", s * C, (s + 1) * C), "st_a", 32)
-            act(("p", 256, NW), ("w", 0, NW, ("lu", L_W + 16, L_W + C)), AF.Copy)
-        big(0)
-        scan(("M", 0, 2 * C), ("mmul", 0, 2 * C), ("pK", KW, KW + 2 * C), A.mult, A.max)
-        big(1)
-        tt(("D", 0, 4), ("M", C + 15, 2 * C, 16), ("M", 15, C, 16), A.subtract)
-        big(2)
-        ts(("Z", 0, 4), ("D", 0, 4), W - 1, A.bitwise_and)
-        big(3)
-        cp(IDX, ("Z", 0, 4))
-        tt(("hit", 0, C), ("Z", 0, 4, ("lu", L_C, L_C + 4)), ("colN" if last else "colL", 0, C), A.is_equal)
+            keep([1, 3, 0])
+        kw, ks = (C, 0) if last else (0, C)
+        for (h, op) in both:
+            tt(at("l1", h * QW, QW), ps(PM[2], QW), at("ms", QW, QW), op)
         if last:
-            cp(("p", 0, 2 * NW, IDX), ("quart", 0, C))
-            store("Y", T.yw[:], ("p", 0, NW), "st_a", 32)
-        elif late:
-            new_weight()
+            keep([2])
+        for (h, op) in both:
+            for half in range(2):
+                o = PT + h * QW + half * 2 * C
+                tt(at("l2", h * 2 * C, 2 * C) if half else ps(o, 2 * C), ps(o, 2 * C), at("l1", h * QW + half * 2 * C, 2 * C), op)
+        for (h, op) in both:
+            for half in range(2):
+                o = PT + h * QW + half * C
+                tt(at("l3", h * C, C) if half else ps(o, C), ps(o, C), at("l2", h * 2 * C + half * C, C), op)
+            if h == 0 and not last:
+                offsets(s + 1, 2)
+        mm(ps(PK, 2 * C), at("rot", 0, 128), at("cK", kw, 2 * C), True, False)
+        for (h, op) in both:
+            for half in range(2):
+                o = PT + h * QW
+                tt(at("l4", (2 * h + half) * C, C), ps(o, C), at("l3", h * C, C), op)
+        for k in range(OFF):
+            mm(ps(PD + k * C, C), at("nid", 0, 128), at("l4", 2 * C, C), False, k == OFF - 1)
+        mm(ps(PK + ks, C), at("i1k", 0, 128), at("sgn", 0, C), False, False)
+
+        def signs():
+            if OFF:
+                act(at("kmax", QW, OFF * C), ps(PD, OFF * C), AF.Sign)
+        if not (spec and SG):
+            signs()
+        if s == 0:
+            convert(RCUT, W)
+        todo = [(r, h, k) for h in range(2) for r in range(2) for k in range(0, TP, 2) if h == 0 or k not in helped]
+        for n, (r, h, k) in enumerate(todo):
+            if n == len(todo) - RPOS and spec:
+                take_in(s, VS, signs if SG else None)
+            o = PM[k // 4] + (k % 4) * C
+            tt(("kmax" if h else "kmin", k * C + r, (k + 2) * C, 2), ("ps", o + r, o + 2 * C, 2),
+               ("l4", 2 * h * C + r, 2 * (h + 1) * C, 2), A.is_equal)
+            if n + 1 == len(todo) or todo[n + 1][0] != r:
+                votes(ks if h else kw, "kmax" if h else "kmin", r, n + 1 == len(todo))
+        if last:
+            store("Y", T.yr[:], at("land", s * C, C), "st_a", 32)
+        if spec:
+            if RPOS == 0:
+                take_in(s, VS)
+            own(s + 1, VS)
+            prod(0, PA)
+        for c in range(4):
+            scan(("M", c, 2 * C, 4), at("mkey", 0, 32), ("ps", PK + c, PK + 2 * C, 4), A.mult, A.max)
+        if spec:
+            prod(PA, P1)
+        tt(at("D", 0, 4), at("M", ks + 60, 4), at("M", kw + 60, 4), A.subtract)
+        if spec:
+            prod(P1, P2)
+        ts(at("Z", 0, 4), at("D", 0, 4), W - 1, A.bitwise_and)
+        if spec:
+            prod(P2, P3)
+        if last:
+            cp(IW, at("Z", 0, 4))
+            tails(s, 0)
+            tt(at("hit", 0, C), ("Z", 0, 8, at("lh", 0, 4)), at("col", 0, C), A.is_equal)
+            fix_w()
+            store("Y", T.yw[:], at("w", 0, NW), "st_a", 32)
+            delays(1)
+            delays(2)
         else:
-            ts(("p", 0, 2 * NW, IDX), ("xq", 0, C), 0.25, A.mult, 0.0, A.add)
-        tt(("pN", UU, UU + C), ("pN", DQ, DQ + C), ("hit", 0, C), A.mult)
-        if last:
-            for c in range(4):
-                tt(("ydb", c, C, 4), ("pN", UU + c * 16, UU + c * 16 + 16), ("aL", c * 16, c * 16 + 16), A.add)
-        if late and not last:
-            new_delay(s + 1)
-        tails(s)
-        if late and not last:
-            take_in(s)
-            prod(s + 1, 0, H)
-            if PMODE:
-                prod2(H, NW)
+            cp(IP, at("Z", 0, 4))
+            if late:
+                take_in(s, VG)
+                tt(at("ky", 0, 4), at("cu", 0, 4), at("Z", 0, 4), A.subtract)
+                own(s + 1, VG)
+                prod(0, TP, VG)
+                delays(0)
+                keep(range(4))
+                fix_p()
             else:
-                prod(s + 1, H, NW)
-            ts(("p", 0, 2 * NW, IDX), ("xq", 0, C), 0.25, A.mult, 0.0, A.add)
-    store("S", T.yd[:], ("ydb", 0, C), "st_b", 32)
-    store("S", T.yq[:], ("qL", 0, 12), "st_b", 32)
+                prod(P3, TP)
+                tt(at("ky", 0, 4), at("cu", 0, 4), at("Z", 0, 4), A.subtract)
+                keep(range(1))
+                delays(0)
+                fix_p()
+                keep(range(1, 4))
+    tails(S - 1, 1)
+    store("S", T.yd[:], at("aq", 0, C), "st_b", 32)
+    store("S", T.yq[:], at("aq", C, 12), "st_b", 32)
     emit(g, T, ops)
     g.sync.wait_ge(T.sem.st_a, 32)
     g.scalar.wait_ge(T.sem.st_b, 32)
-    g.wait_ge(T.sem.sent, 2 * ENG * S)
+    g.wait_ge(T.sem.sent, sent)

@@ -4,7 +4,8 @@ from concourse.mybir import AluOpType, ActivationFunctionType
 TP, C, W, S, Q = 16, 64, 4096, 6, 3
 NW = TP * C
 QW = NW // 4
-SL = TP + 1
+SL = TP + 4
+HUGE = 2.0 ** 60
 NP = SL * C
 FAR = 2048
 AQ = C + 4 * Q
@@ -12,17 +13,17 @@ BANK = 512
 ENG = 8
 RCUT = 2560
 OFF = 2
-RPOS = 8
+RPOS = 6
 PA = 7
 LATE = 1
 VG = 5
-VS = 2
+VS = 3
 WIDE = 1
 CUT = 0
 LOOSE = 0
 SG = 0
 P1, P2, P3 = 10, 13, 16
-XFIRST = 1
+XFIRST = 0
 SPLIT = 0
 
 F, B, I, U = "float32", "bfloat16", "int32", "uint16"
@@ -35,7 +36,7 @@ SCRATCH = {
     "Y": ("sbuf", [128, NP], F), "t": ("sbuf", [128, NW], F), "ms": ("sbuf", [128, 2 * QW], F),
     "l1": ("sbuf", [128, 2 * QW], F), "l2": ("sbuf", [128, QW], F), "l3": ("sbuf", [128, 2 * C], F), "l4": ("sbuf", [128, 4 * C], F),
     "kmin": ("sbuf", [128, NW], B), "kmax": ("sbuf", [128, NW], B),
-    "msum": ("sbuf", [128, NP], B), "mkey": ("sbuf", [128, 48], B),
+    "mkey": ("sbuf", [128, 48], B),
     "M": ("sbuf", [128, 3 * C], F), "D": ("sbuf", [128, 8], I), "Z": ("sbuf", [128, 8], I), "idx": ("sbuf", [128, 8], U),
     "aq": ("sbuf", [128, AQ], F), "nL": ("sbuf", [128, 24], F), "ntu": ("sbuf", [128, 24], U),
     "g1": ("sbuf", [128, C], F), "g2": ("sbuf", [128, C], F), "sgn": ("sbuf", [128, C], B),
@@ -45,7 +46,7 @@ SCRATCH = {
     "iX": ("sbuf", [128, 144], F), "iP": ("sbuf", [128, C], F), "lh": ("sbuf", [128, 4], U),
     "ky": ("sbuf", [128, 12], F), "cu": ("sbuf", [128, 8], F), "k16": ("sbuf", [128, TP], F),
     "col": ("sbuf", [128, C], F), "cK": ("sbuf", [128, 3 * C], F),
-    "rot": ("sbuf", [128, 256], F), "nid": ("sbuf", [128, 128], F),
+    "rot": ("sbuf", [128, 256], F), "nid": ("sbuf", [128, 256], F),
     "i1k": ("sbuf", [128, 128], B), "i2k": ("sbuf", [128, 128], B), "vot": ("sbuf", [128, 144], B),
     "send": ("sbuf", [128, S * C], F), "land": ("sbuf", [128, S * C], F),
     "ps": ("psum", [128, 8 * BANK], F),
@@ -287,15 +288,15 @@ def rank_program(g, core, T, topo):
     iota(at("iX", 0, 144), [[1, 144]], 0)
     iota(at("iP", 0, C), [[1, 16], [16 * SL, 4]], 0)
     iota(at("cK", KS, C), [[-W, 16], [0, 4]], 15 * W + FAR - 1 + FAR // 2)
-    fill(at("msum", 0, NP), 1.0)
+    fill(("p", TP + 1, NP, SL), 0.0)
     fill(at("mkey", 0, 48), 1.0)
     P = at("pI", 0, 1)
     ts(at("pb", 0, 1), P, 15, A.bitwise_and)
     ts(at("pb", 1, 1), P, 3, A.bitwise_and)
     ts(at("pb", 2, 1), P, 112, A.bitwise_and)
     ts(at("pb", 3, 1), P, 127, A.bitwise_and)
-    fill(("msum", 0, NP, SL), 0.0)
-    fill(("msum", TP, NP, SL), -1.0)
+    fill(("p", TP + 2, NP, SL), HUGE)
+    fill(("p", TP + 3, NP, SL), -HUGE)
     cp(at("pf", 0, 4), at("pb", 0, 4))
     fill(("mkey", 0, 48, TP), 0.0)
     fill(at("quart", 0, C), 0.25)
@@ -306,7 +307,6 @@ def rank_program(g, core, T, topo):
     ts(at("pg", 1, 1), GRP, 15.0, A.add)
     ts(at("k16", 0, TP), at("iX", 0, TP), -float(TP), A.add)
     ts(at("col", 0, C), at("iX", 0, C), 16.0, A.mult, ROW, A.add)
-    ts(at("rot", 128, 128), at("iX", 0, 128), PAR, A.is_equal)
     ts(at("cK", KP, C), at("iP", 0, C), -1.0, A.mult, at("pg", 0, 1), A.add)
     ts(at("cK", KW, C), at("col", 0, C), -1.0, A.mult, FAR - 1.0, A.add)
     ts(at("lh", 0, 4), at("iX", 0, 4), 0.0, A.mult, LOW, A.add)
@@ -315,7 +315,8 @@ def rank_program(g, core, T, topo):
     fill(at("Z", 4, 4), 0)
     ts(at("i1k", 0, 128), at("iX", 0, 128), PAR, A.is_equal, FAR / 2.0, A.mult)
     ts(at("vot", 0, 144), at("iX", 0, 144), at("pg", 1, 1), A.is_equal, 65536.0, A.mult)
-    ts(at("nid", 0, 128), at("iX", 0, 128), PAR, A.is_equal, -1.0, A.mult)
+    for o in (0, 128):
+        ts(at("nid", o, 128), at("iX", 0, 128), PAR, A.is_equal, -1.0, A.mult)
     if OFF:
         ts(at("cK", KS + 16, 4 * OFF), at("cK", KS + 16, 4 * OFF), 16 * 65536.0, A.add)
 
@@ -354,7 +355,7 @@ def rank_program(g, core, T, topo):
             act(quarter("w", q), ps(PW[q], QW), AF.Copy)
 
     def desired(s):
-        act(("p", TP, NP, SL), at("d0b", s * C, C), AF.Copy)
+        act(("p", TP, NP, SL), at("d0b", s * C, C), AF.Copy, scale=-1.0)
 
     def early(s):
         if s < S - 1:
@@ -467,58 +468,46 @@ def rank_program(g, core, T, topo):
     prod(0, TP, VG)
     cp(at("aq", C, 12), at("qui", 0, 12))
     offsets(1, 0)
-    offsets(1, 1)
     gaps(0, 0)
     for s in range(S):
         last = s == S - 1
         late = s < LATE
-        DF = ("Y", TP, NP, SL)
-        turn = at("rot", 128 - 16 * (1 + s), 128)
-        if SPLIT:
-            for n, b in enumerate(order):
-                lo, hi = b * NP // 2, (b + 1) * NP // 2
-                scan(("Y", lo, hi), ("msum", lo, hi), ("p", lo, hi), A.mult, A.add)
-                mm(ps(PR + b * 32, 32), turn, ("Y", lo + TP, hi, SL), True, True)
-                if n == 0:
-                    if s:
-                        cp(IW, at("ky", 8, 4))
-                        delays(1)
-                        fix_x()
-                else:
-                    if s:
-                        fix_w()
-                    ts(ps(PE, C), DF, -2.0, A.max, 2.0, A.min)
-                ts(at("send", s * C + b * 32, 32), ps(PR + b * 32, 32), -2.0, A.max, 2.0, A.min)
-                pass_on(s, [b])
-            if s:
-                delays(2)
-        else:
-            scan(at("Y", 0, NP), at("msum", 0, NP), at("p", 0, NP), A.mult, A.add)
-            mm(ps(PR, C), turn, DF, True, True)
-            if s:
-                cp(IW, at("ky", 8, 4))
-                delays(1)
-            ts(ps(PE, C), DF, -2.0, A.max, 2.0, A.min)
-            if s:
-                fix_x()
-                delays(2)
+        DF = ("Y", TP // 2, NP // 2, SL // 2)
+        turn = at("nid", 128 - 16 * (1 + s), 128)
+        scan(at("Y", 0, NP // 2), ("p", 0, NP, 2), ("p", 1, NP, 2), A.add, A.add)
+        mm(ps(PR, C), turn, DF, True, True)
+
+        def leave():
             ts(at("send", s * C, C), ps(PR, C), -2.0, A.max, 2.0, A.min)
             for bs in ([[b] for b in order] if WIDE else [order]):
                 pass_on(s, bs)
-            if s:
+            add(None, None, [], [at("land", s * C, C)], ("arr%d" % s, 2 * ENG))
+        if s:
+            cp(IW, at("ky", 8, 4))
+            delays(1)
+        ts(ps(PE, C), DF, -2.0, A.max, 2.0, A.min)
+        if s:
+            fix_x()
+            if XFIRST:
+                delays(2)
+                leave()
                 early(s)
-            if s and XFIRST:
                 fix_w()
-        add(None, None, [], [at("land", s * C, C)], ("arr%d" % s, 2 * ENG))
+            else:
+                fix_w()
+                leave()
         for q in range(4):
             for k in range(4 * q, 4 * q + 4):
                 tt(tap("t", k), ps(PE, C), tap("x", k), A.mult)
-            act(ps(PW[q], QW), quarter("t", q), AF.Copy, scale=0.015625)
-            if s and q == 2 and not SPLIT and not XFIRST:
-                fix_w()
+            act(ps(PW[q], QW), quarter("t", q), AF.Copy, scale=-0.015625)
+            if s == 0 and q == 0:
+                leave()
+                offsets(1, 1)
         for q in range(4):
             tt(ps(PW[q], QW), ps(PW[q], QW), quarter("w", q), A.add)
             act(at("ms", (q // 2) * QW, QW) if q % 2 else ps(PM[q], QW), ps(PW[q], QW), AF.Abs)
+        if s and not XFIRST:
+            delays(2)
 
         if OFF:
             mm(ps(PD, OFF * C), at("rot", 0, 128), at("ms", 0, OFF * C), True, False)
@@ -526,16 +515,14 @@ def rank_program(g, core, T, topo):
         spec = not last and not late
         for (h, op) in both:
             tt(ps(PT + h * QW, QW), ps(PM[0], QW), at("ms", 0, QW), op)
+        if s and not XFIRST:
+            early(s)
         for q in (1, 3):
             act(ps(PM[q], QW), ps(PW[q], QW), AF.Abs)
         small(s)
-        if last:
-            keep([1, 3, 0])
         kw, ks = (C, 0) if last else (0, C)
         for (h, op) in both:
             tt(at("l1", h * QW, QW), ps(PM[2], QW), at("ms", QW, QW), op)
-        if last:
-            keep([2])
         for (h, op) in both:
             for half in range(2):
                 o = PT + h * QW + half * 2 * C
@@ -544,13 +531,15 @@ def rank_program(g, core, T, topo):
             for half in range(2):
                 o = PT + h * QW + half * C
                 tt(at("l3", h * C, C) if half else ps(o, C), ps(o, C), at("l2", h * 2 * C + half * C, C), op)
-            if h == 0 and not last:
+            if h == 0 and not last and XFIRST:
                 offsets(s + 1, 2)
         mm(ps(PK, 2 * C), at("rot", 0, 128), at("cK", kw, 2 * C), True, False)
         for (h, op) in both:
             for half in range(2):
                 o = PT + h * QW
                 tt(at("l4", (2 * h + half) * C, C), ps(o, C), at("l3", h * C, C), op)
+            if h == 0 and not last and not XFIRST:
+                offsets(s + 1, 2)
         for k in range(OFF):
             mm(ps(PD + k * C, C), at("nid", 0, 128), at("l4", 2 * C, C), False, k == OFF - 1)
         mm(ps(PK + ks, C), at("i1k", 0, 128), at("sgn", 0, C), False, False)
@@ -572,7 +561,8 @@ def rank_program(g, core, T, topo):
             if n + 1 == len(todo) or todo[n + 1][0] != r:
                 votes(ks if h else kw, "kmax" if h else "kmin", r, n + 1 == len(todo))
         if last:
-            store("Y", T.yr[:], at("land", s * C, C), "st_a", 32)
+            keep(range(4))
+            store("Y", T.yr[:], at("land", s * C, C), "st_a", 48)
         if spec:
             if RPOS == 0:
                 take_in(s, VS)
@@ -593,7 +583,7 @@ def rank_program(g, core, T, topo):
             tails(s, 0)
             tt(at("hit", 0, C), ("Z", 0, 8, at("lh", 0, 4)), at("col", 0, C), A.is_equal)
             fix_w()
-            store("Y", T.yw[:], at("w", 0, NW), "st_a", 32)
+            store("Y", T.yw[:], at("w", 0, NW), "st_a", 48)
             delays(1)
             delays(2)
         else:
@@ -614,9 +604,9 @@ def rank_program(g, core, T, topo):
                 fix_p()
                 keep(range(1, 4))
     tails(S - 1, 1)
-    store("S", T.yd[:], at("aq", 0, C), "st_b", 32)
-    store("S", T.yq[:], at("aq", C, 12), "st_b", 32)
+    store("Y", T.yd[:], at("aq", 0, C), "st_a", 48)
+    store("S", T.yq[:], at("aq", C, 12), "st_b", 16)
     emit(g, T, ops)
-    g.sync.wait_ge(T.sem.st_a, 32)
-    g.scalar.wait_ge(T.sem.st_b, 32)
+    g.sync.wait_ge(T.sem.st_a, 48)
+    g.scalar.wait_ge(T.sem.st_b, 16)
     g.wait_ge(T.sem.sent, sent)

@@ -8,18 +8,23 @@ SL = TP + 4
 HUGE = 2.0 ** 60
 NP = SL * C
 FAR = 2048
+HP = NP // 2
+WX = NW + 2 * C
+WITHIN = {"w": ("wb", C), "x": ("xb", C), "xq": ("new", C)}
 AQ = C + 4 * Q
 BANK = 512
 ENG = 8
 RCUT = 2560
 OFF = 2
-RPOS = 6
+RPOS = 14
 PA = 7
-LATE = 1
-VG = 5
-VS = 3
+LATE = 0
+VG = 6
+VS = 2
 WIDE = 1
 CUT = 0
+RMID = 3328
+RP0 = 10
 LOOSE = 0
 SG = 0
 P1, P2, P3 = 10, 13, 16
@@ -31,23 +36,22 @@ SCRATCH = {
     "r0b": ("sbuf", [128, W], B), "R": ("sbuf", [128, W], F),
     "w0b": ("sbuf", [128, NW], B), "d0b": ("sbuf", [128, S * C], B),
     "dli": ("sbuf", [128, C], I), "qui": ("sbuf", [128, 12], I), "nti": ("sbuf", [128, 24], I),
-    "w": ("sbuf", [128, FAR + NW], F), "x": ("sbuf", [128, FAR + NW], F), "p": ("sbuf", [128, FAR + NP], F),
-    "xq": ("sbuf", [128, C], F), "quart": ("sbuf", [128, C], F),
+    "wb": ("sbuf", [128, C + FAR + NW], F), "xb": ("sbuf", [128, WX], F), "p": ("sbuf", [128, 2 * NP], F), "new": ("sbuf", [128, 2 * C], F),
     "Y": ("sbuf", [128, NP], F), "t": ("sbuf", [128, NW], F), "ms": ("sbuf", [128, 2 * QW], F),
-    "l1": ("sbuf", [128, 2 * QW], F), "l2": ("sbuf", [128, QW], F), "l3": ("sbuf", [128, 2 * C], F), "l4": ("sbuf", [128, 4 * C], F),
+    "l1": ("sbuf", [128, 2 * QW], F), "l2": ("sbuf", [128, QW], F), "l3": ("sbuf", [128, 2 * C], F), "l4": ("sbuf", [128, 6 * C], F),
     "kmin": ("sbuf", [128, NW], B), "kmax": ("sbuf", [128, NW], B),
     "mkey": ("sbuf", [128, 48], B),
-    "M": ("sbuf", [128, 3 * C], F), "D": ("sbuf", [128, 8], I), "Z": ("sbuf", [128, 8], I), "idx": ("sbuf", [128, 8], U),
+    "M": ("sbuf", [128, 3 * C], F), "D": ("sbuf", [128, 8], I), "Z": ("sbuf", [128, 8], I), "idx": ("sbuf", [128, 12], U),
     "aq": ("sbuf", [128, AQ], F), "nL": ("sbuf", [128, 24], F), "ntu": ("sbuf", [128, 24], U),
     "g1": ("sbuf", [128, C], F), "g2": ("sbuf", [128, C], F), "sgn": ("sbuf", [128, C], B),
     "hit": ("sbuf", [128, C], F), "q16": ("sbuf", [128, 4], F), "junk": ("sbuf", [128, C], F),
     "a2": ("sbuf", [128, AQ], F), "neg": ("sbuf", [128, AQ], B), "ix": ("sbuf", [128, S * AQ], U),
     "pI": ("sbuf", [128, 1], I), "pb": ("sbuf", [128, 8], I), "pf": ("sbuf", [128, 8], F), "pg": ("sbuf", [128, 8], F),
     "iX": ("sbuf", [128, 144], F), "iP": ("sbuf", [128, C], F), "lh": ("sbuf", [128, 4], U),
-    "ky": ("sbuf", [128, 12], F), "cu": ("sbuf", [128, 8], F), "k16": ("sbuf", [128, TP], F),
-    "col": ("sbuf", [128, C], F), "cK": ("sbuf", [128, 3 * C], F),
+    "ky": ("sbuf", [128, 16], F), "cu": ("sbuf", [128, 12], F), "k16": ("sbuf", [128, TP], F),
+    "col": ("sbuf", [128, C], F), "cK": ("sbuf", [128, 4 * C], F),
     "rot": ("sbuf", [128, 256], F), "nid": ("sbuf", [128, 256], F),
-    "i1k": ("sbuf", [128, 128], B), "i2k": ("sbuf", [128, 128], B), "vot": ("sbuf", [128, 144], B),
+    "i1k": ("sbuf", [128, 256], B), "i2k": ("sbuf", [128, 128], B), "vot": ("sbuf", [128, 144], B),
     "send": ("sbuf", [128, S * C], F), "land": ("sbuf", [128, S * C], F),
     "ps": ("psum", [128, 8 * BANK], F),
 }
@@ -59,7 +63,7 @@ PT, PE = 4 * BANK, 4 * BANK
 DQ, UU = 5 * BANK, 5 * BANK + C
 PR, PO, PK = 6 * BANK, 6 * BANK + C, 6 * BANK + 4 * C
 PD = 7 * BANK
-KP, KS, KW = 0, C, 2 * C
+KP, KS, KL, KW = 0, C, 2 * C, 3 * C
 
 
 def routes(T, topo):
@@ -260,10 +264,14 @@ def rank_program(g, core, T, topo):
         add(q, lambda e: e.dma_start(dst, ap(a)).then_inc(T.sem[sem], 16), regs(a), [], (sem, total))
 
     def at(buf, lo, n):
-        return (buf, lo, lo + n)
+        buf, o = WITHIN.get(buf, (buf, 0))
+        return (buf, o + lo, o + lo + n)
 
     def ps(lo, n):
         return ("ps", lo, lo + n)
+
+    def slot(k):
+        return ("p", HP + k, HP + NP, SL)
 
     def tap(buf, k):
         return at(buf, k * C, C)
@@ -286,44 +294,50 @@ def rank_program(g, core, T, topo):
     helped = range(4, 4 + OFF)
     iota(at("pI", 0, 1), [[0, 1]], 0, 1, True)
     iota(at("iX", 0, 144), [[1, 144]], 0)
-    iota(at("iP", 0, C), [[1, 16], [16 * SL, 4]], 0)
-    iota(at("cK", KS, C), [[-W, 16], [0, 4]], 15 * W + FAR - 1 + FAR // 2)
-    fill(("p", TP + 1, NP, SL), 0.0)
+    iota(at("iP", 0, C), [[1, 16], [-HP, 2], [16 * SL, 2]], HP)
+    iota(at("cK", KS, C), [[-W, 16], [HP, 2], [0, 2]], 15 * W + FAR - 1 - HP // 2)
+    iota(at("cK", KL, C), [[-W, 16], [0, 4]], 15 * W + FAR - 1 + FAR // 2)
+    fill(slot(TP + 1), 0.0)
     fill(at("mkey", 0, 48), 1.0)
     P = at("pI", 0, 1)
     ts(at("pb", 0, 1), P, 15, A.bitwise_and)
     ts(at("pb", 1, 1), P, 3, A.bitwise_and)
     ts(at("pb", 2, 1), P, 112, A.bitwise_and)
     ts(at("pb", 3, 1), P, 127, A.bitwise_and)
-    fill(("p", TP + 2, NP, SL), HUGE)
-    fill(("p", TP + 3, NP, SL), -HUGE)
+    fill(slot(TP + 2), HUGE)
+    fill(slot(TP + 3), -HUGE)
     cp(at("pf", 0, 4), at("pb", 0, 4))
     fill(("mkey", 0, 48, TP), 0.0)
-    fill(at("quart", 0, C), 0.25)
+    fill(at("new", 0, C), 0.25)
     ROW, LOW, GRP, PAR = [at("pf", k, 1) for k in range(4)]
     ts(at("rot", 0, 128), at("iX", 0, 128), PAR, A.is_equal)
     ts(at("i2k", 0, 128), at("iX", 0, 128), PAR, A.is_equal, -2048.0, A.mult)
     ts(at("pg", 0, 1), ROW, -float(SL), A.mult, FAR - 1.0, A.add)
     ts(at("pg", 1, 1), GRP, 15.0, A.add)
-    ts(at("k16", 0, TP), at("iX", 0, TP), -float(TP), A.add)
+    ts(at("k16", 0, TP), at("iX", 0, TP), -1.0, A.mult)
     ts(at("col", 0, C), at("iX", 0, C), 16.0, A.mult, ROW, A.add)
     ts(at("cK", KP, C), at("iP", 0, C), -1.0, A.mult, at("pg", 0, 1), A.add)
     ts(at("cK", KW, C), at("col", 0, C), -1.0, A.mult, FAR - 1.0, A.add)
     ts(at("lh", 0, 4), at("iX", 0, 4), 0.0, A.mult, LOW, A.add)
-    ts(at("cu", 0, 4), at("col", 0, 4), float(SL), A.mult, float(TP), A.add)
-    ts(at("cu", 4, 4), at("col", 0, 4), float(NW), A.add)
+    for h in range(2):
+        ts(at("cu", 2 * h, 2), at("col", 2 * h, 2), float(SL), A.mult, float(HP - h * NP), A.add)
+        ts(at("cu", 4 + 2 * h, 2), at("col", 2 * h, 2), float(h * (NW + C)), A.add)
     fill(at("Z", 4, 4), 0)
-    ts(at("i1k", 0, 128), at("iX", 0, 128), PAR, A.is_equal, FAR / 2.0, A.mult)
+    ts(at("i1k", 0, 128), at("iX", 0, 128), PAR, A.is_equal, HP / 2.0, A.mult)
+    ts(at("i1k", 128, 128), at("iX", 0, 128), PAR, A.is_equal, FAR / 2.0, A.mult)
     ts(at("vot", 0, 144), at("iX", 0, 144), at("pg", 1, 1), A.is_equal, 65536.0, A.mult)
     for o in (0, 128):
         ts(at("nid", o, 128), at("iX", 0, 128), PAR, A.is_equal, -1.0, A.mult)
     if OFF:
-        ts(at("cK", KS + 16, 4 * OFF), at("cK", KS + 16, 4 * OFF), 16 * 65536.0, A.add)
+        for key in (KP, KW):
+            ts(at("cK", key + 16, 4 * OFF), at("cK", key + 16, 4 * OFF), 16 * 65536.0, A.add)
 
-    def offsets(s, part, n=AQ):
+    def offsets(s, part, n=AQ, between=None):
         if part == 0:
             for c in range(4):
                 act(("a2", c, n, 4), ("aq", c, n, 4), AF.Identity, bias=at("nL", s * 4 + c, 1), scale=-1.0)
+            if between:
+                between()
             act(at("neg", 0, n), at("a2", 0, n), AF.Sign, bias=-2047.5)
         elif part == 1:
             mm(ps(PO, n), at("rot", 0, 128), at("a2", 0, n), True, False)
@@ -340,7 +354,9 @@ def rank_program(g, core, T, topo):
         elif part == 2:
             act(at("g2", 0, C), at("g1", 0, C), AF.Abs, bias=-2048.0)
         else:
-            act(at("sgn", 0, C), at("g2", 0, C), AF.Sign, bias=1023.5, scale=-1.0)
+            for c in range(4):
+                way = -1.0 if c < 2 and s < S - 1 else 1.0
+                act(("sgn", c, C, 4), ("g2", c, C, 4), AF.Sign, bias=1023.5 * way, scale=-way)
 
     def tails(s, part):
         o = C + (s % Q) * 4
@@ -355,24 +371,14 @@ def rank_program(g, core, T, topo):
             act(quarter("w", q), ps(PW[q], QW), AF.Copy)
 
     def desired(s):
-        act(("p", TP, NP, SL), at("d0b", s * C, C), AF.Copy, scale=-1.0)
+        act(slot(TP), at("d0b", s * C, C), AF.Copy, scale=-1.0)
 
     def early(s):
         if s < S - 1:
-            offsets(s + 1, 0)
+            offsets(s + 1, 0, AQ, lambda: gaps(s, 0))
             offsets(s + 1, 1)
-
-    def small(s):
-        if s:
+        else:
             gaps(s, 0)
-            tails(s - 1, 0)
-        gaps(s, 1)
-        if s < S - 1:
-            desired(s + 1)
-        gaps(s, 2)
-        if s:
-            tails(s - 1, 1)
-        gaps(s, 3)
 
     def window(s, k0, k1):
         return ("R" if s else "r0b", 0, W, ("ix", s * AQ + 4 * k0, s * AQ + 4 * k1))
@@ -383,19 +389,19 @@ def rank_program(g, core, T, topo):
         for i in range(n):
             if between and i == SG:
                 between()
-            act(("x", cuts[i] * C, cuts[i + 1] * C), window(s, cuts[i], cuts[i + 1]), AF.Copy)
+            act(at("x", cuts[i] * C, (cuts[i + 1] - cuts[i]) * C), window(s, cuts[i], cuts[i + 1]), AF.Copy)
             if s and i == n - 1:
                 o = s * AQ + C + ((s - 1) % Q) * 4
                 act(at("xq", 0, C), ("R", 0, W, at("ix", o, 4)), AF.Copy)
 
     def own(s, vg):
         if vg:
-            cp(("x", 0, vg * C), window(s, 0, vg))
+            cp(at("x", 0, vg * C), window(s, 0, vg))
 
     def prod(k0, k1, vg=VS):
         first = vg + (TP - vg) // (4 if vg < 4 else 3)
         for k in (list(range(vg, first)) + list(range(vg)) + list(range(first, TP)))[k0:k1]:
-            tt(("p", k, NP, SL), ps(PW[k // 4] + (k % 4) * C, C), tap("x", k), A.mult)
+            tt(slot(k), ps(PW[k // 4] + (k % 4) * C, C), tap("x", k), A.mult)
 
     mine = [j for j in jobs if j[0] == core]
     taken, masks = [], {}
@@ -420,32 +426,34 @@ def rank_program(g, core, T, topo):
         cp(("R", 0, W, at("ntu", s * 4, 4)), at("land", s * C, C))
         gather(s + 1, vg, between)
 
-    IP, IW = at("idx", 0, 4), at("idx", 4, 4)
+    IP, IW, IWX = at("idx", 0, 4), at("idx", 4, 4), at("idx", 4, 8)
 
     def fix_p():
-        ts(("p", 0, FAR + NP, IP), at("xq", 0, C), 0.25, A.mult, 0.0, A.add)
+        for h in range(2):
+            ts(("p", h * NP, (h + 1) * NP, at("idx", 2 * h, 2)), at("xq", 32 * h, 32), 0.25, A.mult, 0.0, A.add)
 
-    def fix_w():
-        cp(("w", 0, FAR + NW, IW), at("quart", 0, C))
+    def fix_w(lo, n):
+        cp(("wb", lo, lo + n, IW), at("new", 0, C))
 
     def fix_x():
-        cp(("x", 0, FAR + NW, IW), at("xq", 0, C))
+        cp(("xb", 0, WX, IW), at("xq", 0, C))
 
     def delays(part):
         if part == 0:
-            act(at("ky", 4, 4), at("ky", 0, 4), AF.Relu)
+            act(at("ky", 4, 2), at("ky", 0, 2), AF.Relu, bias=1.0)
+            act(at("ky", 6, 2), at("ky", 2, 2), AF.Relu, bias=float(TP), scale=-1.0)
             for c in range(4):
                 act(("junk", c, C, 4), at("k16", 0, TP), AF.Abs, bias=at("ky", c, 1))
             for c in range(4):
-                act(at("ky", 8 + c, 1), at("ky", 4 + c, 1), AF.Identity, bias=at("cu", 4 + c, 1), scale=-float(C))
+                act(at("ky", 8 + c, 1), at("ky", 4 + c, 1), AF.Identity, bias=at("cu", 4 + c, 1), scale=float(C if c < 2 else -C))
             act(at("hit", 0, C), at("junk", 0, C), AF.Relu, bias=1.0, scale=-1.0)
         elif part == 1:
             tt(ps(UU, C), ps(DQ, C), at("hit", 0, C), A.mult)
         else:
             tt(at("aq", 0, C), ps(UU, C), at("aq", 0, C), A.add)
 
-    def votes(key, buf, r, stop):
-        for j in range(r, 16, 2):
+    def votes(key, buf, r, m, stop):
+        for j in range(r, 16, m):
             mm(ps(PK + key, C), at("vot", 15 - j, 128), (buf, j, NW, 16), False, stop and j == 15)
 
     def convert(lo, hi):
@@ -455,10 +463,8 @@ def rank_program(g, core, T, topo):
     cp(at("aq", 0, C), at("dli", 0, C))
     offsets(0, 0, C)
     offsets(0, 1, C)
-    cp(at("ntu", 0, 24), at("nti", 0, 24))
-    cp(at("w", 0, NW), at("w0b", 0, NW))
     for q in range(4):
-        act(ps(PW[q], QW), quarter("w0b", q), AF.Copy)
+        cp(ps(PW[q], QW), quarter("w0b", q))
     offsets(0, 2, C)
     cp(("R", 0, RCUT // 2), ("r0b", 0, RCUT // 2))
     convert(RCUT // 2, RCUT)
@@ -467,14 +473,16 @@ def rank_program(g, core, T, topo):
     desired(0)
     prod(0, TP, VG)
     cp(at("aq", C, 12), at("qui", 0, 12))
-    offsets(1, 0)
-    gaps(0, 0)
+    offsets(1, 0, AQ, lambda: gaps(0, 0))
+    convert(RCUT, RMID)
     for s in range(S):
         last = s == S - 1
         late = s < LATE
         DF = ("Y", TP // 2, NP // 2, SL // 2)
         turn = at("nid", 128 - 16 * (1 + s), 128)
-        scan(at("Y", 0, NP // 2), ("p", 0, NP, 2), ("p", 1, NP, 2), A.add, A.add)
+        for h in range(2):
+            lo = (h + 1) * HP
+            scan(at("Y", h * HP // 2, HP // 2), ("p", lo, lo + HP, 2), ("p", lo + 1, lo + HP, 2), A.add, A.add)
         mm(ps(PR, C), turn, DF, True, True)
 
         def leave():
@@ -485,17 +493,13 @@ def rank_program(g, core, T, topo):
         if s:
             cp(IW, at("ky", 8, 4))
             delays(1)
+        else:
+            cp(at("ntu", 0, 24), at("nti", 0, 24))
         ts(ps(PE, C), DF, -2.0, A.max, 2.0, A.min)
         if s:
             fix_x()
-            if XFIRST:
-                delays(2)
-                leave()
-                early(s)
-                fix_w()
-            else:
-                fix_w()
-                leave()
+            fix_w(0, WX)
+            leave()
         for q in range(4):
             for k in range(4 * q, 4 * q + 4):
                 tt(tap("t", k), ps(PE, C), tap("x", k), A.mult)
@@ -504,22 +508,32 @@ def rank_program(g, core, T, topo):
                 leave()
                 offsets(1, 1)
         for q in range(4):
-            tt(ps(PW[q], QW), ps(PW[q], QW), quarter("w", q), A.add)
+            tt(ps(PW[q], QW), ps(PW[q], QW), quarter("w" if s else "w0b", q), A.add)
             act(at("ms", (q // 2) * QW, QW) if q % 2 else ps(PM[q], QW), ps(PW[q], QW), AF.Abs)
-        if s and not XFIRST:
+        if s:
             delays(2)
 
         if OFF:
             mm(ps(PD, OFF * C), at("rot", 0, 128), at("ms", 0, OFF * C), True, False)
-        both = ((0, A.min), (1, A.max))
+        both = ((1, A.max), (0, A.min))
         spec = not last and not late
         for (h, op) in both:
             tt(ps(PT + h * QW, QW), ps(PM[0], QW), at("ms", 0, QW), op)
-        if s and not XFIRST:
+        if s:
             early(s)
         for q in (1, 3):
             act(ps(PM[q], QW), ps(PW[q], QW), AF.Abs)
-        small(s)
+        gaps(s, 1)
+        if not last:
+            desired(s + 1)
+        if s:
+            tails(s - 1, 0)
+        gaps(s, 2)
+        if s:
+            tails(s - 1, 1)
+        gaps(s, 3)
+        if s == 0:
+            convert(RMID, W)
         kw, ks = (C, 0) if last else (0, C)
         for (h, op) in both:
             tt(at("l1", h * QW, QW), ps(PM[2], QW), at("ms", QW, QW), op)
@@ -531,35 +545,31 @@ def rank_program(g, core, T, topo):
             for half in range(2):
                 o = PT + h * QW + half * C
                 tt(at("l3", h * C, C) if half else ps(o, C), ps(o, C), at("l2", h * 2 * C + half * C, C), op)
-            if h == 0 and not last and XFIRST:
-                offsets(s + 1, 2)
-        mm(ps(PK, 2 * C), at("rot", 0, 128), at("cK", kw, 2 * C), True, False)
-        for (h, op) in both:
-            for half in range(2):
-                o = PT + h * QW
-                tt(at("l4", (2 * h + half) * C, C), ps(o, C), at("l3", h * C, C), op)
-            if h == 0 and not last and not XFIRST:
-                offsets(s + 1, 2)
+        mm(ps(PK, 2 * C), at("rot", 0, 128), at("cK", 2 * kw, 2 * C), True, False)
+        for o in (4 * C, 5 * C):
+            tt(at("l4", o, C), ps(PT + QW, C), at("l3", C, C), A.max)
+        if not last:
+            offsets(s + 1, 2)
+        tt(at("l4", 0, C), ps(PT, C), at("l3", 0, C), A.min)
+        for o in (C, 2 * C, 3 * C):
+            act(at("l4", o, C), at("l4", 0, C), AF.Copy)
         for k in range(OFF):
-            mm(ps(PD + k * C, C), at("nid", 0, 128), at("l4", 2 * C, C), False, k == OFF - 1)
-        mm(ps(PK + ks, C), at("i1k", 0, 128), at("sgn", 0, C), False, False)
-
-        def signs():
-            if OFF:
-                act(at("kmax", QW, OFF * C), ps(PD, OFF * C), AF.Sign)
-        if not (spec and SG):
-            signs()
-        if s == 0:
-            convert(RCUT, W)
-        todo = [(r, h, k) for h in range(2) for r in range(2) for k in range(0, TP, 2) if h == 0 or k not in helped]
-        for n, (r, h, k) in enumerate(todo):
-            if n == len(todo) - RPOS and spec:
-                take_in(s, VS, signs if SG else None)
+            mm(ps(PD + k * C, C), at("nid", 0, 128), at("l4", 0, C), False, k == OFF - 1)
+        if OFF:
+            act(at("kmin", QW, OFF * C), ps(PD, OFF * C), AF.Sign, scale=-1.0)
+        todo = [(1, 2, r, k) for r in range(2) for k in range(0, TP, 2)]
+        todo += [(0, 2, r, 6) for r in range(2) if OFF == 2]
+        todo += [(0, 4, r, k) for r in range(4) for k in range(0, TP, 4) if k not in helped]
+        for n, (h, m, r, k) in enumerate(todo):
+            if n == len(todo) - (RPOS if s else RP0) and spec:
+                take_in(s, VS)
             o = PM[k // 4] + (k % 4) * C
-            tt(("kmax" if h else "kmin", k * C + r, (k + 2) * C, 2), ("ps", o + r, o + 2 * C, 2),
-               ("l4", 2 * h * C + r, 2 * (h + 1) * C, 2), A.is_equal)
-            if n + 1 == len(todo) or todo[n + 1][0] != r:
-                votes(ks if h else kw, "kmax" if h else "kmin", r, n + 1 == len(todo))
+            tt(("kmax" if h else "kmin", k * C + r, (k + m) * C, m), ("ps", o + r, o + m * C, m),
+               ("l4", 4 * h * C + r, (4 * h + m) * C, m), A.is_equal)
+            if k + m == TP:
+                votes(ks if h else kw, "kmax" if h else "kmin", r, m, n + 1 == len(todo))
+                if (h, r) == (1, 1):
+                    mm(ps(PK + ks, C), at("i1k", 128 * last, 128), at("sgn", 0, C), False, False)
         if last:
             keep(range(4))
             store("Y", T.yr[:], at("land", s * C, C), "st_a", 48)
@@ -582,27 +592,18 @@ def rank_program(g, core, T, topo):
             cp(IW, at("Z", 0, 4))
             tails(s, 0)
             tt(at("hit", 0, C), ("Z", 0, 8, at("lh", 0, 4)), at("col", 0, C), A.is_equal)
-            fix_w()
+            fix_w(C, FAR + NW)
             store("Y", T.yw[:], at("w", 0, NW), "st_a", 48)
             delays(1)
             delays(2)
         else:
             cp(IP, at("Z", 0, 4))
-            if late:
-                take_in(s, VG)
-                tt(at("ky", 0, 4), at("cu", 0, 4), at("Z", 0, 4), A.subtract)
-                own(s + 1, VG)
-                prod(0, TP, VG)
-                delays(0)
-                keep(range(4))
-                fix_p()
-            else:
-                prod(P3, TP)
-                tt(at("ky", 0, 4), at("cu", 0, 4), at("Z", 0, 4), A.subtract)
-                keep(range(1))
-                delays(0)
-                fix_p()
-                keep(range(1, 4))
+            prod(P3, TP)
+            tt(at("ky", 0, 4), at("Z", 0, 4), at("cu", 0, 4), A.subtract)
+            keep(range(2))
+            delays(0)
+            fix_p()
+            keep(range(2, 4))
     tails(S - 1, 1)
     store("Y", T.yd[:], at("aq", 0, C), "st_a", 48)
     store("S", T.yq[:], at("aq", C, 12), "st_b", 16)

@@ -6,64 +6,69 @@ NW = TP * C
 QW = NW // 4
 SL = TP + 4
 HUGE = 2.0 ** 60
+ROUND = 1.5 * 2.0 ** 39
 NP = SL * C
-FAR = 2048
 HP = NP // 2
-WX = NW + 2 * C
-WITHIN = {"w": ("wb", C), "x": ("xb", C), "xq": ("new", C)}
+FAR = 2048
+WX = 2 * FAR + NW
+WITHIN = {"xq": ("new", C), "w": ("wb", FAR), "x": ("xb", FAR)}
 AQ = C + 4 * Q
 BANK = 512
-ENG = 8
 RCUT = 2560
-OFF = 2
-RPOS = 14
-PA = 7
-LATE = 0
-VG = 6
-VS = 2
-WIDE = 1
-CUT = 0
-RMID = 3328
-RP0 = 10
-LOOSE = 0
-SG = 0
-P1, P2, P3 = 10, 13, 16
-XFIRST = 0
-SPLIT = 0
+VR = 2304
+GAPS = {"pre": 256, "fp0": 128}
+RS = (0, 3700)
+FILL = {"fw": 2, "l0": 3, "m0a": 9}
+ST = (11, 3, 2, 3, 4)
+WL = 1
+HELP = ((), (4, 5))
+RP0 = 8
+VG, VS0, VS = 5, 2, 0
+TQ = 0
+DS = 1
+HALVES = 1
+MN = 2
+CLASSES = ["m0", "m1", "M0", "M1", "M2", "M3"]
+SUMS = "fp0 fp1 fx s0 uu s1 ki ad fw cl l0 :a"
+UPDATE = "t0 t1 lv t2 t3 a0 a1 a2 a3 px"
+TREES = "m0a M0a m0b M0b :3 :g1 :K01 :g2 :A0 :A1 :R m1a m1b M1a M1b :d m2a m2b M2a M2b :sg m3a m3b M3a M3b kr m4 :t0 M4 :t :X of"
+COMPARE = "c10 ti ga c99"
+KEYS = "ow kw p5 H p3 ks L p4 Hs p4 IP :K23"
+LAST = "c99 :K23 kw H ks L Hs IP"
 
 F, B, I, U = "float32", "bfloat16", "int32", "uint16"
 SCRATCH = {
     "r0b": ("sbuf", [128, W], B), "R": ("sbuf", [128, W], F),
     "w0b": ("sbuf", [128, NW], B), "d0b": ("sbuf", [128, S * C], B),
-    "dli": ("sbuf", [128, C], I), "qui": ("sbuf", [128, 12], I), "nti": ("sbuf", [128, 24], I),
-    "wb": ("sbuf", [128, C + FAR + NW], F), "xb": ("sbuf", [128, WX], F), "p": ("sbuf", [128, 2 * NP], F), "new": ("sbuf", [128, 2 * C], F),
-    "Y": ("sbuf", [128, NP], F), "t": ("sbuf", [128, NW], F), "ms": ("sbuf", [128, 2 * QW], F),
-    "l1": ("sbuf", [128, 2 * QW], F), "l2": ("sbuf", [128, QW], F), "l3": ("sbuf", [128, 2 * C], F), "l4": ("sbuf", [128, 6 * C], F),
-    "kmin": ("sbuf", [128, NW], B), "kmax": ("sbuf", [128, NW], B),
-    "mkey": ("sbuf", [128, 48], B),
-    "M": ("sbuf", [128, 3 * C], F), "D": ("sbuf", [128, 8], I), "Z": ("sbuf", [128, 8], I), "idx": ("sbuf", [128, 12], U),
-    "aq": ("sbuf", [128, AQ], F), "nL": ("sbuf", [128, 24], F), "ntu": ("sbuf", [128, 24], U),
+    "dli": ("sbuf", [128, C], I), "qui": ("sbuf", [128, 12], I), "nti": ("sbuf", [128, 24], I), "i0": ("sbuf", [128, 2 * C], I),
+    "wb": ("sbuf", [128, WX], F), "xb": ("sbuf", [128, WX], F), "p": ("sbuf", [128, 2 * (FAR + HP)], F), "new": ("sbuf", [128, 2 * C], F),
+    "Y": ("sbuf", [128, NP // 2], F), "t": ("sbuf", [128, NW], F), "ms": ("sbuf", [128, QW], F),
+    "l1": ("sbuf", [128, 2 * QW], F), "l2": ("sbuf", [128, QW], F), "l3": ("sbuf", [128, 2 * C], F), "l4": ("sbuf", [128, 8 * C], F),
+    "kmin": ("sbuf", [128, NW], B), "kmax": ("sbuf", [128, NW], B), "mkey": ("sbuf", [128, 2 * TP], B),
+    "Mw": ("sbuf", [128, 4 * C], F), "Ms": ("sbuf", [128, 2 * C], F), "L": ("sbuf", [128, 16], F), "cL": ("sbuf", [128, 40], F),
+    "Mb": ("sbuf", [128, 6 * C], F), "Lb": ("sbuf", [128, 24], F), "uu": ("sbuf", [128, C], F),
+    "idx": ("sbuf", [128, 8], U), "z": ("sbuf", [128, C], F), "z1": ("sbuf", [128, C], F), "ky": ("sbuf", [128, 4], F),
+    "aq": ("sbuf", [128, AQ], F), "nL": ("sbuf", [128, 28], F), "ntu": ("sbuf", [128, 24], U),
     "g1": ("sbuf", [128, C], F), "g2": ("sbuf", [128, C], F), "sgn": ("sbuf", [128, C], B),
     "hit": ("sbuf", [128, C], F), "q16": ("sbuf", [128, 4], F), "junk": ("sbuf", [128, C], F),
     "a2": ("sbuf", [128, AQ], F), "neg": ("sbuf", [128, AQ], B), "ix": ("sbuf", [128, S * AQ], U),
-    "pI": ("sbuf", [128, 1], I), "pb": ("sbuf", [128, 8], I), "pf": ("sbuf", [128, 8], F), "pg": ("sbuf", [128, 8], F),
-    "iX": ("sbuf", [128, 144], F), "iP": ("sbuf", [128, C], F), "lh": ("sbuf", [128, 4], U),
-    "ky": ("sbuf", [128, 16], F), "cu": ("sbuf", [128, 12], F), "k16": ("sbuf", [128, TP], F),
-    "col": ("sbuf", [128, C], F), "cK": ("sbuf", [128, 4 * C], F),
-    "rot": ("sbuf", [128, 256], F), "nid": ("sbuf", [128, 256], F),
-    "i1k": ("sbuf", [128, 256], B), "i2k": ("sbuf", [128, 128], B), "vot": ("sbuf", [128, 144], B),
+    "pI": ("sbuf", [128, 1], I), "pb": ("sbuf", [128, 4], I), "pf": ("sbuf", [128, 4], F), "pg": ("sbuf", [128, 4], F),
+    "iX": ("sbuf", [128, 144], F), "iP": ("sbuf", [128, C + 4], F), "col": ("sbuf", [128, 4], F), "cK": ("sbuf", [128, 2 * C], F), "cB": ("sbuf", [128, 2 * C], F),
+    "rot": ("sbuf", [128, 128], F), "nid": ("sbuf", [128, 256], F), "i64": ("sbuf", [128, 128], F),
+    "i1k": ("sbuf", [128, 128], B), "idb": ("sbuf", [128, 128], B), "i2k": ("sbuf", [128, 128], B), "vot": ("sbuf", [128, 144], B),
     "send": ("sbuf", [128, S * C], F), "land": ("sbuf", [128, S * C], F),
     "ps": ("psum", [128, 8 * BANK], F),
 }
 SEMAPHORES = (["eV", "eS", "eT", "eG", "ld_s", "ld_w", "ld_d", "ld_q", "ld_r0", "ld_r1", "sent", "st_a", "st_b"]
               + ["arr%d" % s for s in range(S)])
-PW = [q * BANK for q in range(4)]
-PM = [q * BANK + QW for q in range(4)]
-PT, PE = 4 * BANK, 4 * BANK
-DQ, UU = 5 * BANK, 5 * BANK + C
-PR, PO, PK = 6 * BANK, 6 * BANK + C, 6 * BANK + 4 * C
-PD = 7 * BANK
-KP, KS, KL, KW = 0, C, 2 * C, 3 * C
+PW = [q * BANK + (1 - q % 2) * QW for q in range(4)]
+PM = [4 * BANK, 5 * BANK, 6 * BANK, 3 * BANK + QW]
+PD = [0, 2 * BANK]
+PKW = BANK + QW
+DQ, UU = 2 * C, 3 * C
+PE, PO, PT = 4 * BANK + QW, 5 * BANK + QW, 6 * BANK + QW
+PR, PKS = 7 * BANK, 7 * BANK + QW
+PR0 = 6 * BANK + QW
 
 
 def routes(T, topo):
@@ -83,24 +88,14 @@ def routes(T, topo):
     return out
 
 
-def pick(topo, src, dst, taken):
-    eng = [e for e in topo.engines(src, dst) if e not in taken][:ENG]
-    taken.extend(eng)
-    m = 0
-    for e in eng:
-        m |= 1 << e
-    return m
-
-
 def helper_program(g, core, T, topo, job):
     src, dst, via, b = job
     rid, pid = topo.addr(dst, core)
-    m = pick(topo, core, dst, [])
     for s in range(S):
         piece = T.land[:, s * C + b * 32:s * C + b * 32 + 32]
-        g.wait_ge(T.sem["arr%d" % s], len(topo.engines(src, core)) if WIDE else ENG)
-        g.remote_dma(piece, piece, T.sem["arr%d" % s], T.sem.sent, pid, rid, m)
-    g.wait_ge(T.sem.sent, S * ENG)
+        g.wait_ge(T.sem["arr%d" % s], len(topo.engines(src, core)))
+        g.remote_dma(piece, piece, T.sem["arr%d" % s], T.sem.sent, pid, rid, topo.mask(core, dst))
+    g.wait_ge(T.sem.sent, S * len(topo.engines(core, dst)))
 
 
 def columns(a):
@@ -134,9 +129,7 @@ def emit(g, T, ops):
             for (o2, mode2, m2) in acc.get((buf, q) if banks else buf, []):
                 if not m & m2 or (mode2 == "r" and mode == "r"):
                     continue
-                if banks and q == "T" and m == m2 and op["more"]:
-                    continue
-                if LOOSE and mode == "w" and q in "VS" and o2["key"] == q:
+                if banks and q == "T" and op["more"]:
                     continue
                 deps.append(o2)
         op["waits"] = []
@@ -197,7 +190,7 @@ def rank_program(g, core, T, topo):
     ops = []
 
     def add(q, fn, r, w, tok=None, more=False):
-        ops.append({"q": q, "fn": fn, "r": r, "w": w, "tok": tok, "flag": False, "n": len(ops), "more": more})
+        ops.append({"q": q, "fn": fn, "r": r, "w": w, "tok": tok, "flag": False, "more": more})
 
     def ap(a):
         if len(a) == 3:
@@ -216,10 +209,6 @@ def rank_program(g, core, T, topo):
         return ap(a) if isinstance(a, tuple) else a
 
     def tt(out, a, b, op):
-        if CUT and len(out) == len(a) == len(b) == 3 and out[2] - out[1] > C:
-            for o in range(0, out[2] - out[1], C):
-                tt(at(out[0], out[1] + o, C), at(a[0], a[1] + o, C), at(b[0], b[1] + o, C), op)
-            return
         add("V", lambda e: e.tensor_tensor(ap(out), ap(a), ap(b), op), regs(a, b) + lists(out, a), regs(out))
 
     def ts(out, a, s1, op0, s2=None, op1=None):
@@ -264,6 +253,8 @@ def rank_program(g, core, T, topo):
         add(q, lambda e: e.dma_start(dst, ap(a)).then_inc(T.sem[sem], 16), regs(a), [], (sem, total))
 
     def at(buf, lo, n):
+        if buf == "cK" and "kb" in KEYS:
+            buf, lo = "cB", (lo + C) % (2 * C)
         buf, o = WITHIN.get(buf, (buf, 0))
         return (buf, o + lo, o + lo + n)
 
@@ -271,79 +262,83 @@ def rank_program(g, core, T, topo):
         return ("ps", lo, lo + n)
 
     def slot(k):
-        return ("p", HP + k, HP + NP, SL)
+        return ("p", FAR + k, FAR + NP, SL)
 
-    def tap(buf, k):
-        return at(buf, k * C, C)
+    def tap(buf, k, n=1):
+        return at(buf, k * C, n * C)
 
     def quarter(buf, q):
         return at(buf, q * QW, QW)
 
-    def size(k):
-        q, o = k // 4, (k % 4) * C
-        return at("ms", (q // 2) * QW + o, C) if q % 2 else ps(PM[q] + o, C)
-
     load("S", at("dli", 0, C), T.dl[:], "ld_s", 32)
-    load("S", at("nti", 0, 24), T.nt[:], "ld_s", 32)
-    load("Y", at("w0b", 0, NW), T.w0[:], "ld_w")
+    load("Y", at("nti", 0, 24), T.nt[:], "ld_s", 32)
+    if WL == 0:
+        load("Y", at("w0b", 0, NW), T.w0[:], "ld_w")
     load("Y", ("r0b", 0, RCUT), T.r0[:, 0:RCUT], "ld_r0")
     load("Y", ("r0b", RCUT, W), T.r0[:, RCUT:W], "ld_r1")
+    if WL:
+        load("Y", at("w0b", 0, NW), T.w0[:], "ld_w")
     load("Y", at("d0b", 0, S * C), T.d0[:], "ld_d")
     load("Y", at("qui", 0, 12), T.qu[:], "ld_q")
 
-    helped = range(4, 4 + OFF)
     iota(at("pI", 0, 1), [[0, 1]], 0, 1, True)
     iota(at("iX", 0, 144), [[1, 144]], 0)
-    iota(at("iP", 0, C), [[1, 16], [-HP, 2], [16 * SL, 2]], HP)
-    iota(at("cK", KS, C), [[-W, 16], [HP, 2], [0, 2]], 15 * W + FAR - 1 - HP // 2)
-    iota(at("cK", KL, C), [[-W, 16], [0, 4]], 15 * W + FAR - 1 + FAR // 2)
-    fill(slot(TP + 1), 0.0)
-    fill(at("mkey", 0, 48), 1.0)
+    iota(at("iP", 0, C), [[1, 16], [0, 2], [16 * SL, 2]], FAR // 2)
+    iota(at("iP", C, 4), [[FAR + 32, 2], [16, 2]], FAR // 2)
+    iota(at("cK", C, C), [[-W, 16], [0, 4]], 15 * W)
+    mark = len(ops)
     P = at("pI", 0, 1)
-    ts(at("pb", 0, 1), P, 15, A.bitwise_and)
-    ts(at("pb", 1, 1), P, 3, A.bitwise_and)
-    ts(at("pb", 2, 1), P, 112, A.bitwise_and)
-    ts(at("pb", 3, 1), P, 127, A.bitwise_and)
+    ROW, GRP, PAR = [at("pf", k, 1) for k in range(3)]
+    BOTH = "kb" in KEYS
+    KW = PKS + C if BOTH else PKW
+    fill(slot(TP + 1), 0.0)
     fill(slot(TP + 2), HUGE)
     fill(slot(TP + 3), -HUGE)
-    cp(at("pf", 0, 4), at("pb", 0, 4))
-    fill(("mkey", 0, 48, TP), 0.0)
+    fill(at("mkey", 0, TP), 1.0)
+    for i, m in enumerate((15, 112, 127)):
+        ts(at("pb", i, 1), P, m, A.bitwise_and)
+    for i, v in enumerate((0.0, -1.0, float(C), 1.0 / C)):
+        fill(("cL", i, 16, 4), v)
+    cp(at("pf", 0, 3), at("pb", 0, 3))
+    fill(at("mkey", 0, 1), 0.0)
     fill(at("new", 0, C), 0.25)
-    ROW, LOW, GRP, PAR = [at("pf", k, 1) for k in range(4)]
-    ts(at("rot", 0, 128), at("iX", 0, 128), PAR, A.is_equal)
-    ts(at("i2k", 0, 128), at("iX", 0, 128), PAR, A.is_equal, -2048.0, A.mult)
-    ts(at("pg", 0, 1), ROW, -float(SL), A.mult, FAR - 1.0, A.add)
+    ts(at("pg", 0, 1), ROW, -float(SL), A.mult)
     ts(at("pg", 1, 1), GRP, 15.0, A.add)
-    ts(at("k16", 0, TP), at("iX", 0, TP), -1.0, A.mult)
-    ts(at("col", 0, C), at("iX", 0, C), 16.0, A.mult, ROW, A.add)
-    ts(at("cK", KP, C), at("iP", 0, C), -1.0, A.mult, at("pg", 0, 1), A.add)
-    ts(at("cK", KW, C), at("col", 0, C), -1.0, A.mult, FAR - 1.0, A.add)
-    ts(at("lh", 0, 4), at("iX", 0, 4), 0.0, A.mult, LOW, A.add)
-    for h in range(2):
-        ts(at("cu", 2 * h, 2), at("col", 2 * h, 2), float(SL), A.mult, float(HP - h * NP), A.add)
-        ts(at("cu", 4 + 2 * h, 2), at("col", 2 * h, 2), float(h * (NW + C)), A.add)
-    fill(at("Z", 4, 4), 0)
-    ts(at("i1k", 0, 128), at("iX", 0, 128), PAR, A.is_equal, HP / 2.0, A.mult)
-    ts(at("i1k", 128, 128), at("iX", 0, 128), PAR, A.is_equal, FAR / 2.0, A.mult)
-    ts(at("vot", 0, 144), at("iX", 0, 144), at("pg", 1, 1), A.is_equal, 65536.0, A.mult)
     for o in (0, 128):
         ts(at("nid", o, 128), at("iX", 0, 128), PAR, A.is_equal, -1.0, A.mult)
-    if OFF:
-        for key in (KP, KW):
-            ts(at("cK", key + 16, 4 * OFF), at("cK", key + 16, 4 * OFF), 16 * 65536.0, A.add)
+    ts(at("cK", 0, C), at("iP", 0, C), -1.0, A.mult, at("pg", 0, 1), A.add)
+    ts(at("rot", 0, 128), at("iX", 0, 128), PAR, A.is_equal)
+    ts(at("col", 0, 4), at("iP", C, 4), ROW, A.add)
+    ts(at("i2k", 0, 128), at("iX", 0, 128), PAR, A.is_equal, -2048.0, A.mult)
+    for h in range(2):
+        if HELP[h]:
+            ts(at("cK", h * C + 4 * HELP[h][0], 8), at("cK", h * C + 4 * HELP[h][0], 8), 16 * 65536.0, A.add)
+    ts(at("vot", 0, 144), at("iX", 0, 144), at("pg", 1, 1), A.is_equal, 65536.0, A.mult)
+    ts(at("i1k", 0, 128), at("iX", 0, 128), PAR, A.is_equal, FAR / 2.0, A.mult)
+    ts(("Mw", C - 1, 4 * C, C), at("col", 0, 4), -1.0 / C, A.mult)
+    for c in range(4):
+        ts(at("Mw", c * C + 3 * TP - 1, 1), at("cK", c, 1), float(C), A.mult, at("col", c, 1), A.add)
+    if TQ:
+        ts(at("i64", 0, 128), at("iX", 0, 128), PAR, A.is_equal, -0.015625, A.mult)
+    later = ops[mark:]
+    del ops[mark:]
+    ONE = at("rot", 0, 128)
 
-    def offsets(s, part, n=AQ, between=None):
+    def statics(n):
+        ops.extend(later[:n])
+        del later[:n]
+
+    def offsets(s, part, between=None):
         if part == 0:
             for c in range(4):
-                act(("a2", c, n, 4), ("aq", c, n, 4), AF.Identity, bias=at("nL", s * 4 + c, 1), scale=-1.0)
-            if between:
-                between()
-            act(at("neg", 0, n), at("a2", 0, n), AF.Sign, bias=-2047.5)
+                act(("a2", c, AQ, 4), ("aq", c, AQ, 4), AF.Identity, bias=at("nL", s * 4 + c, 1), scale=-1.0)
+            between()
+            act(at("neg", 0, AQ), at("a2", 0, AQ), AF.Sign, bias=-2047.5)
         elif part == 1:
-            mm(ps(PO, n), at("rot", 0, 128), at("a2", 0, n), True, False)
-            mm(ps(PO, n), at("i2k", 0, 128), at("neg", 0, n), False, True)
+            mm(ps(PO, AQ), ONE, at("a2", 0, AQ), True, False)
+            mm(ps(PO, AQ), at("i2k", 0, 128), at("neg", 0, AQ), False, True)
         else:
-            cp(at("ix", s * AQ, n), ps(PO, n))
+            cp(at("ix", s * AQ, AQ), ps(PO, AQ))
 
     def gaps(s, part):
         if part == 0:
@@ -354,9 +349,7 @@ def rank_program(g, core, T, topo):
         elif part == 2:
             act(at("g2", 0, C), at("g1", 0, C), AF.Abs, bias=-2048.0)
         else:
-            for c in range(4):
-                way = -1.0 if c < 2 and s < S - 1 else 1.0
-                act(("sgn", c, C, 4), ("g2", c, C, 4), AF.Sign, bias=1023.5 * way, scale=-way)
+            act(at("sgn", 0, C), at("g2", 0, C), AF.Sign, bias=1023.5, scale=-1.0)
 
     def tails(s, part):
         o = C + (s % Q) * 4
@@ -366,247 +359,314 @@ def rank_program(g, core, T, topo):
         for c in range(4):
             act(("junk", c, C, 4), ("ps", UU + c, UU + C, 4), AF.Identity, bias=at("q16", c, 1), scale=-1.0, acc=at("aq", o + c, 1))
 
-    def keep(quarters):
-        for q in quarters:
-            act(quarter("w", q), ps(PW[q], QW), AF.Copy)
-
     def desired(s):
         act(slot(TP), at("d0b", s * C, C), AF.Copy, scale=-1.0)
 
-    def early(s):
-        if s < S - 1:
-            offsets(s + 1, 0, AQ, lambda: gaps(s, 0))
+    def convert(lo, hi):
+        if hi > lo:
+            act(("R", lo, hi), ("r0b", lo, hi), AF.Copy)
+
+    def size(q, half):
+        act(ps(PM[q] + half * 2 * C, 2 * C), ps(PW[q] + half * 2 * C, 2 * C), AF.Abs)
+
+    def scalar(s, name):
+        if name == "a" and 0 < s < S - 1:
+            offsets(s + 1, 0, lambda: gaps(s, 0))
             offsets(s + 1, 1)
-        else:
+        elif name == "a" and s:
             gaps(s, 0)
+        elif name in ("g1", "g2", "sg"):
+            gaps(s, ("g1", "g2", "sg").index(name) + 1)
+        elif name in ("S", "X") and HELP[name == "X"]:
+            h = int(name == "X")
+            act(tap("kmax" if h else "kmin", HELP[h][0], 2), ps(PD[h], 2 * C), AF.Sign, scale=1.0 if h else -1.0)
+        elif name == "R" and s == 0:
+            convert(RS[1], W)
+        elif name == "d" and s < S - 1:
+            desired(s + 1)
+        elif name == "t0" and s:
+            tails(s - 1, 0)
+        elif name == "t" and s:
+            tails(s - 1, 1)
+        elif name[0] == "K":
+            act(at("w", int(name[1]) * QW, len(name[1:]) * QW), ps(PW[int(name[1])], len(name[1:]) * QW), AF.Copy)
+        elif name == "3":
+            act(ps(PM[3], QW), ps(PW[3], QW), AF.Abs)
+        elif name[0] == "A" and (HELP[0] != HELP[1] or 2 + 2 * int(name[1]) not in HELP[0]):
+            size(int(name[1]), 1 - int(name[1]))
 
     def window(s, k0, k1):
         return ("R" if s else "r0b", 0, W, ("ix", s * AQ + 4 * k0, s * AQ + 4 * k1))
 
-    def gather(s, vg=0, between=None):
+    def gather(s, vg):
         n = 4 if vg < 4 else 3
         cuts = [vg + (TP - vg) * i // n for i in range(n + 1)]
         for i in range(n):
-            if between and i == SG:
-                between()
             act(at("x", cuts[i] * C, (cuts[i + 1] - cuts[i]) * C), window(s, cuts[i], cuts[i + 1]), AF.Copy)
-            if s and i == n - 1:
-                o = s * AQ + C + ((s - 1) % Q) * 4
-                act(at("xq", 0, C), ("R", 0, W, at("ix", o, 4)), AF.Copy)
+        if s:
+            o = s * AQ + C + ((s - 1) % Q) * 4
+            act(at("xq", 0, C), ("R", 0, W, at("ix", o, 4)), AF.Copy)
 
     def own(s, vg):
         if vg:
             cp(at("x", 0, vg * C), window(s, 0, vg))
 
-    def prod(k0, k1, vg=VS):
+    def prod(k0, k1, vg):
         first = vg + (TP - vg) // (4 if vg < 4 else 3)
         for k in (list(range(vg, first)) + list(range(vg)) + list(range(first, TP)))[k0:k1]:
             tt(slot(k), ps(PW[k // 4] + (k % 4) * C, C), tap("x", k), A.mult)
 
     mine = [j for j in jobs if j[0] == core]
-    taken, masks = [], {}
-    for j in sorted(mine, key=lambda j: j[2] is not None):
-        to = j[1] if j[2] is None else j[2]
-        masks[j[3]] = topo.mask(core, to) if WIDE else pick(topo, core, to, taken)
+    masks = [topo.mask(core, j[1] if j[2] is None else j[2]) for j in mine]
     order = [j[3] for j in sorted(mine, key=lambda j: j[2] is None)]
-    sent = S * sum(bin(m).count("1") for m in masks.values())
+    sent = S * sum(bin(m).count("1") for m in masks)
+    come = sum(len(topo.engines(j[0] if j[2] is None else j[2], core)) for j in jobs if j[1] == core)
 
-    def pass_on(s, blocks):
+    def pass_on(s, b):
         def fn(e):
-            trs = []
-            for (src, dst, via, b) in [mine[b] for b in blocks]:
-                rid, pid = topo.addr(dst if via is None else via, core)
-                lo = s * C + b * 32
-                trs.append(RemoteDMATransfer(dst_ids=[DstId(rid=rid, pnc=pid)], dma_engine_mask=masks[b],
-                                             remote_sem=T.sem["arr%d" % s], src=T.send[:, lo:lo + 32], dst=T.land[:, lo:lo + 32]))
-            return e.remote_dma_fused(trs, local_sem=T.sem.sent)
-        add("G", fn, [at("send", s * C + b * 32, 32) for b in blocks], [], ("sent", sent))
+            src, dst, via, _ = mine[b]
+            rid, pid = topo.addr(dst if via is None else via, core)
+            lo = s * C + b * 32
+            tr = RemoteDMATransfer(dst_ids=[DstId(rid=rid, pnc=pid)], dma_engine_mask=masks[b], remote_sem=T.sem["arr%d" % s],
+                                   src=T.send[:, lo:lo + 32], dst=T.land[:, lo:lo + 32])
+            return e.remote_dma_fused([tr], local_sem=T.sem.sent)
+        add("G", fn, [at("send", s * C + b * 32, 32)], [], ("sent", sent))
 
-    def take_in(s, vg=0, between=None):
-        cp(("R", 0, W, at("ntu", s * 4, 4)), at("land", s * C, C))
-        gather(s + 1, vg, between)
+    def leave(s, blocks):
+        lo, n = 32 * min(blocks), 32 * len(blocks)
+        ts(at("send", s * C + lo, n), ps(PR if order[1] in blocks else PR0, n), -2.0, A.max, 2.0, A.min)
+        for b in blocks:
+            pass_on(s, b)
+        if order[1] in blocks:
+            add(None, None, [], [at("land", s * C, C)], ("arr%d" % s, come))
 
-    IP, IW, IWX = at("idx", 0, 4), at("idx", 4, 4), at("idx", 4, 8)
+    def strong(c, lane):
+        return at("Ms", 2 * TP * c + TP * lane + TP - 1, 1)
 
-    def fix_p():
-        for h in range(2):
-            ts(("p", h * NP, (h + 1) * NP, at("idx", 2 * h, 2)), at("xq", 32 * h, 32), 0.25, A.mult, 0.0, A.add)
-
-    def fix_w(lo, n):
-        cp(("wb", lo, lo + n, IW), at("new", 0, C))
-
-    def fix_x():
-        cp(("xb", 0, WX, IW), at("xq", 0, C))
-
-    def delays(part):
-        if part == 0:
-            act(at("ky", 4, 2), at("ky", 0, 2), AF.Relu, bias=1.0)
-            act(at("ky", 6, 2), at("ky", 2, 2), AF.Relu, bias=float(TP), scale=-1.0)
-            for c in range(4):
-                act(("junk", c, C, 4), at("k16", 0, TP), AF.Abs, bias=at("ky", c, 1))
-            for c in range(4):
-                act(at("ky", 8 + c, 1), at("ky", 4 + c, 1), AF.Identity, bias=at("cu", 4 + c, 1), scale=float(C if c < 2 else -C))
-            act(at("hit", 0, C), at("junk", 0, C), AF.Relu, bias=1.0, scale=-1.0)
-        elif part == 1:
-            tt(ps(UU, C), ps(DQ, C), at("hit", 0, C), A.mult)
-        else:
-            tt(at("aq", 0, C), ps(UU, C), at("aq", 0, C), A.add)
-
-    def votes(key, buf, r, m, stop):
+    def votes(h, r, m):
         for j in range(r, 16, m):
-            mm(ps(PK + key, C), at("vot", 15 - j, 128), (buf, j, NW, 16), False, stop and j == 15)
+            mm(ps(PKS if h else KW, C), at("vot", 15 - j, 128), ("kmax" if h else "kmin", j, NW, 16), False, j == 15 and not (BOTH and todo))
 
-    def convert(lo, hi):
-        act(("R", lo, hi), ("r0b", lo, hi), AF.Copy)
+    IW = at("idx", 4, 4)
+    DF = ("Y", TP // 2, NP // 2, SL // 2)
+    OP = (A.min, A.max)
+    made, todo, done = [0], [], [VR]
 
-    ts(at("nL", 0, 24), at("nti", 0, 24), 2048.0, A.add)
+    def call(s, name):
+        last = s == S - 1
+        tq = TQ if s else 0
+        vg = VS if s else VS0
+        if s == 0:
+            statics(FILL.get(name, 0))
+        if s == 0 and name in GAPS:
+            cp(at("R", done[0], GAPS[name]), at("r0b", done[0], GAPS[name]))
+            done[0] += GAPS[name]
+        if name[0] == ":":
+            scalar(s, name[1:])
+        elif name in ("fp0", "fp1", "fx", "fw", "uu", "ad", "pre") and s == 0:
+            pass
+        elif name[:2] == "fp":
+            h = order[int(name[2])]
+            ts(("p", h * (FAR + HP), (h + 1) * (FAR + HP), at("idx", 2 * h, 2)), at("xq", 32 * h, 32), 0.25, A.mult, 0.0, A.add)
+        elif name == "fx":
+            cp(("xb", 0, WX, IW), at("xq", 0, C))
+        elif name == "fw":
+            cp(("wb", 0, WX, IW), at("new", 0, C))
+            for q in range(4 - tq, 4) if made[0] == 0 else []:
+                mm(ps(PW[q], QW), ONE, quarter("w", q), True, False)
+        elif name == "uu":
+            tt(ps(UU, C), ps(DQ, C), at("hit", 0, C), A.mult)
+        elif name == "ad":
+            tt(at("aq", 0, C), ps(UU, C), at("aq", 0, C), A.add)
+        elif name[0] == "s":
+            h = order[int(name[1])]
+            lo = FAR + h * HP
+            scan(at("Y", h * HP // 2, HP // 2), ("p", lo, lo + HP, 2), ("p", lo + 1, lo + HP, 2), A.add, A.add)
+            turn = at("nid", 128 - 16 * (1 + s), 128)
+            if HALVES:
+                mm(ps(PR if name == "s1" else PR0, 32), turn, ("Y", h * HP // 2 + TP // 2, (h + 1) * HP // 2, SL // 2), True, True)
+            elif name == "s1":
+                mm(ps(PR, C), turn, DF, True, True)
+        elif name == "cl":
+            ts(ps(PE, C), DF, -2.0, A.max, 2.0, A.min)
+        elif name == "l0":
+            if HALVES:
+                leave(s, order[:1])
+        elif name == "lv":
+            leave(s, order[1:] if HALVES else order)
+            if s == 0:
+                offsets(1, 1)
+        elif name in ("ti", "ga") and (last or s == 0 and len(todo) > RP0):
+            pass
+        elif name == "ti":
+            cp(("R", 0, W, at("ntu", s * 4, 4)), at("land", s * C, C))
+        elif name == "ga":
+            gather(s + 1, vg)
+        elif name[0] == "t":
+            q = int(name[1])
+            for k in range(4 * q, 4 * q + 4):
+                tt(tap("t", k), ps(PE, C), tap("x", k), A.mult)
+                if q < DS and k % 2:
+                    act(ps(PW[q] + (k % 4 - 1) * C, 2 * C), tap("t", k - 1, 2), AF.Copy, scale=-0.015625)
+            if q >= 4 - tq:
+                mm(ps(PW[q], QW), at("i64", 0, 128), quarter("t", q), False, True)
+            elif q >= DS:
+                act(ps(PW[q], QW), quarter("t", q), AF.Copy, scale=-0.015625)
+        elif name[0] == "a":
+            q = int(name[1])
+            if q < 4 - tq:
+                tt(ps(PW[q], QW), ps(PW[q], QW), quarter("w" if s else "w0b", q), A.add)
+            if q < 2:
+                size(q, q)
+                act(at("ms", q * 2 * C, 2 * C), ps(PW[q] + (1 - q) * 2 * C, 2 * C), AF.Abs)
+            elif q < 3:
+                act(ps(PM[q], QW), ps(PW[q], QW), AF.Abs)
+        elif name in ("pd", "px"):
+            h = int(name == "px")
+            if HELP[h]:
+                mm(ps(PD[h], 2 * C), ONE, tap("ms", HELP[h][0] - 2, 2), True, False)
+        elif name[0] in "mM":
+            h, level, half = "mM".index(name[0]), int(name[1]), int(name[2:] == "b")
+            o, l1 = PT + h * 2 * C, at("l1", h * QW + half * 2 * C, 2 * C)
+            if level == 0:
+                tt(l1, ps(PM[half] + half * 2 * C, 2 * C), at("ms", half * 2 * C, 2 * C), OP[h])
+            elif level == 1:
+                tt(l1, ps(PM[2] + half * 2 * C, 2 * C), l1, OP[h])
+            elif level == 2:
+                for i in range(2):
+                    tt(at("l2", (2 * h + half) * C, C) if i else ps(o + half * C, C), ps(PM[3] + (2 * half + i) * C, C),
+                       at("l1", h * QW + (2 * half + i) * C, C), OP[h])
+            elif level == 3:
+                tt(at("l3", h * C, C) if half else ps(o, C), ps(o + half * C, C), at("l2", h * 2 * C + half * C, C), OP[h])
+            else:
+                for i in range(1 if h else MN):
+                    tt(at("l4", (4 * h + i) * C, C), ps(o, C), at("l3", h * C, C), OP[h])
+                for i in range(1, 4) if h else []:
+                    act(at("l4", (4 + i) * C, C), at("l4", 4 * C, C), AF.Copy)
+                for k in range(len(HELP[h])):
+                    mm(ps(PD[h] + k * C, C), at("nid", 0, 128), at("l4", 4 * h * C, C), False, k == 1)
+        elif name == "of":
+            if not last:
+                offsets(s + 1, 2)
+        elif name == "ki":
+            if BOTH:
+                mm(ps(PKS, 2 * C), ONE, at("cB", 0, 2 * C), True, False)
+            else:
+                mm(ps(PKW, C), ONE, at("cK", 0, C), True, False)
+                mm(ps(PKS, C), ONE, at("cK", C, C), True, False)
+        elif name == "kr":
+            mm(ps(PKS, C), at("i1k", 0, 128), at("sgn", 0, C), False, False)
+        elif name[0] == "c":
+            for _ in range(min(int(name[1:]), len(todo))):
+                if s == 0 and len(todo) == RP0:
+                    call(s, "ti")
+                    call(s, "ga")
+                h, m, r, k = todo.pop(0)
+                o = PM[k // 4] + (k % 4) * C
+                tt(("kmax" if h else "kmin", k * C + r, (k + m) * C, m), ("ps", o + r, o + m * C, m),
+                   ("l4", 4 * h * C + r, (4 * h + m) * C, m), A.is_equal)
+                if k + m == TP:
+                    votes(h, r, m)
+        elif name == "ow":
+            own(s + 1, vg)
+        elif name[0] == "p":
+            prod(made[0], made[0] + int(name[1:]), vg)
+            made[0] += int(name[1:])
+        elif name == "kw":
+            for c in range(4):
+                scan(at("Mw", c * C, TP), at("mkey", 0, TP), ("ps", PKW + c, PKW + C, 4), A.mult, A.max)
+        elif name == "H":
+            ts(("Mw", 2 * TP - 1, 4 * C, C), ("Mw", TP - 1, 4 * C, C), ROUND, A.add, ROUND, A.subtract)
+        elif name == "L":
+            scan(at("L", 0, 16), at("cL", 0, 16), ("Mw", TP - 1, 4 * C, TP), A.mult, A.add)
+            for c in range(4):
+                act(("z", c, C, 4), at("iX", 0, TP), AF.Abs, bias=at("L", 4 * c + 3, 1), scale=-1.0)
+        elif name == "ks":
+            for c in range(4):
+                scan(at("Ms", 2 * TP * c, TP), at("mkey", 0, TP), ("ps", PKS + c, PKS + C, 4), A.mult, A.max)
+        elif name == "Hs":
+            ts(("Ms", 2 * TP - 1, 2 * C, 2 * TP), ("Ms", TP - 1, 2 * C, 2 * TP), ROUND / 16, A.add, ROUND / 16, A.subtract)
+            act(at("z1", 0, C), at("z", 0, C), AF.Identity, bias=1.0 - FAR / 2, scale=-1.0)
+            for c in range(4):
+                act(at("ky", c, 1), strong(c, 0), AF.Identity, bias=strong(c, 1), scale=-1.0)
+            if last:
+                tails(s, 0)
+            for c in range(4):
+                act(("hit", c, C, 4), ("z1", c, C, 4), AF.Relu, bias=at("ky", c, 1))
+        elif name == "kb":
+            for c in range(4):
+                scan(at("Mb", 6 * TP * c + TP, 2 * TP), at("mkey", 0, 2 * TP), ("ps", PKS + c, PKS + 2 * C, 4), A.mult, A.max)
+        elif name == "Hb":
+            for (o, i) in ((1, 2), (4, 3)):
+                ts(("Mb", o * TP - 1, 6 * C, 6 * TP), ("Mb", i * TP - 1, 6 * C, 6 * TP), ROUND / 16, A.add, ROUND / 16, A.subtract)
+        elif name == "Lb":
+            scan(at("Lb", 0, 24), at("cL", 16, 24), ("Mb", TP - 1, 6 * C, TP), A.mult, A.add)
+            for c in range(4):
+                act(("z", c, C, 4), at("iX", 0, TP), AF.Abs, bias=at("Lb", 6 * c + 5, 1), scale=-1.0)
+            act(at("ky", 0, 4), ("Lb", 1, 24, 6), AF.Identity, bias=1.0 - FAR / 2, scale=-1.0)
+            if last:
+                tails(s, 0)
+            for c in range(4):
+                act(("hit", c, C, 4), ("z", c, C, 4), AF.Relu, bias=at("ky", c, 1), scale=-1.0)
+        elif name == "Ib":
+            for c in [2 * h + i for h in order for i in range(2)]:
+                ts(("idx", c, 8, 4), at("Lb", 6 * c + 3, 2), at("Lb", 6 * c + 1, 1), A.subtract if c < 2 else A.add)
+        elif name == "IP":
+            for c in [2 * h + i for h in order for i in range(2)]:
+                ts(("idx", c, 8, 4), at("L", 4 * c + 1, 2), strong(c, c < 2), A.add, strong(c, c >= 2), A.subtract)
+
+    statics(ST[0])
+    cp(at("nL", 24, 4), at("nti", 0, 4))
+    for h in range(0 if WL else 2):
+        act(ps(PW[2 * h], 2 * QW), at("w0b", 2 * h * QW, 2 * QW), AF.Copy)
+    statics(ST[1])
+    for c in range(4):
+        ts(("i0", c, C, 4), ("dli", c, C, 4), -1.0, A.mult, at("nL", 24 + c, 1), A.add)
     cp(at("aq", 0, C), at("dli", 0, C))
-    offsets(0, 0, C)
-    offsets(0, 1, C)
-    for q in range(4):
-        cp(ps(PW[q], QW), quarter("w0b", q))
-    offsets(0, 2, C)
-    cp(("R", 0, RCUT // 2), ("r0b", 0, RCUT // 2))
-    convert(RCUT // 2, RCUT)
+    ts(at("nL", 0, 24), at("nti", 0, 24), 2048.0, A.add)
+    statics(ST[2])
+    ts(at("i0", C, C), at("i0", 0, C), W - 1, A.bitwise_and)
+    statics(ST[3])
+    cp(at("ix", 0, C), at("i0", C, C))
+    statics(ST[4])
+    if WL:
+        ts(at("idb", 0, 128), at("iX", 0, 128), PAR, A.is_equal)
+        for q in range(4):
+            mm(ps(PW[q], QW), at("idb", 0, 128), quarter("w0b", q), True, True)
+    call(0, "pre")
+    if VR:
+        add("G", lambda e: e.affine_select(T.R[:, 0:VR], T.r0b[:, 0:VR], [[0, VR]], A.is_ge, 0.0, 0, 0), [at("r0b", 0, VR)], [at("R", 0, VR)])
+    convert(VR + sum(GAPS.values()), RS[0])
     gather(0, VG)
     own(0, VG)
     desired(0)
     prod(0, TP, VG)
     cp(at("aq", C, 12), at("qui", 0, 12))
-    offsets(1, 0, AQ, lambda: gaps(0, 0))
-    convert(RCUT, RMID)
+    cp(at("ntu", 0, 24), at("nti", 0, 24))
+    offsets(1, 0, lambda: gaps(0, 0))
+    convert(max(RS[0], VR + sum(GAPS.values())), RS[1])
     for s in range(S):
         last = s == S - 1
-        late = s < LATE
-        DF = ("Y", TP // 2, NP // 2, SL // 2)
-        turn = at("nid", 128 - 16 * (1 + s), 128)
-        for h in range(2):
-            lo = (h + 1) * HP
-            scan(at("Y", h * HP // 2, HP // 2), ("p", lo, lo + HP, 2), ("p", lo + 1, lo + HP, 2), A.add, A.add)
-        mm(ps(PR, C), turn, DF, True, True)
-
-        def leave():
-            ts(at("send", s * C, C), ps(PR, C), -2.0, A.max, 2.0, A.min)
-            for bs in ([[b] for b in order] if WIDE else [order]):
-                pass_on(s, bs)
-            add(None, None, [], [at("land", s * C, C)], ("arr%d" % s, 2 * ENG))
-        if s:
-            cp(IW, at("ky", 8, 4))
-            delays(1)
-        else:
-            cp(at("ntu", 0, 24), at("nti", 0, 24))
-        ts(ps(PE, C), DF, -2.0, A.max, 2.0, A.min)
-        if s:
-            fix_x()
-            fix_w(0, WX)
-            leave()
-        for q in range(4):
-            for k in range(4 * q, 4 * q + 4):
-                tt(tap("t", k), ps(PE, C), tap("x", k), A.mult)
-            act(ps(PW[q], QW), quarter("t", q), AF.Copy, scale=-0.015625)
-            if s == 0 and q == 0:
-                leave()
-                offsets(1, 1)
-        for q in range(4):
-            tt(ps(PW[q], QW), ps(PW[q], QW), quarter("w" if s else "w0b", q), A.add)
-            act(at("ms", (q // 2) * QW, QW) if q % 2 else ps(PM[q], QW), ps(PW[q], QW), AF.Abs)
-        if s:
-            delays(2)
-
-        if OFF:
-            mm(ps(PD, OFF * C), at("rot", 0, 128), at("ms", 0, OFF * C), True, False)
-        both = ((1, A.max), (0, A.min))
-        spec = not last and not late
-        for (h, op) in both:
-            tt(ps(PT + h * QW, QW), ps(PM[0], QW), at("ms", 0, QW), op)
-        if s:
-            early(s)
-        for q in (1, 3):
-            act(ps(PM[q], QW), ps(PW[q], QW), AF.Abs)
-        gaps(s, 1)
-        if not last:
-            desired(s + 1)
-        if s:
-            tails(s - 1, 0)
-        gaps(s, 2)
-        if s:
-            tails(s - 1, 1)
-        gaps(s, 3)
-        if s == 0:
-            convert(RMID, W)
-        kw, ks = (C, 0) if last else (0, C)
-        for (h, op) in both:
-            tt(at("l1", h * QW, QW), ps(PM[2], QW), at("ms", QW, QW), op)
-        for (h, op) in both:
-            for half in range(2):
-                o = PT + h * QW + half * 2 * C
-                tt(at("l2", h * 2 * C, 2 * C) if half else ps(o, 2 * C), ps(o, 2 * C), at("l1", h * QW + half * 2 * C, 2 * C), op)
-        for (h, op) in both:
-            for half in range(2):
-                o = PT + h * QW + half * C
-                tt(at("l3", h * C, C) if half else ps(o, C), ps(o, C), at("l2", h * 2 * C + half * C, C), op)
-        mm(ps(PK, 2 * C), at("rot", 0, 128), at("cK", 2 * kw, 2 * C), True, False)
-        for o in (4 * C, 5 * C):
-            tt(at("l4", o, C), ps(PT + QW, C), at("l3", C, C), A.max)
-        if not last:
-            offsets(s + 1, 2)
-        tt(at("l4", 0, C), ps(PT, C), at("l3", 0, C), A.min)
-        for o in (C, 2 * C, 3 * C):
-            act(at("l4", o, C), at("l4", 0, C), AF.Copy)
-        for k in range(OFF):
-            mm(ps(PD + k * C, C), at("nid", 0, 128), at("l4", 0, C), False, k == OFF - 1)
-        if OFF:
-            act(at("kmin", QW, OFF * C), ps(PD, OFF * C), AF.Sign, scale=-1.0)
-        todo = [(1, 2, r, k) for r in range(2) for k in range(0, TP, 2)]
-        todo += [(0, 2, r, 6) for r in range(2) if OFF == 2]
-        todo += [(0, 4, r, k) for r in range(4) for k in range(0, TP, 4) if k not in helped]
-        for n, (h, m, r, k) in enumerate(todo):
-            if n == len(todo) - (RPOS if s else RP0) and spec:
-                take_in(s, VS)
-            o = PM[k // 4] + (k % 4) * C
-            tt(("kmax" if h else "kmin", k * C + r, (k + m) * C, m), ("ps", o + r, o + m * C, m),
-               ("l4", 4 * h * C + r, (4 * h + m) * C, m), A.is_equal)
-            if k + m == TP:
-                votes(ks if h else kw, "kmax" if h else "kmin", r, m, n + 1 == len(todo))
-                if (h, r) == (1, 1):
-                    mm(ps(PK + ks, C), at("i1k", 128 * last, 128), at("sgn", 0, C), False, False)
+        todo[:] = [(0, MN, r, k) for r in range(MN) for k in range(0, TP, MN) if k not in HELP[0]]
+        todo += [(1, 2, r, k ^ 2) for r in range(2) for k in HELP[1][:1]]
+        todo += [(1, 4, r, k) for r in range(4) for k in range(0, TP, 4) if k not in HELP[1] and k + 2 not in HELP[1]]
+        made[0] = 0
+        for name in (SUMS + " " + UPDATE + " " + TREES).split():
+            call(s, name)
         if last:
-            keep(range(4))
             store("Y", T.yr[:], at("land", s * C, C), "st_a", 48)
-        if spec:
-            if RPOS == 0:
-                take_in(s, VS)
-            own(s + 1, VS)
-            prod(0, PA)
-        for c in range(4):
-            scan(("M", c, 2 * C, 4), at("mkey", 0, 32), ("ps", PK + c, PK + 2 * C, 4), A.mult, A.max)
-        if spec:
-            prod(PA, P1)
-        tt(at("D", 0, 4), at("M", ks + 60, 4), at("M", kw + 60, 4), A.subtract)
-        if spec:
-            prod(P1, P2)
-        ts(at("Z", 0, 4), at("D", 0, 4), W - 1, A.bitwise_and)
-        if spec:
-            prod(P2, P3)
-        if last:
-            cp(IW, at("Z", 0, 4))
-            tails(s, 0)
-            tt(at("hit", 0, C), ("Z", 0, 8, at("lh", 0, 4)), at("col", 0, C), A.is_equal)
-            fix_w(C, FAR + NW)
-            store("Y", T.yw[:], at("w", 0, NW), "st_a", 48)
-            delays(1)
-            delays(2)
-        else:
-            cp(IP, at("Z", 0, 4))
-            prod(P3, TP)
-            tt(at("ky", 0, 4), at("Z", 0, 4), at("cu", 0, 4), A.subtract)
-            keep(range(2))
-            delays(0)
-            fix_p()
-            keep(range(2, 4))
+        for name in (LAST if last else COMPARE + " " + KEYS).split():
+            call(s, name)
+    made[0] = TP
+    call(S - 1, "fw")
+    store("Y", T.yw[:], at("w", 0, NW), "st_a", 48)
+    call(S - 1, "uu")
+    call(S - 1, "ad")
     tails(S - 1, 1)
     store("Y", T.yd[:], at("aq", 0, C), "st_a", 48)
     store("S", T.yq[:], at("aq", C, 12), "st_b", 16)
+    for n, op in enumerate(ops):
+        op["n"] = n
     emit(g, T, ops)
     g.sync.wait_ge(T.sem.st_a, 48)
     g.scalar.wait_ge(T.sem.st_b, 16)

from concourse.bass import DstId, RemoteDMATransfer
from concourse.mybir import AluOpType, ActivationFunctionType

TP, C, W, S, Q = 16, 64, 4096, 6, 3
NW = TP * C
QW = NW // 4
SL = TP + 4
HUGE = 2.0 ** 60
ROUND = 1.5 * 2.0 ** 39
NP = SL * C
HP = NP // 2
FAR = 2048
WX = 2 * FAR + NW
WITHIN = {"xq": ("new", C), "w": ("wb", FAR), "x": ("xb", FAR)}
AQ = C + 4 * Q
BANK = 512
RCUT = 2560
VR = 2304
GAPS = {"pre": 256, "fp0": 128}
RS = (0, 3700)
FILL = {"fw": 2, "l0": 3, "m0a": 9}
ST = (11, 3, 2, 3, 4)
WL = 1
HELP = ((), (4, 5))
RP0 = 8
VG, VS0, VS = 5, 2, 0
TQ = 0
DS = 1
HALVES = 1
MN = 2
CLASSES = ["m0", "m1", "M0", "M1", "M2", "M3"]
SUMS = "fp0 fp1 fx s0 uu s1 ki ad fw cl l0 :a"
UPDATE = "t0 t1 lv t2 t3 a0 a1 a2 a3 px"
TREES = "m0a M0a m0b M0b :3 :g1 :K01 :g2 :A0 :A1 :R m1a m1b M1a M1b :d m2a m2b M2a M2b :sg m3a m3b M3a M3b kr m4 :t0 M4 :t :X of"
COMPARE = "c10 ti ga c99"
KEYS = "ow kw p5 H p3 ks L p4 Hs p4 IP :K23"
LAST = "c99 :K23 kw H ks L Hs IP"

F, B, I, U = "float32", "bfloat16", "int32", "uint16"
SCRATCH = {
    "r0b": ("sbuf", [128, W], B), "R": ("sbuf", [128, W], F),
    "w0b": ("sbuf", [128, NW], B), "d0b": ("sbuf", [128, S * C], B),
    "dli": ("sbuf", [128, C], I), "qui": ("sbuf", [128, 12], I), "nti": ("sbuf", [128, 24], I), "i0": ("sbuf", [128, 2 * C], I),
    "wb": ("sbuf", [128, WX], F), "xb": ("sbuf", [128, WX], F), "p": ("sbuf", [128, 2 * (FAR + HP)], F), "new": ("sbuf", [128, 2 * C], F),
    "Y": ("sbuf", [128, NP // 2], F), "t": ("sbuf", [128, NW], F), "ms": ("sbuf", [128, QW], F),
    "l1": ("sbuf", [128, 2 * QW], F), "l2": ("sbuf", [128, QW], F), "l3": ("sbuf", [128, 2 * C], F), "l4": ("sbuf", [128, 8 * C], F),
    "kmin": ("sbuf", [128, NW], B), "kmax": ("sbuf", [128, NW], B), "mkey": ("sbuf", [128, 2 * TP], B),
    "Mw": ("sbuf", [128, 4 * C], F), "Ms": ("sbuf", [128, 2 * C], F), "L": ("sbuf", [128, 16], F), "cL": ("sbuf", [128, 40], F),
    "Mb": ("sbuf", [128, 6 * C], F), "Lb": ("sbuf", [128, 24], F), "uu": ("sbuf", [128, C], F),
    "idx": ("sbuf", [128, 8], U), "z": ("sbuf", [128, C], F), "z1": ("sbuf", [128, C], F), "ky": ("sbuf", [128, 4], F),
    "aq": ("sbuf", [128, AQ], F), "nL": ("sbuf", [128, 28], F), "ntu": ("sbuf", [128, 24], U),
    "g1": ("sbuf", [128, C], F), "g2": ("sbuf", [128, C], F), "sgn": ("sbuf", [128, C], B),
    "hit": ("sbuf", [128, C], F), "q16": ("sbuf", [128, 4], F), "junk": ("sbuf", [128, C], F),
    "a2": ("sbuf", [128, AQ], F), "neg": ("sbuf", [128, AQ], B), "ix": ("sbuf", [128, S * AQ], U),
    "pI": ("sbuf", [128, 1], I), "pb": ("sbuf", [128, 4], I), "pf": ("sbuf", [128, 4], F), "pg": ("sbuf", [128, 4], F),
    "iX": ("sbuf", [128, 144], F), "iP": ("sbuf", [128, C + 4], F), "col": ("sbuf", [128, 4], F), "cK": ("sbuf", [128, 2 * C], F), "cB": ("sbuf", [128, 2 * C], F),
    "rot": ("sbuf", [128, 128], F), "nid": ("sbuf", [128, 256], F), "i64": ("sbuf", [128, 128], F),
    "i1k": ("sbuf", [128, 128], B), "idb": ("sbuf", [128, 128], B), "i2k": ("sbuf", [128, 128], B), "vot": ("sbuf", [128, 144], B),
    "send": ("sbuf", [128, S * C], F), "land": ("sbuf", [128, S * C], F),
    "ps": ("psum", [128, 8 * BANK], F),
}
SEMAPHORES = (["eV", "eS", "eT", "eG", "ld_s", "ld_w", "ld_d", "ld_q", "ld_r0", "ld_r1", "sent", "st_a", "st_b"]
              + ["arr%d" % s for s in range(S)])
PW = [q * BANK + (1 - q % 2) * QW for q in range(4)]
PM = [4 * BANK, 5 * BANK, 6 * BANK, 3 * BANK + QW]
PD = [0, 2 * BANK]
PKW = BANK + QW
DQ, UU = 2 * C, 3 * C
PE, PO, PT = 4 * BANK + QW, 5 * BANK + QW, 6 * BANK + QW
PR, PKS = 7 * BANK, 7 * BANK + QW
PR0 = 6 * BANK + QW


def routes(T, topo):
    out = []
    n = len(T.cores)
    for r, src in enumerate(T.cores):
        used = []
        for b in range(2):
            dst = T.cores[(r + 1 + b) % n]
            via = None
            if not topo.may_write(src, dst):
                cand = [c for c in topo.cores_of(src) if T.rank_of(c) is None and c not in used and topo.may_write(c, dst)]
                cand.sort(key=lambda c: (topo.die(c) != topo.die(src), c))
                via = cand[0]
                used.append(via)
            out.append((src, dst, via, b))
    return out


def helper_program(g, core, T, topo, job):
    src, dst, via, b = job
    rid, pid = topo.addr(dst, core)
    for s in range(S):
        piece = T.land[:, s * C + b * 32:s * C + b * 32 + 32]
        g.wait_ge(T.sem["arr%d" % s], len(topo.engines(src, core)))
        g.remote_dma(piece, piece, T.sem["arr%d" % s], T.sem.sent, pid, rid, topo.mask(core, dst))
    g.wait_ge(T.sem.sent, S * len(topo.engines(core, dst)))


def columns(a):
    step = a[3] if len(a) == 4 and isinstance(a[3], int) else 1
    if step == 1:
        m = ((1 << (a[2] - a[1])) - 1) << a[1]
    else:
        m = 0
        for c in range(a[1], a[2], step):
            m |= 1 << c
    return a[0], m, range(a[1] // BANK, (a[2] - 1) // BANK + 1) if a[0] == "ps" else []


def emit(g, T, ops):
    qs = {"V": g.vector, "S": g.scalar, "T": g.tensor, "G": g, "Y": g.sync}
    known = {q: {} for q in qs}
    seq = {q: 0 for q in qs}
    acc, held = {}, {}
    for op in ops:
        q = op["q"]
        if op["tok"] is None:
            seq[q] += 1
            op["key"], op["val"] = q, seq[q]
        else:
            op["key"], op["val"] = op["tok"]
        deps = []
        touch = [("r", columns(a)) for a in op["r"]] + [("w", columns(a)) for a in op["w"]]
        for mode, (buf, m, banks) in touch:
            for k in banks:
                deps.extend(o2 for q2, o2 in held.get(k, {}).items() if q2 != q)
            for (o2, mode2, m2) in acc.get((buf, q) if banks else buf, []):
                if not m & m2 or (mode2 == "r" and mode == "r"):
                    continue
                if banks and q == "T" and op["more"]:
                    continue
                deps.append(o2)
        op["waits"] = []
        if q is not None:
            kn = known[q]
            best = {}
            for o2 in deps:
                if o2["key"] not in best or best[o2["key"]]["val"] < o2["val"]:
                    best[o2["key"]] = o2
            for o2 in sorted(best.values(), key=lambda o: -o["n"]):
                if kn.get(o2["key"], 0) >= o2["val"]:
                    continue
                op["waits"].append(o2)
                o2["flag"] = True
                kn[o2["key"]] = o2["val"]
                for k, v in o2["clock"].items():
                    if kn.get(k, 0) < v:
                        kn[k] = v
            op["clock"] = dict(kn)
        else:
            op["clock"] = {}
        for mode, (buf, m, banks) in touch:
            for k in banks:
                held.setdefault(k, {})[q] = op
            lst = acc.setdefault((buf, q) if banks else buf, [])
            if mode == "w":
                lst[:] = [a for a in lst if a[2] & ~m or (a[0] is op and a[1] == "r")]
            else:
                lst[:] = [a for a in lst if a[1] == "w" or a[2] & ~m or a[0]["key"] != op["key"]]
            lst.append((op, mode, m))
    cnt = {q: 0 for q in qs}
    for op in ops:
        if op["tok"] is None and op["flag"]:
            cnt[op["q"]] += 1
            op["cnt"] = cnt[op["q"]]
    for op in ops:
        if op["q"] is None:
            continue
        eng = qs[op["q"]]
        for o2 in op["waits"]:
            if o2["tok"] is None:
                eng.wait_ge(T.sem["e" + o2["q"]], o2["cnt"])
            else:
                eng.wait_ge(T.sem[o2["key"]], o2["val"])
        ins = op["fn"](eng)
        if op["tok"] is None and op["flag"]:
            ins.then_inc(T.sem["e" + op["q"]], 1)


def rank_program(g, core, T, topo):
    jobs = routes(T, topo)
    if T.rank_of(core) is None:
        for job in jobs:
            if job[2] == core:
                helper_program(g, core, T, topo, job)
        return
    A, AF = AluOpType, ActivationFunctionType
    ops = []

    def add(q, fn, r, w, tok=None, more=False):
        ops.append({"q": q, "fn": fn, "r": r, "w": w, "tok": tok, "flag": False, "more": more})

    def ap(a):
        if len(a) == 3:
            return T[a[0]][:, a[1]:a[2]]
        if isinstance(a[3], int):
            return T[a[0]][:, a[1]:a[2]:a[3]]
        return T[a[0]][:, a[1]:a[2]].indirect(ap(a[3]))

    def regs(*aps):
        return [a for a in aps if isinstance(a, tuple)]

    def lists(*aps):
        return [a[3] for a in aps if isinstance(a, tuple) and len(a) == 4 and isinstance(a[3], tuple)]

    def val(a):
        return ap(a) if isinstance(a, tuple) else a

    def tt(out, a, b, op):
        add("V", lambda e: e.tensor_tensor(ap(out), ap(a), ap(b), op), regs(a, b) + lists(out, a), regs(out))

    def ts(out, a, s1, op0, s2=None, op1=None):
        if op1 is None:
            fn = lambda e: e.tensor_scalar(ap(out), ap(a), val(s1), None, op0)
        else:
            fn = lambda e: e.tensor_scalar(ap(out), ap(a), val(s1), val(s2), op0, op1)
        add("V", fn, regs(a, s1, s2) + lists(out, a), regs(out))

    def cp(out, a):
        add("V", lambda e: e.tensor_copy(ap(out), ap(a)), regs(a) + lists(out, a), regs(out))

    def scan(out, d0, d1, op0, op1):
        add("V", lambda e: e.tensor_tensor_scan(ap(out), ap(d0), ap(d1), 0.0, op0, op1), regs(d0, d1), regs(out))

    def fill(out, c):
        add("V", lambda e: e.memset(ap(out), c), [], regs(out))

    def act(out, a, func, bias=None, scale=None, acc=None):
        kw = {}
        if bias is not None:
            kw["bias"] = val(bias)
        if scale is not None:
            kw["scale"] = scale
        if acc is not None:
            kw["accum_out"] = ap(acc)
        add("S", lambda e: e.activation(ap(out), ap(a), func, **kw), regs(a, bias) + lists(a), regs(out, acc))

    def mm(out, l, r, start, stop):
        add("T", lambda e: e.matmul(ap(out), ap(l), ap(r), start, stop), regs(l, r), regs(out), None, not start)

    def iota(out, pat, base, cm=0, integer=False):
        if integer:
            add("G", lambda e: e.iota(ap(out), pat, base, cm), [], regs(out))
        else:
            add("G", lambda e: e.iota(ap(out), pat, base, cm, allow_small_or_imprecise_dtypes=True), [], regs(out))

    def load(q, out, src, sem, total=16):
        add(q, lambda e: e.dma_start(ap(out), src).then_inc(T.sem[sem], 16), [], regs(out), (sem, total))

    def store(q, dst, a, sem, total):
        add(q, lambda e: e.dma_start(dst, ap(a)).then_inc(T.sem[sem], 16), regs(a), [], (sem, total))

    def at(buf, lo, n):
        if buf == "cK" and "kb" in KEYS:
            buf, lo = "cB", (lo + C) % (2 * C)
        buf, o = WITHIN.get(buf, (buf, 0))
        return (buf, o + lo, o + lo + n)

    def ps(lo, n):
        return ("ps", lo, lo + n)

    def slot(k):
        return ("p", FAR + k, FAR + NP, SL)

    def tap(buf, k, n=1):
        return at(buf, k * C, n * C)

    def quarter(buf, q):
        return at(buf, q * QW, QW)

    load("S", at("dli", 0, C), T.dl[:], "ld_s", 32)
    load("Y", at("nti", 0, 24), T.nt[:], "ld_s", 32)
    if WL == 0:
        load("Y", at("w0b", 0, NW), T.w0[:], "ld_w")
    load("Y", ("r0b", 0, RCUT), T.r0[:, 0:RCUT], "ld_r0")
    load("Y", ("r0b", RCUT, W), T.r0[:, RCUT:W], "ld_r1")
    if WL:
        load("Y", at("w0b", 0, NW), T.w0[:], "ld_w")
    load("Y", at("d0b", 0, S * C), T.d0[:], "ld_d")
    load("Y", at("qui", 0, 12), T.qu[:], "ld_q")

    iota(at("pI", 0, 1), [[0, 1]], 0, 1, True)
    iota(at("iX", 0, 144), [[1, 144]], 0)
    iota(at("iP", 0, C), [[1, 16], [0, 2], [16 * SL, 2]], FAR // 2)
    iota(at("iP", C, 4), [[FAR + 32, 2], [16, 2]], FAR // 2)
    iota(at("cK", C, C), [[-W, 16], [0, 4]], 15 * W)
    mark = len(ops)
    P = at("pI", 0, 1)
    ROW, GRP, PAR = [at("pf", k, 1) for k in range(3)]
    BOTH = "kb" in KEYS
    KW = PKS + C if BOTH else PKW
    fill(slot(TP + 1), 0.0)
    fill(slot(TP + 2), HUGE)
    fill(slot(TP + 3), -HUGE)
    fill(at("mkey", 0, TP), 1.0)
    for i, m in enumerate((15, 112, 127)):
        ts(at("pb", i, 1), P, m, A.bitwise_and)
    for i, v in enumerate((0.0, -1.0, float(C), 1.0 / C)):
        fill(("cL", i, 16, 4), v)
    cp(at("pf", 0, 3), at("pb", 0, 3))
    fill(at("mkey", 0, 1), 0.0)
    fill(at("new", 0, C), 0.25)
    ts(at("pg", 0, 1), ROW, -float(SL), A.mult)
    ts(at("pg", 1, 1), GRP, 15.0, A.add)
    for o in (0, 128):
        ts(at("nid", o, 128), at("iX", 0, 128), PAR, A.is_equal, -1.0, A.mult)
    ts(at("cK", 0, C), at("iP", 0, C), -1.0, A.mult, at("pg", 0, 1), A.add)
    ts(at("rot", 0, 128), at("iX", 0, 128), PAR, A.is_equal)
    ts(at("col", 0, 4), at("iP", C, 4), ROW, A.add)
    ts(at("i2k", 0, 128), at("iX", 0, 128), PAR, A.is_equal, -2048.0, A.mult)
    for h in range(2):
        if HELP[h]:
            ts(at("cK", h * C + 4 * HELP[h][0], 8), at("cK", h * C + 4 * HELP[h][0], 8), 16 * 65536.0, A.add)
    ts(at("vot", 0, 144), at("iX", 0, 144), at("pg", 1, 1), A.is_equal, 65536.0, A.mult)
    ts(at("i1k", 0, 128), at("iX", 0, 128), PAR, A.is_equal, FAR / 2.0, A.mult)
    ts(("Mw", C - 1, 4 * C, C), at("col", 0, 4), -1.0 / C, A.mult)
    for c in range(4):
        ts(at("Mw", c * C + 3 * TP - 1, 1), at("cK", c, 1), float(C), A.mult, at("col", c, 1), A.add)
    if TQ:
        ts(at("i64", 0, 128), at("iX", 0, 128), PAR, A.is_equal, -0.015625, A.mult)
    later = ops[mark:]
    del ops[mark:]
    ONE = at("rot", 0, 128)

    def statics(n):
        ops.extend(later[:n])
        del later[:n]

    def offsets(s, part, between=None):
        if part == 0:
            for c in range(4):
                act(("a2", c, AQ, 4), ("aq", c, AQ, 4), AF.Identity, bias=at("nL", s * 4 + c, 1), scale=-1.0)
            between()
            act(at("neg", 0, AQ), at("a2", 0, AQ), AF.Sign, bias=-2047.5)
        elif part == 1:
            mm(ps(PO, AQ), ONE, at("a2", 0, AQ), True, False)
            mm(ps(PO, AQ), at("i2k", 0, 128), at("neg", 0, AQ), False, True)
        else:
            cp(at("ix", s * AQ, AQ), ps(PO, AQ))

    def gaps(s, part):
        if part == 0:
            for c in range(4):
                act(("ps", DQ + c, DQ + C, 4), ("aq", c, C, 4), AF.Identity, bias=at("aq", C + (s % Q) * 4 + c, 1), scale=-1.0)
        elif part == 1:
            act(at("g1", 0, C), ps(DQ, C), AF.Abs)
        elif part == 2:
            act(at("g2", 0, C), at("g1", 0, C), AF.Abs, bias=-2048.0)
        else:
            act(at("sgn", 0, C), at("g2", 0, C), AF.Sign, bias=1023.5, scale=-1.0)

    def tails(s, part):
        o = C + (s % Q) * 4
        if part == 0:
            act(at("q16", 0, 4), at("aq", o, 4), AF.Copy, scale=0.0625)
            return
        for c in range(4):
            act(("junk", c, C, 4), ("ps", UU + c, UU + C, 4), AF.Identity, bias=at("q16", c, 1), scale=-1.0, acc=at("aq", o + c, 1))

    def desired(s):
        act(slot(TP), at("d0b", s * C, C), AF.Copy, scale=-1.0)

    def convert(lo, hi):
        if hi > lo:
            act(("R", lo, hi), ("r0b", lo, hi), AF.Copy)

    def size(q, half):
        act(ps(PM[q] + half * 2 * C, 2 * C), ps(PW[q] + half * 2 * C, 2 * C), AF.Abs)

    def scalar(s, name):
        if name == "a" and 0 < s < S - 1:
            offsets(s + 1, 0, lambda: gaps(s, 0))
            offsets(s + 1, 1)
        elif name == "a" and s:
            gaps(s, 0)
        elif name in ("g1", "g2", "sg"):
            gaps(s, ("g1", "g2", "sg").index(name) + 1)
        elif name in ("S", "X") and HELP[name == "X"]:
            h = int(name == "X")
            act(tap("kmax" if h else "kmin", HELP[h][0], 2), ps(PD[h], 2 * C), AF.Sign, scale=1.0 if h else -1.0)
        elif name == "R" and s == 0:
            convert(RS[1], W)
        elif name == "d" and s < S - 1:
            desired(s + 1)
        elif name == "t0" and s:
            tails(s - 1, 0)
        elif name == "t" and s:
            tails(s - 1, 1)
        elif name[0] == "K":
            act(at("w", int(name[1]) * QW, len(name[1:]) * QW), ps(PW[int(name[1])], len(name[1:]) * QW), AF.Copy)
        elif name == "3":
            act(ps(PM[3], QW), ps(PW[3], QW), AF.Abs)
        elif name[0] == "A" and (HELP[0] != HELP[1] or 2 + 2 * int(name[1]) not in HELP[0]):
            size(int(name[1]), 1 - int(name[1]))

    def window(s, k0, k1):
        return ("R" if s else "r0b", 0, W, ("ix", s * AQ + 4 * k0, s * AQ + 4 * k1))

    def gather(s, vg):
        n = 4 if vg < 4 else 3
        cuts = [vg + (TP - vg) * i // n for i in range(n + 1)]
        for i in range(n):
            act(at("x", cuts[i] * C, (cuts[i + 1] - cuts[i]) * C), window(s, cuts[i], cuts[i + 1]), AF.Copy)
        if s:
            o = s * AQ + C + ((s - 1) % Q) * 4
            act(at("xq", 0, C), ("R", 0, W, at("ix", o, 4)), AF.Copy)

    def own(s, vg):
        if vg:
            cp(at("x", 0, vg * C), window(s, 0, vg))

    def prod(k0, k1, vg):
        first = vg + (TP - vg) // (4 if vg < 4 else 3)
        for k in (list(range(vg, first)) + list(range(vg)) + list(range(first, TP)))[k0:k1]:
            tt(slot(k), ps(PW[k // 4] + (k % 4) * C, C), tap("x", k), A.mult)

    mine = [j for j in jobs if j[0] == core]
    masks = [topo.mask(core, j[1] if j[2] is None else j[2]) for j in mine]
    order = [j[3] for j in sorted(mine, key=lambda j: j[2] is None)]
    sent = S * sum(bin(m).count("1") for m in masks)
    come = sum(len(topo.engines(j[0] if j[2] is None else j[2], core)) for j in jobs if j[1] == core)

    def pass_on(s, b):
        def fn(e):
            src, dst, via, _ = mine[b]
            rid, pid = topo.addr(dst if via is None else via, core)
            lo = s * C + b * 32
            tr = RemoteDMATransfer(dst_ids=[DstId(rid=rid, pnc=pid)], dma_engine_mask=masks[b], remote_sem=T.sem["arr%d" % s],
                                   src=T.send[:, lo:lo + 32], dst=T.land[:, lo:lo + 32])
            return e.remote_dma_fused([tr], local_sem=T.sem.sent)
        add("G", fn, [at("send", s * C + b * 32, 32)], [], ("sent", sent))

    def leave(s, blocks):
        lo, n = 32 * min(blocks), 32 * len(blocks)
        ts(at("send", s * C + lo, n), ps(PR if order[1] in blocks else PR0, n), -2.0, A.max, 2.0, A.min)
        for b in blocks:
            pass_on(s, b)
        if order[1] in blocks:
            add(None, None, [], [at("land", s * C, C)], ("arr%d" % s, come))

    def strong(c, lane):
        return at("Ms", 2 * TP * c + TP * lane + TP - 1, 1)

    def votes(h, r, m):
        for j in range(r, 16, m):
            mm(ps(PKS if h else KW, C), at("vot", 15 - j, 128), ("kmax" if h else "kmin", j, NW, 16), False, j == 15 and not (BOTH and todo))

    IW = at("idx", 4, 4)
    DF = ("Y", TP // 2, NP // 2, SL // 2)
    OP = (A.min, A.max)
    made, todo, done = [0], [], [VR]

    def call(s, name):
        last = s == S - 1
        tq = TQ if s else 0
        vg = VS if s else VS0
        if s == 0:
            statics(FILL.get(name, 0))
        if s == 0 and name in GAPS:
            cp(at("R", done[0], GAPS[name]), at("r0b", done[0], GAPS[name]))
            done[0] += GAPS[name]
        if name[0] == ":":
            scalar(s, name[1:])
        elif name in ("fp0", "fp1", "fx", "fw", "uu", "ad", "pre") and s == 0:
            pass
        elif name[:2] == "fp":
            h = order[int(name[2])]
            ts(("p", h * (FAR + HP), (h + 1) * (FAR + HP), at("idx", 2 * h, 2)), at("xq", 32 * h, 32), 0.25, A.mult, 0.0, A.add)
        elif name == "fx":
            cp(("xb", 0, WX, IW), at("xq", 0, C))
        elif name == "fw":
            cp(("wb", 0, WX, IW), at("new", 0, C))
            for q in range(4 - tq, 4) if made[0] == 0 else []:
                mm(ps(PW[q], QW), ONE, quarter("w", q), True, False)
        elif name == "uu":
            tt(ps(UU, C), ps(DQ, C), at("hit", 0, C), A.mult)
        elif name == "ad":
            tt(at("aq", 0, C), ps(UU, C), at("aq", 0, C), A.add)
        elif name[0] == "s":
            h = order[int(name[1])]
            lo = FAR + h * HP
            scan(at("Y", h * HP // 2, HP // 2), ("p", lo, lo + HP, 2), ("p", lo + 1, lo + HP, 2), A.add, A.add)
            turn = at("nid", 128 - 16 * (1 + s), 128)
            if HALVES:
                mm(ps(PR if name == "s1" else PR0, 32), turn, ("Y", h * HP // 2 + TP // 2, (h + 1) * HP // 2, SL // 2), True, True)
            elif name == "s1":
                mm(ps(PR, C), turn, DF, True, True)
        elif name == "cl":
            ts(ps(PE, C), DF, -2.0, A.max, 2.0, A.min)
        elif name == "l0":
            if HALVES:
                leave(s, order[:1])
        elif name == "lv":
            leave(s, order[1:] if HALVES else order)
            if s == 0:
                offsets(1, 1)
        elif name in ("ti", "ga") and (last or s == 0 and len(todo) > RP0):
            pass
        elif name == "ti":
            cp(("R", 0, W, at("ntu", s * 4, 4)), at("land", s * C, C))
        elif name == "ga":
            gather(s + 1, vg)
        elif name[0] == "t":
            q = int(name[1])
            for k in range(4 * q, 4 * q + 4):
                tt(tap("t", k), ps(PE, C), tap("x", k), A.mult)
                if q < DS and k % 2:
                    act(ps(PW[q] + (k % 4 - 1) * C, 2 * C), tap("t", k - 1, 2), AF.Copy, scale=-0.015625)
            if q >= 4 - tq:
                mm(ps(PW[q], QW), at("i64", 0, 128), quarter("t", q), False, True)
            elif q >= DS:
                act(ps(PW[q], QW), quarter("t", q), AF.Copy, scale=-0.015625)
        elif name[0] == "a":
            q = int(name[1])
            if q < 4 - tq:
                tt(ps(PW[q], QW), ps(PW[q], QW), quarter("w" if s else "w0b", q), A.add)
            if q < 2:
                size(q, q)
                act(at("ms", q * 2 * C, 2 * C), ps(PW[q] + (1 - q) * 2 * C, 2 * C), AF.Abs)
            elif q < 3:
                act(ps(PM[q], QW), ps(PW[q], QW), AF.Abs)
        elif name in ("pd", "px"):
            h = int(name == "px")
            if HELP[h]:
                mm(ps(PD[h], 2 * C), ONE, tap("ms", HELP[h][0] - 2, 2), True, False)
        elif name[0] in "mM":
            h, level, half = "mM".index(name[0]), int(name[1]), int(name[2:] == "b")
            o, l1 = PT + h * 2 * C, at("l1", h * QW + half * 2 * C, 2 * C)
            if level == 0:
                tt(l1, ps(PM[half] + half * 2 * C, 2 * C), at("ms", half * 2 * C, 2 * C), OP[h])
            elif level == 1:
                tt(l1, ps(PM[2] + half * 2 * C, 2 * C), l1, OP[h])
            elif level == 2:
                for i in range(2):
                    tt(at("l2", (2 * h + half) * C, C) if i else ps(o + half * C, C), ps(PM[3] + (2 * half + i) * C, C),
                       at("l1", h * QW + (2 * half + i) * C, C), OP[h])
            elif level == 3:
                tt(at("l3", h * C, C) if half else ps(o, C), ps(o + half * C, C), at("l2", h * 2 * C + half * C, C), OP[h])
            else:
                for i in range(1 if h else MN):
                    tt(at("l4", (4 * h + i) * C, C), ps(o, C), at("l3", h * C, C), OP[h])
                for i in range(1, 4) if h else []:
                    act(at("l4", (4 + i) * C, C), at("l4", 4 * C, C), AF.Copy)
                for k in range(len(HELP[h])):
                    mm(ps(PD[h] + k * C, C), at("nid", 0, 128), at("l4", 4 * h * C, C), False, k == 1)
        elif name == "of":
            if not last:
                offsets(s + 1, 2)
        elif name == "ki":
            if BOTH:
                mm(ps(PKS, 2 * C), ONE, at("cB", 0, 2 * C), True, False)
            else:
                mm(ps(PKW, C), ONE, at("cK", 0, C), True, False)
                mm(ps(PKS, C), ONE, at("cK", C, C), True, False)
        elif name == "kr":
            mm(ps(PKS, C), at("i1k", 0, 128), at("sgn", 0, C), False, False)
        elif name[0] == "c":
            for _ in range(min(int(name[1:]), len(todo))):
                if s == 0 and len(todo) == RP0:
                    call(s, "ti")
                    call(s, "ga")
                h, m, r, k = todo.pop(0)
                o = PM[k // 4] + (k % 4) * C
                tt(("kmax" if h else "kmin", k * C + r, (k + m) * C, m), ("ps", o + r, o + m * C, m),
                   ("l4", 4 * h * C + r, (4 * h + m) * C, m), A.is_equal)
                if k + m == TP:
                    votes(h, r, m)
        elif name == "ow":
            own(s + 1, vg)
        elif name[0] == "p":
            prod(made[0], made[0] + int(name[1:]), vg)
            made[0] += int(name[1:])
        elif name == "kw":
            for c in range(4):
                scan(at("Mw", c * C, TP), at("mkey", 0, TP), ("ps", PKW + c, PKW + C, 4), A.mult, A.max)
        elif name == "H":
            ts(("Mw", 2 * TP - 1, 4 * C, C), ("Mw", TP - 1, 4 * C, C), ROUND, A.add, ROUND, A.subtract)
        elif name == "L":
            scan(at("L", 0, 16), at("cL", 0, 16), ("Mw", TP - 1, 4 * C, TP), A.mult, A.add)
            for c in range(4):
                act(("z", c, C, 4), at("iX", 0, TP), AF.Abs, bias=at("L", 4 * c + 3, 1), scale=-1.0)
        elif name == "ks":
            for c in range(4):
                scan(at("Ms", 2 * TP * c, TP), at("mkey", 0, TP), ("ps", PKS + c, PKS + C, 4), A.mult, A.max)
        elif name == "Hs":
            ts(("Ms", 2 * TP - 1, 2 * C, 2 * TP), ("Ms", TP - 1, 2 * C, 2 * TP), ROUND / 16, A.add, ROUND / 16, A.subtract)
            act(at("z1", 0, C), at("z", 0, C), AF.Identity, bias=1.0 - FAR / 2, scale=-1.0)
            for c in range(4):
                act(at("ky", c, 1), strong(c, 0), AF.Identity, bias=strong(c, 1), scale=-1.0)
            if last:
                tails(s, 0)
            for c in range(4):
                act(("hit", c, C, 4), ("z1", c, C, 4), AF.Relu, bias=at("ky", c, 1))
        elif name == "kb":
            for c in range(4):
                scan(at("Mb", 6 * TP * c + TP, 2 * TP), at("mkey", 0, 2 * TP), ("ps", PKS + c, PKS + 2 * C, 4), A.mult, A.max)
        elif name == "Hb":
            for (o, i) in ((1, 2), (4, 3)):
                ts(("Mb", o * TP - 1, 6 * C, 6 * TP), ("Mb", i * TP - 1, 6 * C, 6 * TP), ROUND / 16, A.add, ROUND / 16, A.subtract)
        elif name == "Lb":
            scan(at("Lb", 0, 24), at("cL", 16, 24), ("Mb", TP - 1, 6 * C, TP), A.mult, A.add)
            for c in range(4):
                act(("z", c, C, 4), at("iX", 0, TP), AF.Abs, bias=at("Lb", 6 * c + 5, 1), scale=-1.0)
            act(at("ky", 0, 4), ("Lb", 1, 24, 6), AF.Identity, bias=1.0 - FAR / 2, scale=-1.0)
            if last:
                tails(s, 0)
            for c in range(4):
                act(("hit", c, C, 4), ("z", c, C, 4), AF.Relu, bias=at("ky", c, 1), scale=-1.0)
        elif name == "Ib":
            for c in [2 * h + i for h in order for i in range(2)]:
                ts(("idx", c, 8, 4), at("Lb", 6 * c + 3, 2), at("Lb", 6 * c + 1, 1), A.subtract if c < 2 else A.add)
        elif name == "IP":
            for c in [2 * h + i for h in order for i in range(2)]:
                ts(("idx", c, 8, 4), at("L", 4 * c + 1, 2), strong(c, c < 2), A.add, strong(c, c >= 2), A.subtract)

    statics(ST[0])
    cp(at("nL", 24, 4), at("nti", 0, 4))
    for h in range(0 if WL else 2):
        act(ps(PW[2 * h], 2 * QW), at("w0b", 2 * h * QW, 2 * QW), AF.Copy)
    statics(ST[1])
    for c in range(4):
        ts(("i0", c, C, 4), ("dli", c, C, 4), -1.0, A.mult, at("nL", 24 + c, 1), A.add)
    cp(at("aq", 0, C), at("dli", 0, C))
    ts(at("nL", 0, 24), at("nti", 0, 24), 2048.0, A.add)
    statics(ST[2])
    ts(at("i0", C, C), at("i0", 0, C), W - 1, A.bitwise_and)
    statics(ST[3])
    cp(at("ix", 0, C), at("i0", C, C))
    statics(ST[4])
    if WL:
        ts(at("idb", 0, 128), at("iX", 0, 128), PAR, A.is_equal)
        for q in range(4):
            mm(ps(PW[q], QW), at("idb", 0, 128), quarter("w0b", q), True, True)
    call(0, "pre")
    if VR:
        add("G", lambda e: e.affine_select(T.R[:, 0:VR], T.r0b[:, 0:VR], [[0, VR]], A.is_ge, 0.0, 0, 0), [at("r0b", 0, VR)], [at("R", 0, VR)])
    convert(VR + sum(GAPS.values()), RS[0])
    gather(0, VG)
    own(0, VG)
    desired(0)
    prod(0, TP, VG)
    cp(at("aq", C, 12), at("qui", 0, 12))
    cp(at("ntu", 0, 24), at("nti", 0, 24))
    offsets(1, 0, lambda: gaps(0, 0))
    convert(max(RS[0], VR + sum(GAPS.values())), RS[1])
    for s in range(S):
        last = s == S - 1
        todo[:] = [(0, MN, r, k) for r in range(MN) for k in range(0, TP, MN) if k not in HELP[0]]
        todo += [(1, 2, r, k ^ 2) for r in range(2) for k in HELP[1][:1]]
        todo += [(1, 4, r, k) for r in range(4) for k in range(0, TP, 4) if k not in HELP[1] and k + 2 not in HELP[1]]
        made[0] = 0
        for name in (SUMS + " " + UPDATE + " " + TREES).split():
            call(s, name)
        if last:
            store("Y", T.yr[:], at("land", s * C, C), "st_a", 48)
        for name in (LAST if last else COMPARE + " " + KEYS).split():
            call(s, name)
    made[0] = TP
    call(S - 1, "fw")
    store("Y", T.yw[:], at("w", 0, NW), "st_a", 48)
    call(S - 1, "uu")
    call(S - 1, "ad")
    tails(S - 1, 1)
    store("Y", T.yd[:], at("aq", 0, C), "st_a", 48)
    store("S", T.yq[:], at("aq", C, 12), "st_b", 16)
    for n, op in enumerate(ops):
        op["n"] = n
    emit(g, T, ops)
    g.sync.wait_ge(T.sem.st_a, 48)
    g.scalar.wait_ge(T.sem.st_b, 16)
    g.wait_ge(T.sem.sent, sent)
